import numpy as np
import ml_dtypes


def mxq(x, axis, fmt="e4m3"):
    dtype, down = {"e4m3": (ml_dtypes.float8_e4m3fn, 7), "e5m2": (ml_dtypes.float8_e5m2, 14)}[fmt]
    v = np.moveaxis(np.asarray(x, np.float32).astype(ml_dtypes.bfloat16).astype(np.float64), axis, -1)
    blocks = v.reshape(v.shape[:-1] + (-1, 32))
    amax = np.abs(blocks).max(-1, keepdims=True)
    byte = np.maximum(np.where(amax > 0, np.frexp(amax)[1] - 1 + 127, 0) - down, 1)
    scale = np.exp2(byte - 127.0)
    codes = (blocks / scale).astype(np.float32).astype(dtype).astype(np.float64)
    return np.moveaxis((codes * scale).reshape(v.shape), -1, axis)


WIDE = False


def mx_kscale(k):
    if not WIDE:
        return np.ones(k)
    levels = np.array([10, -10, 5, -5, 0])
    if k % 512:
        return np.exp2(np.random.permutation(np.resize(levels, k // 32))).repeat(32)
    a = np.empty((k // 512, 16))
    for p in range(k // 512):
        a[p, :8] = np.random.permutation(np.resize(levels, 8))
        for g in range(8):
            far = levels[np.abs(levels - a[p, g]) >= 10]
            a[p, g + 8] = far[np.random.randint(len(far))]
    return np.exp2(a.ravel()).repeat(32)


def f64(x):
    return np.asarray(x).astype(np.float64)


def striped(idx):
    return np.tile(idx.reshape(-1, 16).T, (8, 1)).astype(np.uint16)


def unstriped(offs):
    return offs[:16].T.reshape(-1).astype(np.int64)


def pack_weight(w):
    k, n = w.shape
    w = f64(np.asarray(w, np.float32).astype(ml_dtypes.bfloat16)).reshape(k // 32, 32, n)
    amax = np.abs(w).max(1)
    byte = np.clip(np.where(amax > 0, np.frexp(amax)[1] - 1 + 127 - 7, 1), 1, 254)
    scaled = (w * np.exp2(127.0 - byte)[:, None, :]).reshape(k, n).astype(np.float32)
    words = np.ascontiguousarray(scaled.reshape(k // 512, 128, 4, n).transpose(0, 1, 3, 2)).astype(ml_dtypes.float8_e4m3fn).view(np.uint8)
    return words, np.ascontiguousarray(byte.astype(np.uint8).reshape(k // 512, 16, n))


def unpack_weight(words, scales):
    g, p, n, _ = words.shape
    vals = np.ascontiguousarray(words).view(ml_dtypes.float8_e4m3fn).astype(np.float64) * np.repeat(np.exp2(scales.astype(np.float64) - 127.0), 8, axis=1)[..., None]
    return vals.transpose(0, 1, 3, 2).reshape(g * 512, n)


def relu(v):
    return np.maximum(v, 0.0)


K, T, S, D, V, H, N, U = 512, 2048, 512, 3, 512, 512, 256, 1024
P = 2 ** 7


def setup_inputs():
    n = np.random.standard_normal
    s = mx_kscale(K)[:, None]
    u = mx_kscale(H)
    packed_w2 = pack_weight(n((H, N)) / np.sqrt(H) / u[:, None])
    return {
        "xT": (n((K, T)) * s).astype(np.float32),
        "w1": (n((K, H)) / np.sqrt(K) / s * u).astype(np.float32),
        "w2_words": packed_w2[0],
        "w2_scales": packed_w2[1],
        "gate": np.tile(np.random.uniform(0.2, 0.6, (D, 1, V)), (1, P, 1)).astype(np.float32),
        "emb": (0.5 * n((H, U)) * u[:, None]).astype(np.float32),
        "offs": striped(np.random.permutation(T)[:S]),
        "cell": striped(np.random.permutation(U)[:S]),
        "pos1": striped(np.random.permutation(U)[:V]),
        "pos2": striped(np.random.permutation(U)[:V]),
        "pos3": striped(np.random.permutation(U)[:V]),
    }


def reference(xT, w1, w2_words, w2_scales, gate, emb, offs, cell, pos1, pos2, pos3):
    xq = mxq(f64(xT)[:, unstriped(offs)], 0, "e4m3")
    up = np.zeros((H, U))
    up[:, unstriped(cell)] = relu(mxq(f64(w1), 0, "e4m3").T @ xq)
    z = up + f64(emb)
    y = unpack_weight(w2_words, w2_scales).T @ mxq(z, 0, "e4m3")
    return y[:, unstriped(pos1)] * f64(gate)[0, :1] + y[:, unstriped(pos2)] * f64(gate)[1, :1] + y[:, unstriped(pos3)] * f64(gate)[2, :1]

@@ -1,0 +1,171 @@
+from contextlib import ExitStack
+
+import concourse.mybir as mybir
+
+K, T, S, D, V, H, N, U = 512, 2048, 512, 3, 512, 512, 256, 1024
+FLOPS = 2 * K * H * S + 2 * H * N * U
+
+F32 = mybir.dt.float32
+BF16 = mybir.dt.bfloat16
+I32 = mybir.dt.int32
+U32 = mybir.dt.uint32
+U16 = mybir.dt.uint16
+U8 = mybir.dt.uint8
+FP8X4 = mybir.dt.float8_e4m3fn_x4
+ADD = mybir.AluOpType.add
+MULT = mybir.AluOpType.mult
+RELU = mybir.ActivationFunctionType.Relu
+
+P = 128
+PACK = 4
+HALF = S // 2
+LIST_COLS = 16
+CHUNK = 256
+CHUNKS = U // CHUNK
+
+
+def tile_picked_devox_none_e_kernel(tc, xT, w1, w2_words, w2_scales, gate, emb, offs, cell, pos1, pos2, pos3, out):
+    nc = tc.nc
+    with ExitStack() as ctx:
+        keep = ctx.enter_context(tc.tile_pool(name="keep", bufs=1))
+        psum = ctx.enter_context(tc.psum_pool(name="psum", bufs=8))
+
+        def list_tile(name, src):
+            tile = keep.tile([P, S // LIST_COLS], U16, name=name)
+            nc.sync.dma_start(tile[:], src)
+            return tile
+
+        w1_raw = keep.tile([P, PACK, H], F32, name="w1_raw")
+        nc.sync.dma_start(w1_raw[:], w1.rearrange("(p j) c -> p j c", j=PACK))
+        offs_sb = list_tile("offs_sb", offs)
+        x_rows = xT.rearrange("(p j) t -> j p t", j=PACK)
+        x_planes = []
+        for j in range(PACK):
+            plane = keep.tile([P, T], F32, name="x_plane%d" % j)
+            nc.sync.dma_start(plane[:], x_rows[j])
+            x_planes.append(plane)
+        cell_sb = list_tile("cell_sb", cell)
+        emb_rows = emb.rearrange("(p t) r -> t p r", t=PACK)
+        emb_planes = []
+        for t in range(PACK):
+            plane = keep.tile([P, U], F32, name="emb_plane%d" % t)
+            nc.sync.dma_start(plane[:], emb_rows[t])
+            emb_planes.append(plane)
+        w2_codes = keep.tile([P, N], U32, name="w2_codes", align_bytes=64)
+        nc.sync.dma_start(w2_codes[:].bitcast(I32), w2_words[0].rearrange("p n t -> p (n t)").bitcast(I32))
+        w2_sc = keep.tile([P, N], U8, name="w2_sc", align_bytes=64)
+        nc.vector.memset(w2_sc[:].bitcast(I32), 0)
+        for q in range(4):
+            nc.sync.dma_start(w2_sc[32 * q : 32 * q + 4, :].bitcast(I32), w2_scales[0, 4 * q : 4 * q + 4, :].bitcast(I32))
+        gate_sb = keep.tile([P, D, V], F32, name="gate_sb")
+        nc.sync.dma_start(gate_sb[:], gate.rearrange("d p v -> p d v"))
+        pos_sb = [list_tile("pos%d_sb" % d, src) for d, src in enumerate((pos1, pos2, pos3))]
+
+        up = []
+        for t in range(PACK):
+            tile = keep.tile([P, U], F32, name="up%d" % t)
+            nc.vector.memset(tile[:], 0.0)
+            up.append(tile)
+
+        w1_grouped = keep.tile([P, H * PACK], BF16, name="w1_grouped", align_bytes=64)
+        nc.scalar.copy(w1_grouped[:].rearrange("p (t m j) -> p t m j", t=PACK, j=PACK), w1_raw[:].rearrange("p j (m t) -> p t m j", t=PACK))
+        w1_codes = keep.tile([P, H], U32, name="w1_codes", align_bytes=64)
+        w1_sc = keep.tile([P, H], U8, name="w1_sc", align_bytes=64)
+        nc.vector.quantize_mx(out=w1_codes[:].bitcast(FP8X4), scales=w1_sc[:], in_=w1_grouped[:])
+
+        x_grouped = [keep.tile([P, HALF, PACK], BF16, name="x_grouped%d" % a, align_bytes=64) for a in range(2)]
+        x_codes = [keep.tile([P, HALF], U32, name="x_codes%d" % a, align_bytes=64) for a in range(2)]
+        x_sc = [keep.tile([P, HALF], U8, name="x_sc%d" % a, align_bytes=64) for a in range(2)]
+
+        def half_cols(a):
+            return slice(a * HALF // LIST_COLS, (a + 1) * HALF // LIST_COLS)
+
+        def gather_x(j, a):
+            nc.vector.tensor_copy(x_grouped[a][:, :, j], x_planes[j][:].indirect(offs_sb[:, half_cols(a)]))
+
+        def quantise_x(a):
+            nc.vector.quantize_mx(out=x_codes[a][:].bitcast(FP8X4), scales=x_sc[a][:], in_=x_grouped[a][:].rearrange("p c j -> p (c j)"))
+
+        h = [keep.tile([P, S], F32, name="h%d" % t) for t in range(PACK)]
+
+        def layer1(t, a):
+            acc = psum.tile([P, HALF], F32, name="acc")
+            cols = slice(t * P, (t + 1) * P)
+            nc.tensor.matmul_mx(out=acc[:], lhsT=w1_codes[:, cols].bitcast(FP8X4), lhsT_scale=w1_sc[:, cols], rhs=x_codes[a][:].bitcast(FP8X4), rhs_scale=x_sc[a][:], start=True, stop=True)
+            nc.scalar.activation(h[t][:, a * HALF : (a + 1) * HALF], acc[:], RELU)
+
+        def scatter_half(t, a):
+            nc.vector.tensor_copy(up[t][:].indirect(cell_sb[:, half_cols(a)]), h[t][:, a * HALF : (a + 1) * HALF])
+
+        z_planes = [keep.tile([P, PACK, CHUNK], BF16, name="z_planes%d" % c) for c in range(CHUNKS)]
+
+        def add_emb(engine, t):
+            for c in range(CHUNKS):
+                cols = slice(c * CHUNK, (c + 1) * CHUNK)
+                engine.tensor_tensor(z_planes[c][:, t, :], up[t][:, cols], emb_planes[t][:, cols], ADD)
+
+        for j in range(PACK - 1):
+            for a in range(2):
+                gather_x(j, a)
+        gather_x(PACK - 1, 0)
+        quantise_x(0)
+        for t in range(PACK):
+            layer1(t, 0)
+        gather_x(PACK - 1, 1)
+        scatter_half(0, 0)
+        quantise_x(1)
+        for t in range(PACK):
+            layer1(t, 1)
+        scatter_half(1, 0)
+        scatter_half(0, 1)
+        add_emb(nc.gpsimd, 0)
+        scatter_half(1, 1)
+        add_emb(nc.gpsimd, 1)
+        nc.vector.tensor_copy(up[2][:].indirect(cell_sb[:]), h[2][:])
+        add_emb(nc.gpsimd, 2)
+        nc.vector.tensor_copy(up[3][:].indirect(cell_sb[:]), h[3][:])
+        add_emb(nc.vector, 3)
+
+        z_grouped = [keep.tile([P, CHUNK, PACK], BF16, name="z_grouped%d" % c, align_bytes=64) for c in range(CHUNKS)]
+        z_codes = [keep.tile([P, CHUNK], U32, name="z_codes%d" % c, align_bytes=64) for c in range(CHUNKS)]
+        z_sc = [keep.tile([P, CHUNK], U8, name="z_sc%d" % c, align_bytes=64) for c in range(CHUNKS)]
+        y = [keep.tile([P, U], F32, name="y%d" % b) for b in range(N // P)]
+
+        def weave(c):
+            dst = z_grouped[c][:].rearrange("p (g i) t -> p g t i", i=PACK)
+            src = z_planes[c][:].rearrange("p t (g i) -> p g t i", i=PACK)
+            if c < CHUNKS // 2:
+                nc.scalar.copy(dst, src)
+            else:
+                nc.vector.tensor_copy(dst, src)
+
+        banks = {}
+
+        def layer2(c):
+            nc.vector.quantize_mx(out=z_codes[c][:].bitcast(FP8X4), scales=z_sc[c][:], in_=z_grouped[c][:].rearrange("p c t -> p (c t)"))
+            for b in range(N // P):
+                acc = psum.tile([P, CHUNK], F32, name="acc")
+                cols = slice(b * P, (b + 1) * P)
+                nc.tensor.matmul_mx(out=acc[:], lhsT=w2_codes[:, cols].bitcast(FP8X4), lhsT_scale=w2_sc[:, cols], rhs=z_codes[c][:].bitcast(FP8X4), rhs_scale=z_sc[c][:], start=True, stop=True)
+                banks[(b, c)] = acc
+
+        order = (0, 2, 3, 1)
+        for c in range(CHUNKS):
+            weave(c)
+        for c in order:
+            layer2(c)
+        for b in range(N // P):
+            for c in order:
+                nc.scalar.copy(y[b][:, c * CHUNK : (c + 1) * CHUNK], banks[(b, c)][:])
+
+        for b in range(N // P):
+            terms = []
+            for d in range(D):
+                term = keep.tile([P, V], F32, name="term%d_%d" % (b, d))
+                nc.vector.tensor_tensor(term[:], y[b][:].indirect(pos_sb[d][:]), gate_sb[:, d, :], MULT)
+                terms.append(term)
+            pair = keep.tile([P, V], F32, name="pair%d" % b)
+            nc.vector.tensor_tensor(pair[:], terms[0][:], terms[1][:], ADD)
+            total = keep.tile([P, V], F32, name="total%d" % b)
+            nc.vector.tensor_tensor(total[:], pair[:], terms[2][:], ADD)
+            nc.sync.dma_start(out[b * P : (b + 1) * P, :], total[:])

@@ -1,6 +1,7 @@
 from contextlib import ExitStack
 
 import concourse.mybir as mybir
+from concourse.masks import make_identity
 
 K, T, S, D, V, H, N, U = 512, 2048, 512, 3, 512, 512, 256, 1024
 FLOPS = 2 * K * H * S + 2 * H * N * U
@@ -22,21 +23,28 @@ HALF = S // 2
 LIST_COLS = 16
 CHUNK = 256
 CHUNKS = U // CHUNK
+BANK = 512
+BLOCKS = BANK // P
+LOW, HIGH, THIRD, FOURTH = range(4)
 
 
 def tile_picked_devox_none_e_kernel(tc, xT, w1, w2_words, w2_scales, gate, emb, offs, cell, pos1, pos2, pos3, out):
     nc = tc.nc
     with ExitStack() as ctx:
         keep = ctx.enter_context(tc.tile_pool(name="keep", bufs=1))
-        psum = ctx.enter_context(tc.psum_pool(name="psum", bufs=8))
+        psum = ctx.enter_context(tc.psum_pool(name="psum", bufs=1))
+
+        def bank(number, width=BANK):
+            return psum.tile([P, width], F32, name="bank%d" % number)
 
         def list_tile(name, src):
             tile = keep.tile([P, S // LIST_COLS], U16, name=name)
             nc.sync.dma_start(tile[:], src)
             return tile
 
-        w1_raw = keep.tile([P, PACK, H], F32, name="w1_raw")
-        nc.sync.dma_start(w1_raw[:], w1.rearrange("(p j) c -> p j c", j=PACK))
+        w1_rows = w1.rearrange("(p j) c -> p j c", j=PACK)
+        w1_raw = [keep.tile([P, PACK, H // 2], F32, name="w1_raw%d" % a) for a in range(2)]
+        nc.sync.dma_start(w1_raw[0][:], w1_rows[:, :, : H // 2])
         offs_sb = list_tile("offs_sb", offs)
         x_rows = xT.rearrange("(p j) t -> j p t", j=PACK)
         x_planes = []
@@ -44,13 +52,16 @@ def tile_picked_devox_none_e_kernel(tc, xT, w1, w2_words, w2_scales, gate, emb, 
             plane = keep.tile([P, T], F32, name="x_plane%d" % j)
             nc.sync.dma_start(plane[:], x_rows[j])
             x_planes.append(plane)
+        nc.sync.dma_start(w1_raw[1][:], w1_rows[:, :, H // 2 :])
         cell_sb = list_tile("cell_sb", cell)
+
+        emb_sb = [keep.tile([P, U], F32, name="emb_sb%d" % t) for t in range(PACK)]
+        emb_quads = emb.rearrange("(a q t) r -> a q t r", a=2, t=PACK)
         emb_rows = emb.rearrange("(p t) r -> t p r", t=PACK)
-        emb_planes = []
-        for t in range(PACK):
-            plane = keep.tile([P, U], F32, name="emb_plane%d" % t)
-            nc.sync.dma_start(plane[:], emb_rows[t])
-            emb_planes.append(plane)
+        nc.sync.dma_start(emb_sb[LOW][:], emb_quads[0, :, 0:2, :])
+        nc.sync.dma_start(emb_sb[HIGH][:], emb_quads[1, :, 0:2, :])
+        nc.sync.dma_start(emb_sb[THIRD][:], emb_rows[2])
+        nc.sync.dma_start(emb_sb[FOURTH][:], emb_rows[3])
         w2_codes = keep.tile([P, N], U32, name="w2_codes", align_bytes=64)
         nc.sync.dma_start(w2_codes[:].bitcast(I32), w2_words[0].rearrange("p n t -> p (n t)").bitcast(I32))
         w2_sc = keep.tile([P, N], U8, name="w2_sc", align_bytes=64)
@@ -61,17 +72,29 @@ def tile_picked_devox_none_e_kernel(tc, xT, w1, w2_words, w2_scales, gate, emb, 
         nc.sync.dma_start(gate_sb[:], gate.rearrange("d p v -> p d v"))
         pos_sb = [list_tile("pos%d_sb" % d, src) for d, src in enumerate((pos1, pos2, pos3))]
 
+        ident = keep.tile([P, P], F32, name="ident")
+        make_identity(nc, ident[:])
+
         up = []
         for t in range(PACK):
             tile = keep.tile([P, U], F32, name="up%d" % t)
             nc.vector.memset(tile[:], 0.0)
             up.append(tile)
 
-        w1_grouped = keep.tile([P, H * PACK], BF16, name="w1_grouped", align_bytes=64)
-        nc.scalar.copy(w1_grouped[:].rearrange("p (t m j) -> p t m j", t=PACK, j=PACK), w1_raw[:].rearrange("p j (m t) -> p t m j", t=PACK))
+        w1_grouped = [keep.tile([P, P * PACK], BF16, name="w1_grouped0", align_bytes=64), keep.tile([P, P * PACK], BF16, name="w1_grouped1", align_bytes=64), keep.tile([P, 2 * P * PACK], BF16, name="w1_grouped2", align_bytes=64)]
+        w1_dst = {LOW: w1_grouped[0][:], HIGH: w1_grouped[1][:], THIRD: w1_grouped[2][:, : P * PACK], FOURTH: w1_grouped[2][:, P * PACK :]}
         w1_codes = keep.tile([P, H], U32, name="w1_codes", align_bytes=64)
         w1_sc = keep.tile([P, H], U8, name="w1_sc", align_bytes=64)
-        nc.vector.quantize_mx(out=w1_codes[:].bitcast(FP8X4), scales=w1_sc[:], in_=w1_grouped[:])
+
+        def deal_w1(a):
+            quads = w1_raw[a][:].rearrange("p j (q t) -> p q t j", t=PACK)
+            nc.scalar.copy(w1_dst[(LOW, HIGH)[a]].rearrange("p (q e j) -> p q e j", e=2, j=PACK), quads[:, :, 0:2, :])
+            for t in (THIRD, FOURTH):
+                nc.scalar.copy(w1_dst[t].rearrange("p (a q j) -> p a q j", a=2, j=PACK)[:, a], quads[:, :, t, :])
+
+        def quantise_w1(g, first, count):
+            cols = slice(first * P, (first + count) * P)
+            nc.vector.quantize_mx(out=w1_codes[:, cols].bitcast(FP8X4), scales=w1_sc[:, cols], in_=w1_grouped[g][:])
 
         x_grouped = [keep.tile([P, HALF, PACK], BF16, name="x_grouped%d" % a, align_bytes=64) for a in range(2)]
         x_codes = [keep.tile([P, HALF], U32, name="x_codes%d" % a, align_bytes=64) for a in range(2)]
@@ -89,7 +112,7 @@ def tile_picked_devox_none_e_kernel(tc, xT, w1, w2_words, w2_scales, gate, emb, 
         h = [keep.tile([P, S], F32, name="h%d" % t) for t in range(PACK)]
 
         def layer1(t, a):
-            acc = psum.tile([P, HALF], F32, name="acc")
+            acc = bank((2 * t + a) % 4, HALF)
             cols = slice(t * P, (t + 1) * P)
             nc.tensor.matmul_mx(out=acc[:], lhsT=w1_codes[:, cols].bitcast(FP8X4), lhsT_scale=w1_sc[:, cols], rhs=x_codes[a][:].bitcast(FP8X4), rhs_scale=x_sc[a][:], start=True, stop=True)
             nc.scalar.activation(h[t][:, a * HALF : (a + 1) * HALF], acc[:], RELU)
@@ -97,75 +120,112 @@ def tile_picked_devox_none_e_kernel(tc, xT, w1, w2_words, w2_scales, gate, emb, 
         def scatter_half(t, a):
             nc.vector.tensor_copy(up[t][:].indirect(cell_sb[:, half_cols(a)]), h[t][:, a * HALF : (a + 1) * HALF])
 
+        def turn(dst, src, first, last):
+            blocks = src.shape[1] // P
+            for k in range(blocks):
+                cols = slice(k * P, (k + 1) * P)
+                nc.tensor.matmul(dst[:, cols], src[:, cols], ident[:], start=first and k == 0, stop=last and k == blocks - 1, is_transpose=True)
+
+        pairs_turned = [keep.tile([P, BLOCKS, 2 * P], BF16, name="pairs_turned%d" % g) for g in range(U // BANK)]
         z_planes = [keep.tile([P, PACK, CHUNK], BF16, name="z_planes%d" % c) for c in range(CHUNKS)]
 
-        def add_emb(engine, t):
+        def add_turned(t):
+            sums = [bank(4 + 2 * t + g) for g in range(U // BANK)]
+            for g in range(U // BANK):
+                turn(sums[g], emb_sb[t][:, g * BANK : (g + 1) * BANK], True, False)
+            for g in range(U // BANK):
+                turn(sums[g], up[t][:, g * BANK : (g + 1) * BANK], False, True)
+                nc.scalar.copy(pairs_turned[g][:, :, t * P : (t + 1) * P], sums[g][:].rearrange("r (k m) -> r k m", m=P))
+
+        def add_plain(engine, t):
             for c in range(CHUNKS):
                 cols = slice(c * CHUNK, (c + 1) * CHUNK)
-                engine.tensor_tensor(z_planes[c][:, t, :], up[t][:, cols], emb_planes[t][:, cols], ADD)
+                engine.tensor_tensor(z_planes[c][:, t, :], up[t][:, cols], emb_sb[t][:, cols], ADD)
 
+        def scatter(t):
+            nc.vector.tensor_copy(up[t][:].indirect(cell_sb[:]), h[t][:])
+
+        deal_w1(0)
+        quantise_w1(0, LOW, 1)
         for j in range(PACK - 1):
             for a in range(2):
                 gather_x(j, a)
         gather_x(PACK - 1, 0)
         quantise_x(0)
-        for t in range(PACK):
-            layer1(t, 0)
+        layer1(LOW, 0)
         gather_x(PACK - 1, 1)
-        scatter_half(0, 0)
+        deal_w1(1)
         quantise_x(1)
-        for t in range(PACK):
-            layer1(t, 1)
-        scatter_half(1, 0)
-        scatter_half(0, 1)
-        add_emb(nc.gpsimd, 0)
-        scatter_half(1, 1)
-        add_emb(nc.gpsimd, 1)
-        nc.vector.tensor_copy(up[2][:].indirect(cell_sb[:]), h[2][:])
-        add_emb(nc.gpsimd, 2)
-        nc.vector.tensor_copy(up[3][:].indirect(cell_sb[:]), h[3][:])
-        add_emb(nc.vector, 3)
+        layer1(LOW, 1)
+        scatter_half(LOW, 0)
+        quantise_w1(1, HIGH, 1)
+        quantise_w1(2, THIRD, 2)
+        for t in (HIGH, THIRD, FOURTH):
+            for a in range(2):
+                layer1(t, a)
+        scatter_half(LOW, 1)
+        add_turned(LOW)
+        scatter(HIGH)
+        add_turned(HIGH)
+        for g in range(U // BANK):
+            acc = bank(g)
+            turn(acc, pairs_turned[g][:].rearrange("r k c -> r (k c)").bitcast(F32), True, True)
+            halves = acc[:].bitcast(BF16).rearrange("p (r e) -> p e r", e=2)
+            for e in range(BANK // CHUNK):
+                nc.scalar.copy(z_planes[g * (BANK // CHUNK) + e][:, 0:2, :], halves[:, :, e * CHUNK : (e + 1) * CHUNK])
+        scatter(THIRD)
+        add_plain(nc.gpsimd, THIRD)
+        scatter(FOURTH)
+        add_plain(nc.vector, FOURTH)
 
         z_grouped = [keep.tile([P, CHUNK, PACK], BF16, name="z_grouped%d" % c, align_bytes=64) for c in range(CHUNKS)]
         z_codes = [keep.tile([P, CHUNK], U32, name="z_codes%d" % c, align_bytes=64) for c in range(CHUNKS)]
         z_sc = [keep.tile([P, CHUNK], U8, name="z_sc%d" % c, align_bytes=64) for c in range(CHUNKS)]
         y = [keep.tile([P, U], F32, name="y%d" % b) for b in range(N // P)]
 
-        def weave(c):
-            dst = z_grouped[c][:].rearrange("p (g i) t -> p g t i", i=PACK)
-            src = z_planes[c][:].rearrange("p t (g i) -> p g t i", i=PACK)
-            if c < CHUNKS // 2:
-                nc.scalar.copy(dst, src)
-            else:
-                nc.vector.tensor_copy(dst, src)
-
-        banks = {}
-
-        def layer2(c):
-            nc.vector.quantize_mx(out=z_codes[c][:].bitcast(FP8X4), scales=z_sc[c][:], in_=z_grouped[c][:].rearrange("p c t -> p (c t)"))
-            for b in range(N // P):
-                acc = psum.tile([P, CHUNK], F32, name="acc")
-                cols = slice(b * P, (b + 1) * P)
-                nc.tensor.matmul_mx(out=acc[:], lhsT=w2_codes[:, cols].bitcast(FP8X4), lhsT_scale=w2_sc[:, cols], rhs=z_codes[c][:].bitcast(FP8X4), rhs_scale=z_sc[c][:], start=True, stop=True)
-                banks[(b, c)] = acc
-
-        order = (0, 2, 3, 1)
         for c in range(CHUNKS):
-            weave(c)
-        for c in order:
-            layer2(c)
-        for b in range(N // P):
-            for c in order:
-                nc.scalar.copy(y[b][:, c * CHUNK : (c + 1) * CHUNK], banks[(b, c)][:])
+            weave = nc.scalar.copy if c < CHUNKS // 2 else nc.vector.tensor_copy
+            weave(z_grouped[c][:].rearrange("p (g i) t -> p g t i", i=PACK), z_planes[c][:].rearrange("p t (g i) -> p g t i", i=PACK))
 
-        for b in range(N // P):
-            terms = []
-            for d in range(D):
-                term = keep.tile([P, V], F32, name="term%d_%d" % (b, d))
-                nc.vector.tensor_tensor(term[:], y[b][:].indirect(pos_sb[d][:]), gate_sb[:, d, :], MULT)
-                terms.append(term)
-            pair = keep.tile([P, V], F32, name="pair%d" % b)
-            nc.vector.tensor_tensor(pair[:], terms[0][:], terms[1][:], ADD)
-            total = keep.tile([P, V], F32, name="total%d" % b)
-            nc.vector.tensor_tensor(total[:], pair[:], terms[2][:], ADD)
-            nc.sync.dma_start(out[b * P : (b + 1) * P, :], total[:])
+        def layer2(acc, b, c):
+            cols = slice(b * P, (b + 1) * P)
+            nc.tensor.matmul_mx(out=acc, lhsT=w2_codes[:, cols].bitcast(FP8X4), lhsT_scale=w2_sc[:, cols], rhs=z_codes[c][:].bitcast(FP8X4), rhs_scale=z_sc[c][:], start=True, stop=True)
+
+        late_banks = [bank(2 + g) for g in range(U // BANK)]
+        for c in (0, 2, 3, 1):
+            nc.vector.quantize_mx(out=z_codes[c][:].bitcast(FP8X4), scales=z_sc[c][:], in_=z_grouped[c][:].rearrange("p c t -> p (c t)"))
+            acc = bank(4 + c, CHUNK)
+            layer2(acc[:], 0, c)
+            unload = nc.vector.tensor_copy if c == 1 else nc.scalar.copy
+            unload(y[0][:, c * CHUNK : (c + 1) * CHUNK], acc[:])
+            e = c % (BANK // CHUNK)
+            layer2(late_banks[c // (BANK // CHUNK)][:, e * CHUNK : (e + 1) * CHUNK], 1, c)
+        for g in range(U // BANK):
+            nc.scalar.copy(y[1][:, g * BANK : (g + 1) * BANK], late_banks[g][:])
+
+        def weighted(b, d, first, count):
+            term = keep.tile([P, count], F32, name="term%d_%d_%d" % (b, d, first))
+            nc.vector.tensor_tensor(term[:], y[b][:].indirect(pos_sb[d][:, first // LIST_COLS : (first + count) // LIST_COLS]), gate_sb[:, d, first : first + count], MULT)
+            return term
+
+        sum_turned = bank(0)
+        for d in range(D):
+            turn(sum_turned, weighted(0, d, 0, V), d == 0, d == D - 1)
+        sum_sb = keep.tile([P, V], F32, name="sum_sb")
+        nc.scalar.copy(sum_sb[:], sum_turned[:])
+        sum_back = bank(1)
+        turn(sum_back, sum_sb, True, True)
+        result0 = keep.tile([P, V], F32, name="result0")
+        nc.scalar.copy(result0[:], sum_back[:])
+        nc.sync.dma_start(out[0:P, :], result0[:])
+
+        terms = [weighted(1, d, 0, V) for d in range(D - 1)]
+        last = [weighted(1, D - 1, 0, V // 2)]
+        pair = keep.tile([P, V], F32, name="pair")
+        nc.vector.tensor_tensor(pair[:], terms[0][:], terms[1][:], ADD)
+        last.append(weighted(1, D - 1, V // 2, V // 2))
+        for a in range(2):
+            cols = slice(a * V // 2, (a + 1) * V // 2)
+            result1 = keep.tile([P, V // 2], F32, name="result1_%d" % a)
+            nc.vector.tensor_tensor(result1[:], pair[:, cols], last[a][:], ADD)
+            nc.sync.dma_start(out[P : 2 * P, cols], result1[:])

@@ -82,15 +82,13 @@ def tile_picked_devox_none_e_kernel(tc, xT, w1, w2_words, w2_scales, gate, emb, 
             up.append(tile)
 
         w1_grouped = [keep.tile([P, P * PACK], BF16, name="w1_grouped0", align_bytes=64), keep.tile([P, P * PACK], BF16, name="w1_grouped1", align_bytes=64), keep.tile([P, 2 * P * PACK], BF16, name="w1_grouped2", align_bytes=64)]
-        w1_dst = {LOW: w1_grouped[0][:], HIGH: w1_grouped[1][:], THIRD: w1_grouped[2][:, : P * PACK], FOURTH: w1_grouped[2][:, P * PACK :]}
         w1_codes = keep.tile([P, H], U32, name="w1_codes", align_bytes=64)
         w1_sc = keep.tile([P, H], U8, name="w1_sc", align_bytes=64)
 
         def deal_w1(a):
             quads = w1_raw[a][:].rearrange("p j (q t) -> p q t j", t=PACK)
-            nc.scalar.copy(w1_dst[(LOW, HIGH)[a]].rearrange("p (q e j) -> p q e j", e=2, j=PACK), quads[:, :, 0:2, :])
-            for t in (THIRD, FOURTH):
-                nc.scalar.copy(w1_dst[t].rearrange("p (a q j) -> p a q j", a=2, j=PACK)[:, a], quads[:, :, t, :])
+            nc.scalar.copy(w1_grouped[a][:].rearrange("p (q e j) -> p q e j", e=2, j=PACK), quads[:, :, 0:2, :])
+            nc.scalar.copy(w1_grouped[2][:].rearrange("p (e a q j) -> p a q e j", e=2, a=2, j=PACK)[:, a], quads[:, :, 2:4, :])
 
         def quantise_w1(g, first, count):
             cols = slice(first * P, (first + count) * P)
@@ -178,54 +176,63 @@ def tile_picked_devox_none_e_kernel(tc, xT, w1, w2_words, w2_scales, gate, emb, 
         scatter(FOURTH)
         add_plain(nc.vector, FOURTH)
 
-        z_grouped = [keep.tile([P, CHUNK, PACK], BF16, name="z_grouped%d" % c, align_bytes=64) for c in range(CHUNKS)]
-        z_codes = [keep.tile([P, CHUNK], U32, name="z_codes%d" % c, align_bytes=64) for c in range(CHUNKS)]
-        z_sc = [keep.tile([P, CHUNK], U8, name="z_sc%d" % c, align_bytes=64) for c in range(CHUNKS)]
         y = [keep.tile([P, U], F32, name="y%d" % b) for b in range(N // P)]
+        pieces = [(0, CHUNK), (2 * CHUNK, CHUNK), (3 * CHUNK, CHUNK), (CHUNK, CHUNK // 2), (CHUNK + CHUNK // 2, CHUNK // 2)]
+        z_grouped = {}
+        for first, count in sorted(pieces):
+            z_grouped[first] = keep.tile([P, count, PACK], BF16, name="z_grouped%d" % first, align_bytes=64)
+            planes = z_planes[first // CHUNK][:, :, first % CHUNK : first % CHUNK + count]
+            if first < U // 2:
+                nc.scalar.copy(z_grouped[first][:].rearrange("p (g i) t -> p g t i", i=PACK), planes.rearrange("p t (g i) -> p g t i", i=PACK))
+            else:
+                nc.vector.tensor_copy(z_grouped[first][:], planes.rearrange("p t r -> p r t"))
 
-        for c in range(CHUNKS):
-            weave = nc.scalar.copy if c < CHUNKS // 2 else nc.vector.tensor_copy
-            weave(z_grouped[c][:].rearrange("p (g i) t -> p g t i", i=PACK), z_planes[c][:].rearrange("p t (g i) -> p g t i", i=PACK))
+        z_codes = {}
+        z_sc = {}
 
-        def layer2(acc, b, c):
+        def layer2(dst, b, first):
             cols = slice(b * P, (b + 1) * P)
-            nc.tensor.matmul_mx(out=acc, lhsT=w2_codes[:, cols].bitcast(FP8X4), lhsT_scale=w2_sc[:, cols], rhs=z_codes[c][:].bitcast(FP8X4), rhs_scale=z_sc[c][:], start=True, stop=True)
+            nc.tensor.matmul_mx(out=dst, lhsT=w2_codes[:, cols].bitcast(FP8X4), lhsT_scale=w2_sc[:, cols], rhs=z_codes[first][:].bitcast(FP8X4), rhs_scale=z_sc[first][:], start=True, stop=True)
 
-        late_banks = [bank(2 + g) for g in range(U // BANK)]
-        for c in (0, 2, 3, 1):
-            nc.vector.quantize_mx(out=z_codes[c][:].bitcast(FP8X4), scales=z_sc[c][:], in_=z_grouped[c][:].rearrange("p c t -> p (c t)"))
-            acc = bank(4 + c, CHUNK)
-            layer2(acc[:], 0, c)
-            unload = nc.vector.tensor_copy if c == 1 else nc.scalar.copy
-            unload(y[0][:, c * CHUNK : (c + 1) * CHUNK], acc[:])
-            e = c % (BANK // CHUNK)
-            layer2(late_banks[c // (BANK // CHUNK)][:, e * CHUNK : (e + 1) * CHUNK], 1, c)
+        for n, (first, count) in enumerate(pieces):
+            z_codes[first] = keep.tile([P, count], U32, name="z_codes%d" % first, align_bytes=64)
+            z_sc[first] = keep.tile([P, count], U8, name="z_sc%d" % first, align_bytes=64)
+            nc.vector.quantize_mx(out=z_codes[first][:].bitcast(FP8X4), scales=z_sc[first][:], in_=z_grouped[first][:].rearrange("p c t -> p (c t)"))
+            acc = bank(n, count)
+            layer2(acc[:], 0, first)
+            unload = nc.vector.tensor_copy if n == len(pieces) - 1 else nc.scalar.copy
+            unload(y[0][:, first : first + count], acc[:])
         for g in range(U // BANK):
-            nc.scalar.copy(y[1][:, g * BANK : (g + 1) * BANK], late_banks[g][:])
+            acc = bank(len(pieces) - 2 + g)
+            for first, count in sorted(pieces):
+                if first // BANK == g:
+                    layer2(acc[:, first % BANK : first % BANK + count], 1, first)
+            nc.scalar.copy(y[1][:, g * BANK : (g + 1) * BANK], acc[:])
 
         def weighted(b, d, first, count):
             term = keep.tile([P, count], F32, name="term%d_%d_%d" % (b, d, first))
             nc.vector.tensor_tensor(term[:], y[b][:].indirect(pos_sb[d][:, first // LIST_COLS : (first + count) // LIST_COLS]), gate_sb[:, d, first : first + count], MULT)
             return term
 
-        sum_turned = bank(0)
+        sum_turned = bank(5)
         for d in range(D):
             turn(sum_turned, weighted(0, d, 0, V), d == 0, d == D - 1)
         sum_sb = keep.tile([P, V], F32, name="sum_sb")
         nc.scalar.copy(sum_sb[:], sum_turned[:])
-        sum_back = bank(1)
+        sum_back = bank(6)
         turn(sum_back, sum_sb, True, True)
         result0 = keep.tile([P, V], F32, name="result0")
         nc.scalar.copy(result0[:], sum_back[:])
         nc.sync.dma_start(out[0:P, :], result0[:])
 
         terms = [weighted(1, d, 0, V) for d in range(D - 1)]
-        last = [weighted(1, D - 1, 0, V // 2)]
+        parts = [(0, 3 * V // 4), (3 * V // 4, V // 4)]
+        last = [weighted(1, D - 1, *parts[0])]
         pair = keep.tile([P, V], F32, name="pair")
         nc.vector.tensor_tensor(pair[:], terms[0][:], terms[1][:], ADD)
-        last.append(weighted(1, D - 1, V // 2, V // 2))
-        for a in range(2):
-            cols = slice(a * V // 2, (a + 1) * V // 2)
-            result1 = keep.tile([P, V // 2], F32, name="result1_%d" % a)
+        last.append(weighted(1, D - 1, *parts[1]))
+        for a, (first, count) in enumerate(parts):
+            cols = slice(first, first + count)
+            result1 = keep.tile([P, count], F32, name="result1_%d" % a)
             nc.vector.tensor_tensor(result1[:], pair[:, cols], last[a][:], ADD)
             nc.sync.dma_start(out[P : 2 * P, cols], result1[:])

@@ -22,7 +22,6 @@ PACK = 4
 HALF = S // 2
 LIST_COLS = 16
 CHUNK = 256
-CHUNKS = U // CHUNK
 BANK = 512
 BLOCKS = BANK // P
 LOW, HIGH, THIRD, FOURTH = range(4)
@@ -44,24 +43,23 @@ def tile_picked_devox_none_e_kernel(tc, xT, w1, w2_words, w2_scales, gate, emb, 
 
         w1_rows = w1.rearrange("(p j) c -> p j c", j=PACK)
         w1_raw = [keep.tile([P, PACK, H // 2], F32, name="w1_raw%d" % a) for a in range(2)]
-        nc.sync.dma_start(w1_raw[0][:], w1_rows[:, :, : H // 2])
-        offs_sb = list_tile("offs_sb", offs)
         x_rows = xT.rearrange("(p j) t -> j p t", j=PACK)
         x_planes = []
         for j in range(PACK):
             plane = keep.tile([P, T], F32, name="x_plane%d" % j)
             nc.sync.dma_start(plane[:], x_rows[j])
             x_planes.append(plane)
-        nc.sync.dma_start(w1_raw[1][:], w1_rows[:, :, H // 2 :])
+            if j == 0:
+                offs_sb = list_tile("offs_sb", offs)
+        nc.sync.dma_start(w1_raw[0][:], w1_rows[:, :, : H // 2])
         cell_sb = list_tile("cell_sb", cell)
+        nc.sync.dma_start(w1_raw[1][:], w1_rows[:, :, H // 2 :])
 
         emb_sb = [keep.tile([P, U], F32, name="emb_sb%d" % t) for t in range(PACK)]
         emb_quads = emb.rearrange("(a q t) r -> a q t r", a=2, t=PACK)
         emb_rows = emb.rearrange("(p t) r -> t p r", t=PACK)
         nc.sync.dma_start(emb_sb[LOW][:], emb_quads[0, :, 0:2, :])
         nc.sync.dma_start(emb_sb[HIGH][:], emb_quads[1, :, 0:2, :])
-        nc.sync.dma_start(emb_sb[THIRD][:], emb_rows[2])
-        nc.sync.dma_start(emb_sb[FOURTH][:], emb_rows[3])
         w2_codes = keep.tile([P, N], U32, name="w2_codes", align_bytes=64)
         nc.sync.dma_start(w2_codes[:].bitcast(I32), w2_words[0].rearrange("p n t -> p (n t)").bitcast(I32))
         w2_sc = keep.tile([P, N], U8, name="w2_sc", align_bytes=64)
@@ -71,6 +69,8 @@ def tile_picked_devox_none_e_kernel(tc, xT, w1, w2_words, w2_scales, gate, emb, 
         gate_sb = keep.tile([P, D, V], F32, name="gate_sb")
         nc.sync.dma_start(gate_sb[:], gate.rearrange("d p v -> p d v"))
         pos_sb = [list_tile("pos%d_sb" % d, src) for d, src in enumerate((pos1, pos2, pos3))]
+        nc.sync.dma_start(emb_sb[THIRD][:], emb_rows[2])
+        nc.sync.dma_start(emb_sb[FOURTH][:], emb_rows[3])
 
         ident = keep.tile([P, P], F32, name="ident")
         make_identity(nc, ident[:])
@@ -109,14 +109,15 @@ def tile_picked_devox_none_e_kernel(tc, xT, w1, w2_words, w2_scales, gate, emb, 
 
         h = [keep.tile([P, S], F32, name="h%d" % t) for t in range(PACK)]
 
-        def layer1(t, a):
-            acc = bank((2 * t + a) % 4, HALF)
+        def layer1(t, first, count, number):
+            acc = bank(number, count)
             cols = slice(t * P, (t + 1) * P)
-            nc.tensor.matmul_mx(out=acc[:], lhsT=w1_codes[:, cols].bitcast(FP8X4), lhsT_scale=w1_sc[:, cols], rhs=x_codes[a][:].bitcast(FP8X4), rhs_scale=x_sc[a][:], start=True, stop=True)
-            nc.scalar.activation(h[t][:, a * HALF : (a + 1) * HALF], acc[:], RELU)
+            a, points = first // HALF, slice(first % HALF, first % HALF + count)
+            nc.tensor.matmul_mx(out=acc[:], lhsT=w1_codes[:, cols].bitcast(FP8X4), lhsT_scale=w1_sc[:, cols], rhs=x_codes[a][:, points].bitcast(FP8X4), rhs_scale=x_sc[a][:, points], start=True, stop=True)
+            nc.scalar.activation(h[t][:, first : first + count], acc[:], RELU)
 
-        def scatter_half(t, a):
-            nc.vector.tensor_copy(up[t][:].indirect(cell_sb[:, half_cols(a)]), h[t][:, a * HALF : (a + 1) * HALF])
+        def scatter_part(t, first, count):
+            nc.vector.tensor_copy(up[t][:].indirect(cell_sb[:, first // LIST_COLS : (first + count) // LIST_COLS]), h[t][:, first : first + count])
 
         def turn(dst, src, first, last):
             blocks = src.shape[1] // P
@@ -125,7 +126,9 @@ def tile_picked_devox_none_e_kernel(tc, xT, w1, w2_words, w2_scales, gate, emb, 
                 nc.tensor.matmul(dst[:, cols], src[:, cols], ident[:], start=first and k == 0, stop=last and k == blocks - 1, is_transpose=True)
 
         pairs_turned = [keep.tile([P, BLOCKS, 2 * P], BF16, name="pairs_turned%d" % g) for g in range(U // BANK)]
-        z_planes = [keep.tile([P, PACK, CHUNK], BF16, name="z_planes%d" % c) for c in range(CHUNKS)]
+        pieces = [(0, CHUNK), (2 * CHUNK, CHUNK), (3 * CHUNK, CHUNK), (CHUNK, CHUNK // 2), (CHUNK + CHUNK // 2, CHUNK // 2)]
+        z_planes = {first: keep.tile([P, 2, count], BF16, name="z_planes%d" % first) for first, count in pieces}
+        z_grouped = {first: keep.tile([P, count, PACK], BF16, name="z_grouped%d" % first, align_bytes=64) for first, count in pieces}
 
         def add_turned(t):
             sums = [bank(4 + 2 * t + g) for g in range(U // BANK)]
@@ -136,56 +139,51 @@ def tile_picked_devox_none_e_kernel(tc, xT, w1, w2_words, w2_scales, gate, emb, 
                 nc.scalar.copy(pairs_turned[g][:, :, t * P : (t + 1) * P], sums[g][:].rearrange("r (k m) -> r k m", m=P))
 
         def add_plain(engine, t):
-            for c in range(CHUNKS):
-                cols = slice(c * CHUNK, (c + 1) * CHUNK)
-                engine.tensor_tensor(z_planes[c][:, t, :], up[t][:, cols], emb_sb[t][:, cols], ADD)
+            for first, count in sorted(pieces):
+                cols = slice(first, first + count)
+                engine.tensor_tensor(z_planes[first][:, t - THIRD, :], up[t][:, cols], emb_sb[t][:, cols], ADD)
 
         def scatter(t):
             nc.vector.tensor_copy(up[t][:].indirect(cell_sb[:]), h[t][:])
 
-        deal_w1(0)
-        quantise_w1(0, LOW, 1)
-        for j in range(PACK - 1):
+        for j in range(PACK):
             for a in range(2):
                 gather_x(j, a)
-        gather_x(PACK - 1, 0)
+        deal_w1(0)
         quantise_x(0)
-        layer1(LOW, 0)
-        gather_x(PACK - 1, 1)
-        deal_w1(1)
+        quantise_w1(0, LOW, 1)
+        layer1(LOW, 0, HALF // 2, 0)
+        layer1(LOW, HALF // 2, HALF // 2, 1)
         quantise_x(1)
-        layer1(LOW, 1)
-        scatter_half(LOW, 0)
+        layer1(LOW, HALF, HALF, 2)
+        deal_w1(1)
+        scatter_part(LOW, 0, HALF // 2)
+        scatter_part(LOW, HALF // 2, HALF // 2)
         quantise_w1(1, HIGH, 1)
         quantise_w1(2, THIRD, 2)
         for t in (HIGH, THIRD, FOURTH):
             for a in range(2):
-                layer1(t, a)
-        scatter_half(LOW, 1)
+                layer1(t, a * HALF, HALF, (2 * t + a + 1) % 4)
+        scatter_part(LOW, HALF, HALF)
         add_turned(LOW)
         scatter(HIGH)
         add_turned(HIGH)
         for g in range(U // BANK):
             acc = bank(g)
             turn(acc, pairs_turned[g][:].rearrange("r k c -> r (k c)").bitcast(F32), True, True)
-            halves = acc[:].bitcast(BF16).rearrange("p (r e) -> p e r", e=2)
-            for e in range(BANK // CHUNK):
-                nc.scalar.copy(z_planes[g * (BANK // CHUNK) + e][:, 0:2, :], halves[:, :, e * CHUNK : (e + 1) * CHUNK])
+            halves = acc[:].bitcast(BF16).rearrange("p (r e) -> p r e", e=2)
+            for first, count in sorted(pieces):
+                if first // BANK == g:
+                    nc.scalar.copy(z_grouped[first][:, :, 0:2], halves[:, first % BANK : first % BANK + count, :])
         scatter(THIRD)
         add_plain(nc.gpsimd, THIRD)
         scatter(FOURTH)
         add_plain(nc.vector, FOURTH)
 
         y = [keep.tile([P, U], F32, name="y%d" % b) for b in range(N // P)]
-        pieces = [(0, CHUNK), (2 * CHUNK, CHUNK), (3 * CHUNK, CHUNK), (CHUNK, CHUNK // 2), (CHUNK + CHUNK // 2, CHUNK // 2)]
-        z_grouped = {}
         for first, count in sorted(pieces):
-            z_grouped[first] = keep.tile([P, count, PACK], BF16, name="z_grouped%d" % first, align_bytes=64)
-            planes = z_planes[first // CHUNK][:, :, first % CHUNK : first % CHUNK + count]
-            if first < U // 2:
-                nc.scalar.copy(z_grouped[first][:].rearrange("p (g i) t -> p g t i", i=PACK), planes.rearrange("p t (g i) -> p g t i", i=PACK))
-            else:
-                nc.vector.tensor_copy(z_grouped[first][:], planes.rearrange("p t r -> p r t"))
+            place = nc.scalar.copy if first < U // 2 else nc.vector.tensor_copy
+            place(z_grouped[first][:, :, 2:4], z_planes[first][:].rearrange("p t r -> p r t"))
 
         z_codes = {}
         z_sc = {}

@@ -42,7 +42,8 @@ def tile_picked_devox_none_e_kernel(tc, xT, w1, w2_words, w2_scales, gate, emb, 
             return tile
 
         w1_rows = w1.rearrange("(p j) c -> p j c", j=PACK)
-        w1_raw = [keep.tile([P, PACK, H // 2], F32, name="w1_raw%d" % a) for a in range(2)]
+        w1_first = [keep.tile([P, 2, H // 2], F32, name="w1_first%d" % u) for u in range(2)]
+        w1_second = keep.tile([P, PACK, H // 2], F32, name="w1_second")
         x_rows = xT.rearrange("(p j) t -> j p t", j=PACK)
         x_planes = []
         for j in range(PACK):
@@ -51,9 +52,10 @@ def tile_picked_devox_none_e_kernel(tc, xT, w1, w2_words, w2_scales, gate, emb, 
             x_planes.append(plane)
             if j == 0:
                 offs_sb = list_tile("offs_sb", offs)
-        nc.sync.dma_start(w1_raw[0][:], w1_rows[:, :, : H // 2])
+        for u in range(2):
+            nc.sync.dma_start(w1_first[u][:], w1_rows[:, 2 * u : 2 * u + 2, : H // 2])
         cell_sb = list_tile("cell_sb", cell)
-        nc.sync.dma_start(w1_raw[1][:], w1_rows[:, :, H // 2 :])
+        nc.sync.dma_start(w1_second[:], w1_rows[:, :, H // 2 :])
 
         emb_sb = [keep.tile([P, U], F32, name="emb_sb%d" % t) for t in range(PACK)]
         emb_quads = emb.rearrange("(a q t) r -> a q t r", a=2, t=PACK)
@@ -81,21 +83,23 @@ def tile_picked_devox_none_e_kernel(tc, xT, w1, w2_words, w2_scales, gate, emb, 
             nc.vector.memset(tile[:], 0.0)
             up.append(tile)
 
-        w1_grouped = [keep.tile([P, P * PACK], BF16, name="w1_grouped0", align_bytes=64), keep.tile([P, P * PACK], BF16, name="w1_grouped1", align_bytes=64), keep.tile([P, 2 * P * PACK], BF16, name="w1_grouped2", align_bytes=64)]
-        w1_codes = keep.tile([P, H], U32, name="w1_codes", align_bytes=64)
-        w1_sc = keep.tile([P, H], U8, name="w1_sc", align_bytes=64)
+        def deal(dst, raw, slots):
+            quads = raw[:].rearrange("p j (q t) -> p q t j", t=PACK)
+            nc.scalar.copy(dst, quads[:, :, slots, :])
 
-        def deal_w1(a):
-            quads = w1_raw[a][:].rearrange("p j (q t) -> p q t j", t=PACK)
-            nc.scalar.copy(w1_grouped[a][:].rearrange("p (q e j) -> p q e j", e=2, j=PACK), quads[:, :, 0:2, :])
-            nc.scalar.copy(w1_grouped[2][:].rearrange("p (e a q j) -> p a q e j", e=2, a=2, j=PACK)[:, a], quads[:, :, 2:4, :])
+        def staged(name, shape, dtype):
+            return keep.tile(shape, dtype, name=name, tag="w1_stage", align_bytes=64)
 
-        def quantise_w1(g, first, count):
-            cols = slice(first * P, (first + count) * P)
-            nc.vector.quantize_mx(out=w1_codes[:, cols].bitcast(FP8X4), scales=w1_sc[:, cols], in_=w1_grouped[g][:])
+        def quantise(name, grouped, codes=None):
+            count = grouped.shape[1] // PACK
+            if codes is None:
+                codes = keep.tile([P, count], U32, name=name + "_codes", align_bytes=64)
+            scales = keep.tile([P, count], U8, name=name + "_sc", align_bytes=64)
+            nc.vector.quantize_mx(out=codes[:].bitcast(FP8X4), scales=scales[:], in_=grouped)
+            return codes, scales
 
         x_grouped = [keep.tile([P, HALF, PACK], BF16, name="x_grouped%d" % a, align_bytes=64) for a in range(2)]
-        x_codes = [keep.tile([P, HALF], U32, name="x_codes%d" % a, align_bytes=64) for a in range(2)]
+        x_codes = {}
         x_sc = [keep.tile([P, HALF], U8, name="x_sc%d" % a, align_bytes=64) for a in range(2)]
 
         def half_cols(a):
@@ -104,17 +108,23 @@ def tile_picked_devox_none_e_kernel(tc, xT, w1, w2_words, w2_scales, gate, emb, 
         def gather_x(j, a):
             nc.vector.tensor_copy(x_grouped[a][:, :, j], x_planes[j][:].indirect(offs_sb[:, half_cols(a)]))
 
-        def quantise_x(a):
+        def quantise_x(a, tag):
+            x_codes[a] = keep.tile([P, HALF], U32, name="x_codes%d" % a, tag=tag, align_bytes=64)
             nc.vector.quantize_mx(out=x_codes[a][:].bitcast(FP8X4), scales=x_sc[a][:], in_=x_grouped[a][:].rearrange("p c j -> p (c j)"))
 
         h = [keep.tile([P, S], F32, name="h%d" % t) for t in range(PACK)]
 
-        def layer1(t, first, count, number):
+        w1_mx = {}
+
+        def product(t, first, count, number):
             acc = bank(number, count)
-            cols = slice(t * P, (t + 1) * P)
+            w1_codes, w1_sc, cols = w1_mx[t]
             a, points = first // HALF, slice(first % HALF, first % HALF + count)
             nc.tensor.matmul_mx(out=acc[:], lhsT=w1_codes[:, cols].bitcast(FP8X4), lhsT_scale=w1_sc[:, cols], rhs=x_codes[a][:, points].bitcast(FP8X4), rhs_scale=x_sc[a][:, points], start=True, stop=True)
-            nc.scalar.activation(h[t][:, first : first + count], acc[:], RELU)
+            return acc
+
+        def layer1(t, first, count, number):
+            nc.scalar.activation(h[t][:, first : first + count], product(t, first, count, number)[:], RELU)
 
         def scatter_part(t, first, count):
             nc.vector.tensor_copy(up[t][:].indirect(cell_sb[:, first // LIST_COLS : (first + count) // LIST_COLS]), h[t][:, first : first + count])
@@ -127,7 +137,7 @@ def tile_picked_devox_none_e_kernel(tc, xT, w1, w2_words, w2_scales, gate, emb, 
 
         pairs_turned = [keep.tile([P, BLOCKS, 2 * P], BF16, name="pairs_turned%d" % g) for g in range(U // BANK)]
         pieces = [(0, CHUNK), (2 * CHUNK, CHUNK), (3 * CHUNK, CHUNK), (CHUNK, CHUNK // 2), (CHUNK + CHUNK // 2, CHUNK // 2)]
-        z_planes = {first: keep.tile([P, 2, count], BF16, name="z_planes%d" % first) for first, count in pieces}
+        z_planes = keep.tile([P, 2, U], BF16, name="z_planes")
         z_grouped = {first: keep.tile([P, count, PACK], BF16, name="z_grouped%d" % first, align_bytes=64) for first, count in pieces}
 
         def add_turned(t):
@@ -138,10 +148,10 @@ def tile_picked_devox_none_e_kernel(tc, xT, w1, w2_words, w2_scales, gate, emb, 
                 turn(sums[g], up[t][:, g * BANK : (g + 1) * BANK], False, True)
                 nc.scalar.copy(pairs_turned[g][:, :, t * P : (t + 1) * P], sums[g][:].rearrange("r (k m) -> r k m", m=P))
 
-        def add_plain(engine, t):
-            for first, count in sorted(pieces):
-                cols = slice(first, first + count)
-                engine.tensor_tensor(z_planes[first][:, t - THIRD, :], up[t][:, cols], emb_sb[t][:, cols], ADD)
+        def add_plain(engine, t, width):
+            for first in range(0, U, width):
+                cols = slice(first, first + width)
+                engine.tensor_tensor(z_planes[:, t - THIRD, cols], up[t][:, cols], emb_sb[t][:, cols], ADD)
 
         def scatter(t):
             nc.vector.tensor_copy(up[t][:].indirect(cell_sb[:]), h[t][:])
@@ -149,22 +159,32 @@ def tile_picked_devox_none_e_kernel(tc, xT, w1, w2_words, w2_scales, gate, emb, 
         for j in range(PACK):
             for a in range(2):
                 gather_x(j, a)
-        deal_w1(0)
-        quantise_x(0)
-        quantise_w1(0, LOW, 1)
+        low_grouped = keep.tile([P, P * PACK], BF16, name="low_grouped", tag="low_grouped", align_bytes=64)
+        for u in range(2):
+            deal(low_grouped[:].rearrange("p (q e j) -> p q e j", e=2, j=PACK)[:, :, :, 2 * u : 2 * u + 2], w1_first[u], slice(0, 2))
+        quantise_x(0, "x_codes0")
+        w1_mx[LOW] = quantise("low", low_grouped[:], staged("low_codes", [P, P], U32)) + (slice(0, P),)
         layer1(LOW, 0, HALF // 2, 0)
         layer1(LOW, HALF // 2, HALF // 2, 1)
-        quantise_x(1)
-        layer1(LOW, HALF, HALF, 2)
-        deal_w1(1)
+        quantise_x(1, "low_grouped")
+        low_acc = product(LOW, HALF, HALF, 2)
+        high_grouped = staged("high_grouped", [P, P * PACK], BF16)
+        deal(high_grouped[:].rearrange("p (q e j) -> p q e j", e=2, j=PACK), w1_second, slice(0, 2))
+        nc.scalar.activation(h[LOW][:, HALF:], low_acc[:], RELU)
         scatter_part(LOW, 0, HALF // 2)
-        scatter_part(LOW, HALF // 2, HALF // 2)
-        quantise_w1(1, HIGH, 1)
-        quantise_w1(2, THIRD, 2)
+        w1_mx[HIGH] = quantise("high", high_grouped[:]) + (slice(0, P),)
+        planes_grouped = staged("planes_grouped", [P, 2 * P * PACK], BF16)
+        dealt = planes_grouped[:].rearrange("p (e a q j) -> p a q e j", e=2, a=2, j=PACK)
+        for u in range(2):
+            deal(dealt[:, 0, :, :, 2 * u : 2 * u + 2], w1_first[u], slice(2, 4))
+        deal(dealt[:, 1], w1_second, slice(2, 4))
+        planes_mx = quantise("planes", planes_grouped[:])
+        w1_mx[THIRD] = planes_mx + (slice(0, P),)
+        w1_mx[FOURTH] = planes_mx + (slice(P, 2 * P),)
         for t in (HIGH, THIRD, FOURTH):
             for a in range(2):
                 layer1(t, a * HALF, HALF, (2 * t + a + 1) % 4)
-        scatter_part(LOW, HALF, HALF)
+        scatter_part(LOW, HALF // 2, S - HALF // 2)
         add_turned(LOW)
         scatter(HIGH)
         add_turned(HIGH)
@@ -176,14 +196,14 @@ def tile_picked_devox_none_e_kernel(tc, xT, w1, w2_words, w2_scales, gate, emb, 
                 if first // BANK == g:
                     nc.scalar.copy(z_grouped[first][:, :, 0:2], halves[:, first % BANK : first % BANK + count, :])
         scatter(THIRD)
-        add_plain(nc.gpsimd, THIRD)
+        add_plain(nc.gpsimd, THIRD, U)
         scatter(FOURTH)
-        add_plain(nc.vector, FOURTH)
+        add_plain(nc.vector, FOURTH, CHUNK)
 
         y = [keep.tile([P, U], F32, name="y%d" % b) for b in range(N // P)]
         for first, count in sorted(pieces):
             place = nc.scalar.copy if first < U // 2 else nc.vector.tensor_copy
-            place(z_grouped[first][:, :, 2:4], z_planes[first][:].rearrange("p t r -> p r t"))
+            place(z_grouped[first][:, :, 2:4], z_planes[:, :, first : first + count].rearrange("p t r -> p r t"))
 
         z_codes = {}
         z_sc = {}
@@ -224,13 +244,19 @@ def tile_picked_devox_none_e_kernel(tc, xT, w1, w2_words, w2_scales, gate, emb, 
         nc.sync.dma_start(out[0:P, :], result0[:])
 
         terms = [weighted(1, d, 0, V) for d in range(D - 1)]
-        parts = [(0, 3 * V // 4), (3 * V // 4, V // 4)]
-        last = [weighted(1, D - 1, *parts[0])]
+        parts = [(0, V // 2), (V // 2, V // 4), (3 * V // 4, V // 4)]
         pair = keep.tile([P, V], F32, name="pair")
-        nc.vector.tensor_tensor(pair[:], terms[0][:], terms[1][:], ADD)
-        last.append(weighted(1, D - 1, *parts[1]))
-        for a, (first, count) in enumerate(parts):
+
+        def finish(a, last):
+            first, count = parts[a]
             cols = slice(first, first + count)
             result1 = keep.tile([P, count], F32, name="result1_%d" % a)
-            nc.vector.tensor_tensor(result1[:], pair[:, cols], last[a][:], ADD)
+            nc.vector.tensor_tensor(result1[:], pair[:, cols], last[:], ADD)
             nc.sync.dma_start(out[P : 2 * P, cols], result1[:])
+
+        last = [weighted(1, D - 1, *parts[0])]
+        nc.vector.tensor_tensor(pair[:], terms[0][:], terms[1][:], ADD)
+        for a in range(1, len(parts)):
+            last.append(weighted(1, D - 1, *parts[a]))
+            finish(a - 1, last[a - 1])
+        finish(len(parts) - 1, last[-1])

@@ -21,7 +21,7 @@ P = 128
 PACK = 4
 HALF = S // 2
 LIST_COLS = 16
-CHUNK = 256
+SPLIT = 640
 BANK = 512
 BLOCKS = BANK // P
 LOW, HIGH, THIRD, FOURTH = range(4)
@@ -57,7 +57,7 @@ def tile_picked_devox_none_e_kernel(tc, xT, w1, w2_words, w2_scales, gate, emb, 
         cell_sb = list_tile("cell_sb", cell)
         nc.sync.dma_start(w1_second[:], w1_rows[:, :, H // 2 :])
 
-        emb_sb = [keep.tile([P, U], F32, name="emb_sb%d" % t) for t in range(PACK)]
+        emb_sb = [keep.tile([P, U], F32, name="emb_sb%d" % t, tag="emb_sb%d" % t, align_bytes=64) for t in range(PACK)]
         emb_quads = emb.rearrange("(a q t) r -> a q t r", a=2, t=PACK)
         emb_rows = emb.rearrange("(p t) r -> t p r", t=PACK)
         nc.sync.dma_start(emb_sb[LOW][:], emb_quads[0, :, 0:2, :])
@@ -136,8 +136,13 @@ def tile_picked_devox_none_e_kernel(tc, xT, w1, w2_words, w2_scales, gate, emb, 
                 nc.tensor.matmul(dst[:, cols], src[:, cols], ident[:], start=first and k == 0, stop=last and k == blocks - 1, is_transpose=True)
 
         pairs_turned = [keep.tile([P, BLOCKS, 2 * P], BF16, name="pairs_turned%d" % g) for g in range(U // BANK)]
-        pieces = [(0, CHUNK), (2 * CHUNK, CHUNK), (3 * CHUNK, CHUNK), (CHUNK, CHUNK // 2), (CHUNK + CHUNK // 2, CHUNK // 2)]
-        z_planes = keep.tile([P, 2, U], BF16, name="z_planes")
+        pieces = [(0, 256), (640, 128), (768, 256), (256, 256), (512, 128)]
+        z_planes = {0: keep.tile([P, 2, SPLIT], BF16, name="z_planes0"), SPLIT: keep.tile([P, 2, U - SPLIT], BF16, name="z_planes1", tag="z_planes1", align_bytes=64)}
+
+        def planes(first, count):
+            start = 0 if first < SPLIT else SPLIT
+            return z_planes[start][:, :, first - start : first - start + count]
+
         z_grouped = {first: keep.tile([P, count, PACK], BF16, name="z_grouped%d" % first, align_bytes=64) for first, count in pieces}
 
         def add_turned(t):
@@ -148,10 +153,10 @@ def tile_picked_devox_none_e_kernel(tc, xT, w1, w2_words, w2_scales, gate, emb, 
                 turn(sums[g], up[t][:, g * BANK : (g + 1) * BANK], False, True)
                 nc.scalar.copy(pairs_turned[g][:, :, t * P : (t + 1) * P], sums[g][:].rearrange("r (k m) -> r k m", m=P))
 
-        def add_plain(engine, t, width):
-            for first in range(0, U, width):
-                cols = slice(first, first + width)
-                engine.tensor_tensor(z_planes[:, t - THIRD, cols], up[t][:, cols], emb_sb[t][:, cols], ADD)
+        def add_plain(engine, t, borders):
+            for first, end in zip(borders, borders[1:]):
+                cols = slice(first, end)
+                engine.tensor_tensor(planes(first, end - first)[:, t - THIRD, :], up[t][:, cols], emb_sb[t][:, cols], ADD)
 
         def scatter(t):
             nc.vector.tensor_copy(up[t][:].indirect(cell_sb[:]), h[t][:])
@@ -196,14 +201,14 @@ def tile_picked_devox_none_e_kernel(tc, xT, w1, w2_words, w2_scales, gate, emb, 
                 if first // BANK == g:
                     nc.scalar.copy(z_grouped[first][:, :, 0:2], halves[:, first % BANK : first % BANK + count, :])
         scatter(THIRD)
-        add_plain(nc.gpsimd, THIRD, U)
+        add_plain(nc.gpsimd, THIRD, [0, SPLIT, U])
         scatter(FOURTH)
-        add_plain(nc.vector, FOURTH, CHUNK)
+        add_plain(nc.vector, FOURTH, [0, 256, SPLIT, 768, U])
 
         y = [keep.tile([P, U], F32, name="y%d" % b) for b in range(N // P)]
         for first, count in sorted(pieces):
-            place = nc.scalar.copy if first < U // 2 else nc.vector.tensor_copy
-            place(z_grouped[first][:, :, 2:4], z_planes[:, :, first : first + count].rearrange("p t r -> p r t"))
+            place = nc.scalar.copy if first < SPLIT else nc.vector.tensor_copy
+            place(z_grouped[first][:, :, 2:4], planes(first, count).rearrange("p t r -> p r t"))
 
         z_codes = {}
         z_sc = {}
@@ -212,16 +217,22 @@ def tile_picked_devox_none_e_kernel(tc, xT, w1, w2_words, w2_scales, gate, emb, 
             cols = slice(b * P, (b + 1) * P)
             nc.tensor.matmul_mx(out=dst, lhsT=w2_codes[:, cols].bitcast(FP8X4), lhsT_scale=w2_sc[:, cols], rhs=z_codes[first][:].bitcast(FP8X4), rhs_scale=z_sc[first][:], start=True, stop=True)
 
-        for n, (first, count) in enumerate(pieces):
+        late_codes = keep.tile([P, 384], U32, name="late_codes", tag="z_planes1", align_bytes=64)
+        z_codes[0] = keep.tile([P, 256], U32, name="z_codes0", tag="emb_sb%d" % FOURTH, align_bytes=64)
+        for first, count in pieces[1:3]:
             z_codes[first] = keep.tile([P, count], U32, name="z_codes%d" % first, align_bytes=64)
+        for first, count in pieces[3:]:
+            z_codes[first] = late_codes[:, first - 256 : first - 256 + count]
+        for first, count in pieces:
             z_sc[first] = keep.tile([P, count], U8, name="z_sc%d" % first, align_bytes=64)
             nc.vector.quantize_mx(out=z_codes[first][:].bitcast(FP8X4), scales=z_sc[first][:], in_=z_grouped[first][:].rearrange("p c t -> p (c t)"))
+        for n, (first, count) in enumerate(pieces):
             acc = bank(n, count)
             layer2(acc[:], 0, first)
-            unload = nc.vector.tensor_copy if n == len(pieces) - 1 else nc.scalar.copy
+            unload = nc.vector.tensor_copy if n == len(pieces) - 2 else nc.scalar.copy
             unload(y[0][:, first : first + count], acc[:])
         for g in range(U // BANK):
-            acc = bank(len(pieces) - 2 + g)
+            acc = bank(len(pieces) - 1)
             for first, count in sorted(pieces):
                 if first // BANK == g:
                     layer2(acc[:, first % BANK : first % BANK + count], 1, first)
@@ -241,7 +252,7 @@ def tile_picked_devox_none_e_kernel(tc, xT, w1, w2_words, w2_scales, gate, emb, 
         turn(sum_back, sum_sb, True, True)
         result0 = keep.tile([P, V], F32, name="result0")
         nc.scalar.copy(result0[:], sum_back[:])
-        nc.sync.dma_start(out[0:P, :], result0[:])
+        nc.scalar.dma_start(out[0:P, :], result0[:])
 
         terms = [weighted(1, d, 0, V) for d in range(D - 1)]
         parts = [(0, V // 2), (V // 2, V // 4), (3 * V // 4, V // 4)]

@@ -68,8 +68,9 @@ def tile_picked_devox_none_e_kernel(tc, xT, w1, w2_words, w2_scales, gate, emb, 
         nc.vector.memset(w2_sc[:].bitcast(I32), 0)
         for q in range(4):
             nc.sync.dma_start(w2_sc[32 * q : 32 * q + 4, :].bitcast(I32), w2_scales[0, 4 * q : 4 * q + 4, :].bitcast(I32))
-        gate_sb = keep.tile([P, D, V], F32, name="gate_sb")
-        nc.sync.dma_start(gate_sb[:], gate.rearrange("d p v -> p d v"))
+        gate_sb = [keep.tile([P, V], F32, name="gate_sb%d" % d, tag="gate_sb%d" % d) for d in range(D)]
+        for d in range(D):
+            nc.sync.dma_start(gate_sb[d][:], gate[d])
         pos_sb = [list_tile("pos%d_sb" % d, src) for d, src in enumerate((pos1, pos2, pos3))]
         nc.sync.dma_start(emb_sb[THIRD][:], emb_rows[2])
         nc.sync.dma_start(emb_sb[FOURTH][:], emb_rows[3])
@@ -80,12 +81,14 @@ def tile_picked_devox_none_e_kernel(tc, xT, w1, w2_words, w2_scales, gate, emb, 
         up = []
         for t in range(PACK):
             tile = keep.tile([P, U], F32, name="up%d" % t)
-            nc.vector.memset(tile[:], 0.0)
+            (nc.vector if t < THIRD else nc.gpsimd).memset(tile[:], 0.0)
             up.append(tile)
+        up_first = keep.tile([P, U], F32, name="up_first")
+        nc.vector.memset(up_first[:], 0.0)
 
-        def deal(dst, raw, slots):
+        def deal(dst, raw, slots, copy=nc.scalar.copy):
             quads = raw[:].rearrange("p j (q t) -> p q t j", t=PACK)
-            nc.scalar.copy(dst, quads[:, :, slots, :])
+            copy(dst, quads[:, :, slots, :])
 
         def staged(name, shape, dtype):
             return keep.tile(shape, dtype, name=name, tag="w1_stage", align_bytes=64)
@@ -143,18 +146,22 @@ def tile_picked_devox_none_e_kernel(tc, xT, w1, w2_words, w2_scales, gate, emb, 
             start = 0 if first < SPLIT else SPLIT
             return z_planes[start][:, :, first - start : first - start + count]
 
-        z_grouped = {first: keep.tile([P, count, PACK], BF16, name="z_grouped%d" % first, align_bytes=64) for first, count in pieces}
+        placings = [(0, 256), (256, 256), (512, 128), (SPLIT, U - SPLIT)]
+        placed = {first: keep.tile([P, count, PACK], BF16, name="placed%d" % first, align_bytes=64) for first, count in placings}
+        z_grouped = {first: placed[min(first, SPLIT)][:, first - min(first, SPLIT) : first - min(first, SPLIT) + count, :] for first, count in pieces}
 
-        def add_turned(t):
+        def add_turned(t, *more):
             sums = [bank(4 + 2 * t + g) for g in range(U // BANK)]
             for g in range(U // BANK):
                 turn(sums[g], emb_sb[t][:, g * BANK : (g + 1) * BANK], True, False)
+                for window in more:
+                    turn(sums[g], window[:, g * BANK : (g + 1) * BANK], False, False)
             for g in range(U // BANK):
                 turn(sums[g], up[t][:, g * BANK : (g + 1) * BANK], False, True)
                 nc.scalar.copy(pairs_turned[g][:, :, t * P : (t + 1) * P], sums[g][:].rearrange("r (k m) -> r k m", m=P))
 
-        def add_plain(engine, t, borders):
-            for first, end in zip(borders, borders[1:]):
+        def add_plain(engine, t, spans):
+            for first, end in spans:
                 cols = slice(first, end)
                 engine.tensor_tensor(planes(first, end - first)[:, t - THIRD, :], up[t][:, cols], emb_sb[t][:, cols], ADD)
 
@@ -172,11 +179,10 @@ def tile_picked_devox_none_e_kernel(tc, xT, w1, w2_words, w2_scales, gate, emb, 
         layer1(LOW, 0, HALF // 2, 0)
         layer1(LOW, HALF // 2, HALF // 2, 1)
         quantise_x(1, "low_grouped")
-        low_acc = product(LOW, HALF, HALF, 2)
-        high_grouped = staged("high_grouped", [P, P * PACK], BF16)
-        deal(high_grouped[:].rearrange("p (q e j) -> p q e j", e=2, j=PACK), w1_second, slice(0, 2))
-        nc.scalar.activation(h[LOW][:, HALF:], low_acc[:], RELU)
-        scatter_part(LOW, 0, HALF // 2)
+        layer1(LOW, HALF, HALF, 2)
+        high_grouped = keep.tile([P, P * PACK], BF16, name="high_grouped", align_bytes=64)
+        deal(high_grouped[:].rearrange("p (q e j) -> p q e j", e=2, j=PACK), w1_second, slice(0, 2), nc.gpsimd.tensor_copy)
+        nc.vector.tensor_copy(up_first[:].indirect(cell_sb[:, : HALF // 2 // LIST_COLS]), h[LOW][:, : HALF // 2])
         w1_mx[HIGH] = quantise("high", high_grouped[:]) + (slice(0, P),)
         planes_grouped = staged("planes_grouped", [P, 2 * P * PACK], BF16)
         dealt = planes_grouped[:].rearrange("p (e a q j) -> p a q e j", e=2, a=2, j=PACK)
@@ -190,25 +196,25 @@ def tile_picked_devox_none_e_kernel(tc, xT, w1, w2_words, w2_scales, gate, emb, 
             for a in range(2):
                 layer1(t, a * HALF, HALF, (2 * t + a + 1) % 4)
         scatter_part(LOW, HALF // 2, S - HALF // 2)
-        add_turned(LOW)
+        add_turned(LOW, up_first)
         scatter(HIGH)
         add_turned(HIGH)
         for g in range(U // BANK):
             acc = bank(g)
             turn(acc, pairs_turned[g][:].rearrange("r k c -> r (k c)").bitcast(F32), True, True)
             halves = acc[:].bitcast(BF16).rearrange("p (r e) -> p r e", e=2)
-            for first, count in sorted(pieces):
+            for first, count in placings:
                 if first // BANK == g:
-                    nc.scalar.copy(z_grouped[first][:, :, 0:2], halves[:, first % BANK : first % BANK + count, :])
+                    nc.scalar.copy(placed[first][:, :, 0:2], halves[:, first % BANK : first % BANK + count, :])
         scatter(THIRD)
-        add_plain(nc.gpsimd, THIRD, [0, SPLIT, U])
+        add_plain(nc.gpsimd, THIRD, [(0, SPLIT), (SPLIT, U)])
         scatter(FOURTH)
-        add_plain(nc.vector, FOURTH, [0, 256, SPLIT, 768, U])
+        add_plain(nc.vector, FOURTH, [(0, 256), (SPLIT, U), (256, SPLIT)])
 
         y = [keep.tile([P, U], F32, name="y%d" % b) for b in range(N // P)]
-        for first, count in sorted(pieces):
+        for first, count in placings:
             place = nc.scalar.copy if first < SPLIT else nc.vector.tensor_copy
-            place(z_grouped[first][:, :, 2:4], planes(first, count).rearrange("p t r -> p r t"))
+            place(placed[first][:, :, 2:4], planes(first, count).rearrange("p t r -> p r t"))
 
         z_codes = {}
         z_sc = {}
@@ -225,27 +231,28 @@ def tile_picked_devox_none_e_kernel(tc, xT, w1, w2_words, w2_scales, gate, emb, 
             z_codes[first] = late_codes[:, first - 256 : first - 256 + count]
         for first, count in pieces:
             z_sc[first] = keep.tile([P, count], U8, name="z_sc%d" % first, align_bytes=64)
-            nc.vector.quantize_mx(out=z_codes[first][:].bitcast(FP8X4), scales=z_sc[first][:], in_=z_grouped[first][:].rearrange("p c t -> p (c t)"))
+            nc.vector.quantize_mx(out=z_codes[first][:].bitcast(FP8X4), scales=z_sc[first][:], in_=z_grouped[first].rearrange("p c t -> p (c t)"))
         for n, (first, count) in enumerate(pieces):
             acc = bank(n, count)
             layer2(acc[:], 0, first)
             unload = nc.vector.tensor_copy if n == len(pieces) - 2 else nc.scalar.copy
             unload(y[0][:, first : first + count], acc[:])
         for g in range(U // BANK):
-            acc = bank(len(pieces) - 1)
+            acc = bank(len(pieces) - 1 - g)
             for first, count in sorted(pieces):
                 if first // BANK == g:
                     layer2(acc[:, first % BANK : first % BANK + count], 1, first)
             nc.scalar.copy(y[1][:, g * BANK : (g + 1) * BANK], acc[:])
 
-        def weighted(b, d, first, count):
-            term = keep.tile([P, count], F32, name="term%d_%d_%d" % (b, d, first))
-            nc.vector.tensor_tensor(term[:], y[b][:].indirect(pos_sb[d][:, first // LIST_COLS : (first + count) // LIST_COLS]), gate_sb[:, d, first : first + count], MULT)
-            return term
+        def weighted(term, b, d, first):
+            count = term.shape[1]
+            nc.vector.tensor_tensor(term, y[b][:].indirect(pos_sb[d][:, first // LIST_COLS : (first + count) // LIST_COLS]), gate_sb[d][:, first : first + count], MULT)
 
         sum_turned = bank(5)
         for d in range(D):
-            turn(sum_turned, weighted(0, d, 0, V), d == 0, d == D - 1)
+            term = keep.tile([P, V], F32, name="term0_%d" % d)
+            weighted(term[:], 0, d, 0)
+            turn(sum_turned, term, d == 0, d == D - 1)
         sum_sb = keep.tile([P, V], F32, name="sum_sb")
         nc.scalar.copy(sum_sb[:], sum_turned[:])
         sum_back = bank(6)
@@ -254,20 +261,19 @@ def tile_picked_devox_none_e_kernel(tc, xT, w1, w2_words, w2_scales, gate, emb, 
         nc.scalar.copy(result0[:], sum_back[:])
         nc.scalar.dma_start(out[0:P, :], result0[:])
 
-        terms = [weighted(1, d, 0, V) for d in range(D - 1)]
-        parts = [(0, V // 2), (V // 2, V // 4), (3 * V // 4, V // 4)]
+        terms = [keep.tile([P, V], F32, name="term1_%d" % d) for d in range(D - 1)]
+        for d in range(D - 1):
+            weighted(terms[d][:], 1, d, 0)
+        last_early = keep.tile([P, V // 2], F32, name="last_early")
+        weighted(last_early[:], 1, D - 1, 0)
         pair = keep.tile([P, V], F32, name="pair")
-
-        def finish(a, last):
-            first, count = parts[a]
-            cols = slice(first, first + count)
-            result1 = keep.tile([P, count], F32, name="result1_%d" % a)
-            nc.vector.tensor_tensor(result1[:], pair[:, cols], last[:], ADD)
-            nc.sync.dma_start(out[P : 2 * P, cols], result1[:])
-
-        last = [weighted(1, D - 1, *parts[0])]
         nc.vector.tensor_tensor(pair[:], terms[0][:], terms[1][:], ADD)
-        for a in range(1, len(parts)):
-            last.append(weighted(1, D - 1, *parts[a]))
-            finish(a - 1, last[a - 1])
-        finish(len(parts) - 1, last[-1])
+        last_late = keep.tile([P, V // 2], F32, name="last_late", tag="gate_sb1")
+        parts = [(0, last_early[:]), (V // 2, last_late[:, : V // 4]), (3 * V // 4, last_late[:, V // 4 :])]
+        for first, last in parts[1:]:
+            weighted(last, 1, D - 1, first)
+        for first, last in parts:
+            cols = slice(first, first + last.shape[1])
+            result1 = keep.tile([P, last.shape[1]], F32, name="result1_%d" % first)
+            nc.vector.tensor_tensor(result1[:], pair[:, cols], last, ADD)
+            nc.sync.dma_start(out[P : 2 * P, cols], result1[:])

@@ -54,8 +54,8 @@ def tile_picked_devox_none_e_kernel(tc, xT, w1, w2_words, w2_scales, gate, emb, 
                 offs_sb = list_tile("offs_sb", offs)
         for u in range(2):
             nc.sync.dma_start(w1_first[u][:], w1_rows[:, 2 * u : 2 * u + 2, : H // 2])
-        cell_sb = list_tile("cell_sb", cell)
         nc.sync.dma_start(w1_second[:], w1_rows[:, :, H // 2 :])
+        cell_sb = list_tile("cell_sb", cell)
 
         emb_sb = [keep.tile([P, U], F32, name="emb_sb%d" % t, tag="emb_sb%d" % t, align_bytes=64) for t in range(PACK)]
         emb_quads = emb.rearrange("(a q t) r -> a q t r", a=2, t=PACK)
@@ -86,18 +86,14 @@ def tile_picked_devox_none_e_kernel(tc, xT, w1, w2_words, w2_scales, gate, emb, 
         up_first = keep.tile([P, U], F32, name="up_first")
         nc.vector.memset(up_first[:], 0.0)
 
-        def deal(dst, raw, slots, copy=nc.scalar.copy):
+        def deal(dst, raw, slots):
             quads = raw[:].rearrange("p j (q t) -> p q t j", t=PACK)
-            copy(dst, quads[:, :, slots, :])
+            nc.scalar.copy(dst, quads[:, :, slots, :])
 
-        def staged(name, shape, dtype):
-            return keep.tile(shape, dtype, name=name, tag="w1_stage", align_bytes=64)
-
-        def quantise(name, grouped, codes=None):
+        def quantise(name, grouped):
             count = grouped.shape[1] // PACK
-            if codes is None:
-                codes = keep.tile([P, count], U32, name=name + "_codes", align_bytes=64)
-            scales = keep.tile([P, count], U8, name=name + "_sc", align_bytes=64)
+            codes = keep.tile([P, count], U32, name=name + "_codes", tag=name + "_codes", align_bytes=64)
+            scales = keep.tile([P, count], U8, name=name + "_sc", tag=name + "_sc", align_bytes=64)
             nc.vector.quantize_mx(out=codes[:].bitcast(FP8X4), scales=scales[:], in_=grouped)
             return codes, scales
 
@@ -175,16 +171,18 @@ def tile_picked_devox_none_e_kernel(tc, xT, w1, w2_words, w2_scales, gate, emb, 
         for u in range(2):
             deal(low_grouped[:].rearrange("p (q e j) -> p q e j", e=2, j=PACK)[:, :, :, 2 * u : 2 * u + 2], w1_first[u], slice(0, 2))
         quantise_x(0, "x_codes0")
-        w1_mx[LOW] = quantise("low", low_grouped[:], staged("low_codes", [P, P], U32)) + (slice(0, P),)
+        w1_mx[LOW] = quantise("low", low_grouped[:]) + (slice(0, P),)
         layer1(LOW, 0, HALF // 2, 0)
         layer1(LOW, HALF // 2, HALF // 2, 1)
         quantise_x(1, "low_grouped")
-        layer1(LOW, HALF, HALF, 2)
-        high_grouped = keep.tile([P, P * PACK], BF16, name="high_grouped", align_bytes=64)
-        deal(high_grouped[:].rearrange("p (q e j) -> p q e j", e=2, j=PACK), w1_second, slice(0, 2), nc.gpsimd.tensor_copy)
-        nc.vector.tensor_copy(up_first[:].indirect(cell_sb[:, : HALF // 2 // LIST_COLS]), h[LOW][:, : HALF // 2])
+        low_acc = product(LOW, HALF, HALF, 2)
+        high_grouped = keep.tile([P, P * PACK], BF16, name="high_grouped", tag="low_codes", align_bytes=64)
+        deal(high_grouped[:].rearrange("p (q e j) -> p q e j", e=2, j=PACK), w1_second, slice(0, 2))
+        nc.scalar.activation(h[LOW][:, HALF:], low_acc[:], RELU)
+        scatter_part(LOW, 0, HALF // 2)
+        nc.vector.tensor_copy(up_first[:].indirect(cell_sb[:, HALF // 2 // LIST_COLS : HALF // LIST_COLS]), h[LOW][:, HALF // 2 : HALF])
         w1_mx[HIGH] = quantise("high", high_grouped[:]) + (slice(0, P),)
-        planes_grouped = staged("planes_grouped", [P, 2 * P * PACK], BF16)
+        planes_grouped = keep.tile([P, 2 * P * PACK], BF16, name="planes_grouped", tag="low_sc", align_bytes=64)
         dealt = planes_grouped[:].rearrange("p (e a q j) -> p a q e j", e=2, a=2, j=PACK)
         for u in range(2):
             deal(dealt[:, 0, :, :, 2 * u : 2 * u + 2], w1_first[u], slice(2, 4))
@@ -195,7 +193,7 @@ def tile_picked_devox_none_e_kernel(tc, xT, w1, w2_words, w2_scales, gate, emb, 
         for t in (HIGH, THIRD, FOURTH):
             for a in range(2):
                 layer1(t, a * HALF, HALF, (2 * t + a + 1) % 4)
-        scatter_part(LOW, HALF // 2, S - HALF // 2)
+        scatter_part(LOW, HALF, HALF)
         add_turned(LOW, up_first)
         scatter(HIGH)
         add_turned(HIGH)

@@ -22,8 +22,9 @@ PACK = 4
 HALF = S // 2
 LIST_COLS = 16
 SPLIT = 640
+FIRST = 64
 BANK = 512
-BLOCKS = BANK // P
+CHUNK = 256
 LOW, HIGH, THIRD, FOURTH = range(4)
 
 
@@ -83,6 +84,8 @@ def tile_picked_devox_none_e_kernel(tc, xT, w1, w2_words, w2_scales, gate, emb, 
             tile = keep.tile([P, U], F32, name="up%d" % t)
             (nc.vector if t < THIRD else nc.gpsimd).memset(tile[:], 0.0)
             up.append(tile)
+        zeros = keep.tile([P, FIRST], F32, name="zeros")
+        nc.vector.memset(zeros[:], 0.0)
         up_first = keep.tile([P, U], F32, name="up_first")
         nc.vector.memset(up_first[:], 0.0)
 
@@ -134,7 +137,7 @@ def tile_picked_devox_none_e_kernel(tc, xT, w1, w2_words, w2_scales, gate, emb, 
                 cols = slice(k * P, (k + 1) * P)
                 nc.tensor.matmul(dst[:, cols], src[:, cols], ident[:], start=first and k == 0, stop=last and k == blocks - 1, is_transpose=True)
 
-        pairs_turned = [keep.tile([P, BLOCKS, 2 * P], BF16, name="pairs_turned%d" % g) for g in range(U // BANK)]
+        pairs_turned = [keep.tile([P, CHUNK // P, 2 * P], BF16, name="pairs_turned%d" % c) for c in range(U // CHUNK)]
         pieces = [(0, 256), (640, 128), (768, 256), (256, 256), (512, 128)]
         z_planes = {0: keep.tile([P, 2, SPLIT], BF16, name="z_planes0"), SPLIT: keep.tile([P, 2, U - SPLIT], BF16, name="z_planes1", tag="z_planes1", align_bytes=64)}
 
@@ -146,15 +149,16 @@ def tile_picked_devox_none_e_kernel(tc, xT, w1, w2_words, w2_scales, gate, emb, 
         placed = {first: keep.tile([P, count, PACK], BF16, name="placed%d" % first, align_bytes=64) for first, count in placings}
         z_grouped = {first: placed[min(first, SPLIT)][:, first - min(first, SPLIT) : first - min(first, SPLIT) + count, :] for first, count in pieces}
 
-        def add_turned(t, *more):
-            sums = [bank(4 + 2 * t + g) for g in range(U // BANK)]
-            for g in range(U // BANK):
-                turn(sums[g], emb_sb[t][:, g * BANK : (g + 1) * BANK], True, False)
-                for window in more:
-                    turn(sums[g], window[:, g * BANK : (g + 1) * BANK], False, False)
-            for g in range(U // BANK):
-                turn(sums[g], up[t][:, g * BANK : (g + 1) * BANK], False, True)
-                nc.scalar.copy(pairs_turned[g][:, :, t * P : (t + 1) * P], sums[g][:].rearrange("r (k m) -> r k m", m=P))
+        def add_turned(t, numbers, *more):
+            width = U // len(numbers)
+            sums = [bank(number, width) for number in numbers]
+            for g, acc in enumerate(sums):
+                for n, window in enumerate((emb_sb[t],) + more):
+                    turn(acc, window[:, g * width : (g + 1) * width], n == 0, False)
+            for g, acc in enumerate(sums):
+                turn(acc, up[t][:, g * width : (g + 1) * width], False, True)
+                for e in range(width // CHUNK):
+                    nc.scalar.copy(pairs_turned[g * width // CHUNK + e][:, :, t * P : (t + 1) * P], acc[:, e * CHUNK : (e + 1) * CHUNK].rearrange("r (k m) -> r k m", m=P))
 
         def add_plain(engine, t, spans):
             for first, end in spans:
@@ -172,15 +176,16 @@ def tile_picked_devox_none_e_kernel(tc, xT, w1, w2_words, w2_scales, gate, emb, 
             deal(low_grouped[:].rearrange("p (q e j) -> p q e j", e=2, j=PACK)[:, :, :, 2 * u : 2 * u + 2], w1_first[u], slice(0, 2))
         quantise_x(0, "x_codes0")
         w1_mx[LOW] = quantise("low", low_grouped[:]) + (slice(0, P),)
-        layer1(LOW, 0, HALF // 2, 0)
+        layer1(LOW, 0, FIRST, 0)
+        layer1(LOW, FIRST, FIRST, 3)
         layer1(LOW, HALF // 2, HALF // 2, 1)
         quantise_x(1, "low_grouped")
         low_acc = product(LOW, HALF, HALF, 2)
         high_grouped = keep.tile([P, P * PACK], BF16, name="high_grouped", tag="low_codes", align_bytes=64)
         deal(high_grouped[:].rearrange("p (q e j) -> p q e j", e=2, j=PACK), w1_second, slice(0, 2))
         nc.scalar.activation(h[LOW][:, HALF:], low_acc[:], RELU)
-        scatter_part(LOW, 0, HALF // 2)
-        nc.vector.tensor_copy(up_first[:].indirect(cell_sb[:, HALF // 2 // LIST_COLS : HALF // LIST_COLS]), h[LOW][:, HALF // 2 : HALF])
+        nc.vector.tensor_tensor(up[LOW][:].indirect(cell_sb[:, : FIRST // LIST_COLS]), h[LOW][:, :FIRST], zeros[:], ADD)
+        nc.vector.tensor_copy(up_first[:].indirect(cell_sb[:, FIRST // LIST_COLS : HALF // LIST_COLS]), h[LOW][:, FIRST:HALF])
         w1_mx[HIGH] = quantise("high", high_grouped[:]) + (slice(0, P),)
         planes_grouped = keep.tile([P, 2 * P * PACK], BF16, name="planes_grouped", tag="low_sc", align_bytes=64)
         dealt = planes_grouped[:].rearrange("p (e a q j) -> p a q e j", e=2, a=2, j=PACK)
@@ -194,16 +199,17 @@ def tile_picked_devox_none_e_kernel(tc, xT, w1, w2_words, w2_scales, gate, emb, 
             for a in range(2):
                 layer1(t, a * HALF, HALF, (2 * t + a + 1) % 4)
         scatter_part(LOW, HALF, HALF)
-        add_turned(LOW, up_first)
+        add_turned(LOW, [4, 5], up_first)
         scatter(HIGH)
-        add_turned(HIGH)
-        for g in range(U // BANK):
-            acc = bank(g)
-            turn(acc, pairs_turned[g][:].rearrange("r k c -> r (k c)").bitcast(F32), True, True)
-            halves = acc[:].bitcast(BF16).rearrange("p (r e) -> p r e", e=2)
+        add_turned(HIGH, [6, 7, 2, 3])
+        for c, number in enumerate((0, 1, 4, 5)):
+            acc = bank(number, CHUNK)
+            turn(acc, pairs_turned[c][:].rearrange("r k c -> r (k c)").bitcast(F32), True, True)
+            words = acc[:].bitcast(BF16).rearrange("p (r e) -> p r e", e=2)
             for first, count in placings:
-                if first // BANK == g:
-                    nc.scalar.copy(placed[first][:, :, 0:2], halves[:, first % BANK : first % BANK + count, :])
+                low, high = max(first, c * CHUNK), min(first + count, (c + 1) * CHUNK)
+                if low < high:
+                    nc.scalar.copy(placed[first][:, low - first : high - first, 0:2], words[:, low - c * CHUNK : high - c * CHUNK, :])
         scatter(THIRD)
         add_plain(nc.gpsimd, THIRD, [(0, SPLIT), (SPLIT, U)])
         scatter(FOURTH)
@@ -246,18 +252,23 @@ def tile_picked_devox_none_e_kernel(tc, xT, w1, w2_words, w2_scales, gate, emb, 
             count = term.shape[1]
             nc.vector.tensor_tensor(term, y[b][:].indirect(pos_sb[d][:, first // LIST_COLS : (first + count) // LIST_COLS]), gate_sb[d][:, first : first + count], MULT)
 
-        sum_turned = bank(5)
+        halves = [slice(a * V // 2, (a + 1) * V // 2) for a in range(2)]
+        sum_turned = [bank(5 + a, V // 2) for a in range(2)]
         for d in range(D):
             term = keep.tile([P, V], F32, name="term0_%d" % d)
             weighted(term[:], 0, d, 0)
-            turn(sum_turned, term, d == 0, d == D - 1)
-        sum_sb = keep.tile([P, V], F32, name="sum_sb")
-        nc.scalar.copy(sum_sb[:], sum_turned[:])
-        sum_back = bank(6)
-        turn(sum_back, sum_sb, True, True)
-        result0 = keep.tile([P, V], F32, name="result0")
-        nc.scalar.copy(result0[:], sum_back[:])
-        nc.scalar.dma_start(out[0:P, :], result0[:])
+            for a in range(2):
+                turn(sum_turned[a], term[:, halves[a]], d == 0, d == D - 1)
+        sum_back = []
+        for a in range(2):
+            sum_sb = keep.tile([P, V // 2], F32, name="sum_sb%d" % a)
+            nc.scalar.copy(sum_sb[:], sum_turned[a][:])
+            sum_back.append(bank((7, 0)[a], V // 2))
+            turn(sum_back[a], sum_sb, True, True)
+        for a in range(2):
+            result0 = keep.tile([P, V // 2], F32, name="result0_%d" % a)
+            nc.scalar.copy(result0[:], sum_back[a][:])
+            nc.scalar.dma_start(out[0:P, halves[a]], result0[:])
 
         terms = [keep.tile([P, V], F32, name="term1_%d" % d) for d in range(D - 1)]
         for d in range(D - 1):

@@ -138,16 +138,17 @@ def tile_picked_devox_none_e_kernel(tc, xT, w1, w2_words, w2_scales, gate, emb, 
                 nc.tensor.matmul(dst[:, cols], src[:, cols], ident[:], start=first and k == 0, stop=last and k == blocks - 1, is_transpose=True)
 
         pairs_turned = [keep.tile([P, CHUNK // P, 2 * P], BF16, name="pairs_turned%d" % c) for c in range(U // CHUNK)]
-        pieces = [(0, 256), (640, 128), (768, 256), (256, 256), (512, 128)]
+        pieces = [(0, 256), (768, 256), (256, 128), (640, 128), (384, 128), (512, 64), (576, 64)]
         z_planes = {0: keep.tile([P, 2, SPLIT], BF16, name="z_planes0"), SPLIT: keep.tile([P, 2, U - SPLIT], BF16, name="z_planes1", tag="z_planes1", align_bytes=64)}
 
         def planes(first, count):
             start = 0 if first < SPLIT else SPLIT
             return z_planes[start][:, :, first - start : first - start + count]
 
-        placings = [(0, 256), (256, 256), (512, 128), (SPLIT, U - SPLIT)]
-        placed = {first: keep.tile([P, count, PACK], BF16, name="placed%d" % first, align_bytes=64) for first, count in placings}
-        z_grouped = {first: placed[min(first, SPLIT)][:, first - min(first, SPLIT) : first - min(first, SPLIT) + count, :] for first, count in pieces}
+        placings = [(0, 256), (256, 128), (384, 128), (512, 128), (SPLIT, U - SPLIT)]
+        placed = {first: keep.tile([P, count, PACK], BF16, name="placed%d" % first, tag="placed%d" % first, align_bytes=64) for first, count in placings}
+        home = {first: max(start for start, width in placings if start <= first) for first, count in pieces}
+        z_grouped = {first: placed[home[first]][:, first - home[first] : first - home[first] + count, :] for first, count in pieces}
 
         def add_turned(t, numbers, *more):
             width = U // len(numbers)
@@ -225,24 +226,25 @@ def tile_picked_devox_none_e_kernel(tc, xT, w1, w2_words, w2_scales, gate, emb, 
 
         def layer2(dst, b, first):
             cols = slice(b * P, (b + 1) * P)
-            nc.tensor.matmul_mx(out=dst, lhsT=w2_codes[:, cols].bitcast(FP8X4), lhsT_scale=w2_sc[:, cols], rhs=z_codes[first][:].bitcast(FP8X4), rhs_scale=z_sc[first][:], start=True, stop=True)
+            nc.tensor.matmul_mx(out=dst, lhsT=w2_codes[:, cols].bitcast(FP8X4), lhsT_scale=w2_sc[:, cols], rhs=z_codes[first].bitcast(FP8X4), rhs_scale=z_sc[first][:], start=True, stop=True)
 
-        late_codes = keep.tile([P, 384], U32, name="late_codes", tag="z_planes1", align_bytes=64)
-        z_codes[0] = keep.tile([P, 256], U32, name="z_codes0", tag="emb_sb%d" % FOURTH, align_bytes=64)
-        for first, count in pieces[1:3]:
-            z_codes[first] = keep.tile([P, count], U32, name="z_codes%d" % first, align_bytes=64)
-        for first, count in pieces[3:]:
-            z_codes[first] = late_codes[:, first - 256 : first - 256 + count]
-        for first, count in pieces:
+        def quantise_cells(first, count, codes):
+            z_codes[first] = codes
             z_sc[first] = keep.tile([P, count], U8, name="z_sc%d" % first, align_bytes=64)
-            nc.vector.quantize_mx(out=z_codes[first][:].bitcast(FP8X4), scales=z_sc[first][:], in_=z_grouped[first].rearrange("p c t -> p (c t)"))
+            nc.vector.quantize_mx(out=codes.bitcast(FP8X4), scales=z_sc[first][:], in_=z_grouped[first].rearrange("p c t -> p (c t)"))
+
+        for (first, count), tag in zip(pieces[:3], ("emb_sb%d" % FOURTH, "z_codes", "z_planes1")):
+            quantise_cells(first, count, keep.tile([P, count], U32, name="z_codes%d" % first, tag=tag, align_bytes=64)[:])
+        late_codes = keep.tile([P, 384], U32, name="late_codes", tag="placed0", align_bytes=64)
+        for first, count in pieces[3:]:
+            quantise_cells(first, count, late_codes[:, first - 384 : first - 384 + count])
         for n, (first, count) in enumerate(pieces):
-            acc = bank(n, count)
+            acc = bank((0, 1, 2, 3, 6, 7, 4)[n], count)
             layer2(acc[:], 0, first)
-            unload = nc.vector.tensor_copy if n == len(pieces) - 2 else nc.scalar.copy
+            unload = nc.vector.tensor_copy if n in (1, 3) else nc.scalar.copy
             unload(y[0][:, first : first + count], acc[:])
         for g in range(U // BANK):
-            acc = bank(len(pieces) - 1 - g)
+            acc = bank(4 - g)
             for first, count in sorted(pieces):
                 if first // BANK == g:
                     layer2(acc[:, first % BANK : first % BANK + count], 1, first)

@@ -88,6 +88,8 @@ def tile_picked_devox_none_e_kernel(tc, xT, w1, w2_words, w2_scales, gate, emb, 
         nc.vector.memset(zeros[:], 0.0)
         up_first = keep.tile([P, U], F32, name="up_first")
         nc.vector.memset(up_first[:], 0.0)
+        up_high = keep.tile([P, U], F32, name="up_high")
+        nc.gpsimd.memset(up_high[:], 0.0)
 
         def deal(dst, raw, slots):
             quads = raw[:].rearrange("p j (q t) -> p q t j", t=PACK)
@@ -201,8 +203,9 @@ def tile_picked_devox_none_e_kernel(tc, xT, w1, w2_words, w2_scales, gate, emb, 
                 layer1(t, a * HALF, HALF, (2 * t + a + 1) % 4)
         scatter_part(LOW, HALF, HALF)
         add_turned(LOW, [4, 5], up_first)
-        scatter(HIGH)
-        add_turned(HIGH, [6, 7, 2, 3])
+        nc.vector.tensor_copy(up_high[:].indirect(cell_sb[:, : HALF // LIST_COLS]), h[HIGH][:, :HALF])
+        scatter_part(HIGH, HALF, HALF)
+        add_turned(HIGH, [6, 7, 2, 3], up_high)
         for c, number in enumerate((0, 1, 4, 5)):
             acc = bank(number, CHUNK)
             turn(acc, pairs_turned[c][:].rearrange("r k c -> r (k c)").bitcast(F32), True, True)

@@ -16,16 +16,13 @@ FP8X4 = mybir.dt.float8_e4m3fn_x4
 ADD = mybir.AluOpType.add
 MULT = mybir.AluOpType.mult
 RELU = mybir.ActivationFunctionType.Relu
+COPY = mybir.ActivationFunctionType.Copy
 
 P = 128
 PACK = 4
 HALF = S // 2
 LIST_COLS = 16
-SPLIT = 640
-FIRST = 64
 BANK = 512
-CHUNK = 256
-LOW, HIGH, THIRD, FOURTH = range(4)
 
 
 def tile_picked_devox_none_e_kernel(tc, xT, w1, w2_words, w2_scales, gate, emb, offs, cell, pos1, pos2, pos3, out):
@@ -42,9 +39,9 @@ def tile_picked_devox_none_e_kernel(tc, xT, w1, w2_words, w2_scales, gate, emb, 
             nc.sync.dma_start(tile[:], src)
             return tile
 
-        w1_rows = w1.rearrange("(p j) c -> p j c", j=PACK)
-        w1_first = [keep.tile([P, 2, H // 2], F32, name="w1_first%d" % u) for u in range(2)]
-        w1_second = keep.tile([P, PACK, H // 2], F32, name="w1_second")
+        def entries(tile, first, count):
+            return tile[:, first // LIST_COLS : (first + count) // LIST_COLS]
+
         x_rows = xT.rearrange("(p j) t -> j p t", j=PACK)
         x_planes = []
         for j in range(PACK):
@@ -53,198 +50,132 @@ def tile_picked_devox_none_e_kernel(tc, xT, w1, w2_words, w2_scales, gate, emb, 
             x_planes.append(plane)
             if j == 0:
                 offs_sb = list_tile("offs_sb", offs)
+        w1_rows = w1.rearrange("(p j) c -> p j c", j=PACK)
+        w1_sb = [keep.tile([P, 2, H], F32, name="w1_sb%d" % u) for u in range(2)]
         for u in range(2):
-            nc.sync.dma_start(w1_first[u][:], w1_rows[:, 2 * u : 2 * u + 2, : H // 2])
-        nc.sync.dma_start(w1_second[:], w1_rows[:, :, H // 2 :])
+            nc.sync.dma_start(w1_sb[u][:], w1_rows[:, 2 * u : 2 * u + 2, :])
         cell_sb = list_tile("cell_sb", cell)
 
-        emb_sb = [keep.tile([P, U], F32, name="emb_sb%d" % t, tag="emb_sb%d" % t, align_bytes=64) for t in range(PACK)]
-        emb_quads = emb.rearrange("(a q t) r -> a q t r", a=2, t=PACK)
         emb_rows = emb.rearrange("(p t) r -> t p r", t=PACK)
-        nc.sync.dma_start(emb_sb[LOW][:], emb_quads[0, :, 0:2, :])
-        nc.sync.dma_start(emb_sb[HIGH][:], emb_quads[1, :, 0:2, :])
+        emb_sb = [keep.tile([P, U], F32, name="emb_sb%d" % t) for t in range(PACK)]
+        for t in range(2):
+            nc.sync.dma_start(emb_sb[t][:], emb_rows[t])
         w2_codes = keep.tile([P, N], U32, name="w2_codes", align_bytes=64)
         nc.sync.dma_start(w2_codes[:].bitcast(I32), w2_words[0].rearrange("p n t -> p (n t)").bitcast(I32))
         w2_sc = keep.tile([P, N], U8, name="w2_sc", align_bytes=64)
         nc.vector.memset(w2_sc[:].bitcast(I32), 0)
         for q in range(4):
             nc.sync.dma_start(w2_sc[32 * q : 32 * q + 4, :].bitcast(I32), w2_scales[0, 4 * q : 4 * q + 4, :].bitcast(I32))
-        gate_sb = [keep.tile([P, V], F32, name="gate_sb%d" % d, tag="gate_sb%d" % d) for d in range(D)]
+        for t in range(2, PACK):
+            nc.sync.dma_start(emb_sb[t][:], emb_rows[t])
+        gate_sb = [keep.tile([P, V], F32, name="gate_sb%d" % d) for d in range(D)]
         for d in range(D):
             nc.sync.dma_start(gate_sb[d][:], gate[d])
         pos_sb = [list_tile("pos%d_sb" % d, src) for d, src in enumerate((pos1, pos2, pos3))]
-        nc.sync.dma_start(emb_sb[THIRD][:], emb_rows[2])
-        nc.sync.dma_start(emb_sb[FOURTH][:], emb_rows[3])
 
         ident = keep.tile([P, P], F32, name="ident")
         make_identity(nc, ident[:])
-
         up = []
         for t in range(PACK):
             tile = keep.tile([P, U], F32, name="up%d" % t)
-            (nc.vector if t < THIRD else nc.gpsimd).memset(tile[:], 0.0)
+            (nc.vector if t < 2 else nc.gpsimd).memset(tile[:], 0.0)
             up.append(tile)
-        zeros = keep.tile([P, FIRST], F32, name="zeros")
-        nc.vector.memset(zeros[:], 0.0)
-        up_first = keep.tile([P, U], F32, name="up_first")
-        nc.vector.memset(up_first[:], 0.0)
-        up_high = keep.tile([P, U], F32, name="up_high")
-        nc.gpsimd.memset(up_high[:], 0.0)
-
-        def deal(dst, raw, slots):
-            quads = raw[:].rearrange("p j (q t) -> p q t j", t=PACK)
-            nc.scalar.copy(dst, quads[:, :, slots, :])
-
-        def quantise(name, grouped):
-            count = grouped.shape[1] // PACK
-            codes = keep.tile([P, count], U32, name=name + "_codes", tag=name + "_codes", align_bytes=64)
-            scales = keep.tile([P, count], U8, name=name + "_sc", tag=name + "_sc", align_bytes=64)
-            nc.vector.quantize_mx(out=codes[:].bitcast(FP8X4), scales=scales[:], in_=grouped)
-            return codes, scales
 
         x_grouped = [keep.tile([P, HALF, PACK], BF16, name="x_grouped%d" % a, align_bytes=64) for a in range(2)]
-        x_codes = {}
-        x_sc = [keep.tile([P, HALF], U8, name="x_sc%d" % a, align_bytes=64) for a in range(2)]
+        x_codes = keep.tile([P, S], U32, name="x_codes", align_bytes=64)
+        x_sc = keep.tile([P, S], U8, name="x_sc", align_bytes=64)
+        for j in range(PACK):
+            for a in range(2):
+                nc.vector.tensor_copy(x_grouped[a][:, :, j], x_planes[j][:].indirect(entries(offs_sb, a * HALF, HALF)))
+        for a in range(2):
+            points = slice(a * HALF, (a + 1) * HALF)
+            nc.vector.quantize_mx(out=x_codes[:, points].bitcast(FP8X4), scales=x_sc[:, points], in_=x_grouped[a][:].rearrange("p c j -> p (c j)"))
 
-        def half_cols(a):
-            return slice(a * HALF // LIST_COLS, (a + 1) * HALF // LIST_COLS)
+        w1_grouped = [keep.tile([P, 2, P, PACK], BF16, name="w1_grouped%d" % g, align_bytes=64) for g in range(2)]
+        w1_codes = [keep.tile([P, 2 * P], U32, name="w1_codes%d" % g, align_bytes=64) for g in range(2)]
+        w1_sc = [keep.tile([P, 2 * P], U8, name="w1_sc%d" % g, align_bytes=64) for g in range(2)]
 
-        def gather_x(j, a):
-            nc.vector.tensor_copy(x_grouped[a][:, :, j], x_planes[j][:].indirect(offs_sb[:, half_cols(a)]))
+        def deal(copy, g, u):
+            copy(w1_grouped[g][:, :, :, 2 * u : 2 * u + 2], w1_sb[u][:].rearrange("p j (m t) -> p t m j", t=PACK)[:, 2 * g : 2 * g + 2, :, :])
 
-        def quantise_x(a, tag):
-            x_codes[a] = keep.tile([P, HALF], U32, name="x_codes%d" % a, tag=tag, align_bytes=64)
-            nc.vector.quantize_mx(out=x_codes[a][:].bitcast(FP8X4), scales=x_sc[a][:], in_=x_grouped[a][:].rearrange("p c j -> p (c j)"))
+        for g in range(2):
+            deal(nc.scalar.copy, g, 0)
+        for g in range(2):
+            deal(nc.vector.tensor_copy, g, 1)
+            nc.vector.quantize_mx(out=w1_codes[g][:].bitcast(FP8X4), scales=w1_sc[g][:], in_=w1_grouped[g][:].rearrange("p e m j -> p (e m j)"))
 
         h = [keep.tile([P, S], F32, name="h%d" % t) for t in range(PACK)]
 
-        w1_mx = {}
-
         def product(t, first, count, number):
             acc = bank(number, count)
-            w1_codes, w1_sc, cols = w1_mx[t]
-            a, points = first // HALF, slice(first % HALF, first % HALF + count)
-            nc.tensor.matmul_mx(out=acc[:], lhsT=w1_codes[:, cols].bitcast(FP8X4), lhsT_scale=w1_sc[:, cols], rhs=x_codes[a][:, points].bitcast(FP8X4), rhs_scale=x_sc[a][:, points], start=True, stop=True)
+            cols = slice(t % 2 * P, (t % 2 + 1) * P)
+            points = slice(first, first + count)
+            nc.tensor.matmul_mx(out=acc[:], lhsT=w1_codes[t // 2][:, cols].bitcast(FP8X4), lhsT_scale=w1_sc[t // 2][:, cols], rhs=x_codes[:, points].bitcast(FP8X4), rhs_scale=x_sc[:, points], start=True, stop=True)
             return acc
 
-        def layer1(t, first, count, number):
+        def relu_scalar(t, first, count, number):
             nc.scalar.activation(h[t][:, first : first + count], product(t, first, count, number)[:], RELU)
 
-        def scatter_part(t, first, count):
-            nc.vector.tensor_copy(up[t][:].indirect(cell_sb[:, first // LIST_COLS : (first + count) // LIST_COLS]), h[t][:, first : first + count])
+        def relu_vector(t, first, count, number):
+            nc.vector.tensor_scalar_max(h[t][:, first : first + count], product(t, first, count, number)[:], 0.0)
 
-        def turn(dst, src, first, last):
-            blocks = src.shape[1] // P
-            for k in range(blocks):
-                cols = slice(k * P, (k + 1) * P)
-                nc.tensor.matmul(dst[:, cols], src[:, cols], ident[:], start=first and k == 0, stop=last and k == blocks - 1, is_transpose=True)
+        def scatter_scalar(t, first, count):
+            nc.scalar.activation(up[t][:].indirect(entries(cell_sb, first, count)), h[t][:, first : first + count], COPY)
 
-        pairs_turned = [keep.tile([P, CHUNK // P, 2 * P], BF16, name="pairs_turned%d" % c) for c in range(U // CHUNK)]
-        pieces = [(0, 256), (768, 256), (256, 128), (640, 128), (384, 128), (512, 64), (576, 64)]
-        z_planes = {0: keep.tile([P, 2, SPLIT], BF16, name="z_planes0"), SPLIT: keep.tile([P, 2, U - SPLIT], BF16, name="z_planes1", tag="z_planes1", align_bytes=64)}
-
-        def planes(first, count):
-            start = 0 if first < SPLIT else SPLIT
-            return z_planes[start][:, :, first - start : first - start + count]
-
-        placings = [(0, 256), (256, 128), (384, 128), (512, 128), (SPLIT, U - SPLIT)]
-        placed = {first: keep.tile([P, count, PACK], BF16, name="placed%d" % first, tag="placed%d" % first, align_bytes=64) for first, count in placings}
-        home = {first: max(start for start, width in placings if start <= first) for first, count in pieces}
-        z_grouped = {first: placed[home[first]][:, first - home[first] : first - home[first] + count, :] for first, count in pieces}
-
-        def add_turned(t, numbers, *more):
-            width = U // len(numbers)
-            sums = [bank(number, width) for number in numbers]
-            for g, acc in enumerate(sums):
-                for n, window in enumerate((emb_sb[t],) + more):
-                    turn(acc, window[:, g * width : (g + 1) * width], n == 0, False)
-            for g, acc in enumerate(sums):
-                turn(acc, up[t][:, g * width : (g + 1) * width], False, True)
-                for e in range(width // CHUNK):
-                    nc.scalar.copy(pairs_turned[g * width // CHUNK + e][:, :, t * P : (t + 1) * P], acc[:, e * CHUNK : (e + 1) * CHUNK].rearrange("r (k m) -> r k m", m=P))
-
-        def add_plain(engine, t, spans):
-            for first, end in spans:
-                cols = slice(first, end)
-                engine.tensor_tensor(planes(first, end - first)[:, t - THIRD, :], up[t][:, cols], emb_sb[t][:, cols], ADD)
-
-        def scatter(t):
+        def scatter_vector(t):
             nc.vector.tensor_copy(up[t][:].indirect(cell_sb[:]), h[t][:])
 
-        for j in range(PACK):
-            for a in range(2):
-                gather_x(j, a)
-        low_grouped = keep.tile([P, P * PACK], BF16, name="low_grouped", tag="low_grouped", align_bytes=64)
-        for u in range(2):
-            deal(low_grouped[:].rearrange("p (q e j) -> p q e j", e=2, j=PACK)[:, :, :, 2 * u : 2 * u + 2], w1_first[u], slice(0, 2))
-        quantise_x(0, "x_codes0")
-        w1_mx[LOW] = quantise("low", low_grouped[:]) + (slice(0, P),)
-        layer1(LOW, 0, FIRST, 0)
-        layer1(LOW, FIRST, FIRST, 3)
-        layer1(LOW, HALF // 2, HALF // 2, 1)
-        quantise_x(1, "low_grouped")
-        low_acc = product(LOW, HALF, HALF, 2)
-        high_grouped = keep.tile([P, P * PACK], BF16, name="high_grouped", tag="low_codes", align_bytes=64)
-        deal(high_grouped[:].rearrange("p (q e j) -> p q e j", e=2, j=PACK), w1_second, slice(0, 2))
-        nc.scalar.activation(h[LOW][:, HALF:], low_acc[:], RELU)
-        nc.vector.tensor_tensor(up[LOW][:].indirect(cell_sb[:, : FIRST // LIST_COLS]), h[LOW][:, :FIRST], zeros[:], ADD)
-        nc.vector.tensor_copy(up_first[:].indirect(cell_sb[:, FIRST // LIST_COLS : HALF // LIST_COLS]), h[LOW][:, FIRST:HALF])
-        w1_mx[HIGH] = quantise("high", high_grouped[:]) + (slice(0, P),)
-        planes_grouped = keep.tile([P, 2 * P * PACK], BF16, name="planes_grouped", tag="low_sc", align_bytes=64)
-        dealt = planes_grouped[:].rearrange("p (e a q j) -> p a q e j", e=2, a=2, j=PACK)
-        for u in range(2):
-            deal(dealt[:, 0, :, :, 2 * u : 2 * u + 2], w1_first[u], slice(2, 4))
-        deal(dealt[:, 1], w1_second, slice(2, 4))
-        planes_mx = quantise("planes", planes_grouped[:])
-        w1_mx[THIRD] = planes_mx + (slice(0, P),)
-        w1_mx[FOURTH] = planes_mx + (slice(P, 2 * P),)
-        for t in (HIGH, THIRD, FOURTH):
-            for a in range(2):
-                layer1(t, a * HALF, HALF, (2 * t + a + 1) % 4)
-        scatter_part(LOW, HALF, HALF)
-        add_turned(LOW, [4, 5], up_first)
-        nc.vector.tensor_copy(up_high[:].indirect(cell_sb[:, : HALF // LIST_COLS]), h[HIGH][:, :HALF])
-        scatter_part(HIGH, HALF, HALF)
-        add_turned(HIGH, [6, 7, 2, 3], up_high)
-        for c, number in enumerate((0, 1, 4, 5)):
-            acc = bank(number, CHUNK)
-            turn(acc, pairs_turned[c][:].rearrange("r k c -> r (k c)").bitcast(F32), True, True)
-            words = acc[:].bitcast(BF16).rearrange("p (r e) -> p r e", e=2)
-            for first, count in placings:
-                low, high = max(first, c * CHUNK), min(first + count, (c + 1) * CHUNK)
-                if low < high:
-                    nc.scalar.copy(placed[first][:, low - first : high - first, 0:2], words[:, low - c * CHUNK : high - c * CHUNK, :])
-        scatter(THIRD)
-        add_plain(nc.gpsimd, THIRD, [(0, SPLIT), (SPLIT, U)])
-        scatter(FOURTH)
-        add_plain(nc.vector, FOURTH, [(0, 256), (SPLIT, U), (256, SPLIT)])
+        relu_scalar(0, 0, S, 0)
+        relu_scalar(1, 0, HALF, 1)
+        scatter_vector(0)
+        relu_scalar(1, HALF, HALF, 2)
+        scatter_scalar(1, 0, HALF)
+        relu_scalar(3, 0, HALF, 4)
+        scatter_scalar(1, HALF, HALF)
+        relu_vector(2, 0, S, 3)
+        scatter_vector(2)
+        scatter_scalar(3, 0, HALF)
+        relu_scalar(3, HALF, HALF, 5)
+        scatter_scalar(3, HALF, HALF)
 
-        y = [keep.tile([P, U], F32, name="y%d" % b) for b in range(N // P)]
-        for first, count in placings:
-            place = nc.scalar.copy if first < SPLIT else nc.vector.tensor_copy
-            place(placed[first][:, :, 2:4], planes(first, count).rearrange("p t r -> p r t"))
+        spans = [(0, 256), (256, 384), (640, 384)]
+        z_planes = {first: keep.tile([P, PACK, count], BF16, name="z_planes%d" % first, align_bytes=64) for first, count in spans}
+
+        def add_emb(engine, t, first, count):
+            cols = slice(first, first + count)
+            engine.tensor_tensor(z_planes[first][:, t, :], up[t][:, cols], emb_sb[t][:, cols], ADD)
+
+        for t in range(2):
+            for first, count in spans:
+                add_emb(nc.gpsimd, t, first, count)
+        for first, count in spans:
+            for t in range(2, PACK):
+                add_emb(nc.vector, t, first, count)
+
+        pieces = [(0, 256), (640, 256), (256, 256), (896, 128), (512, 128)]
+        z_grouped = {first: keep.tile([P, count, PACK], BF16, name="z_grouped%d" % first, align_bytes=64) for first, count in pieces}
+        for first, count in sorted(pieces):
+            home = max(start for start, width in spans if start <= first)
+            weave = nc.scalar.copy if first < 640 else nc.vector.tensor_copy
+            src = z_planes[home][:, :, first - home : first - home + count]
+            weave(z_grouped[first][:].rearrange("p (c i) t -> p c t i", i=4), src.rearrange("p t (c i) -> p c t i", i=4))
 
         z_codes = {}
         z_sc = {}
+        for first, count in pieces:
+            z_codes[first] = keep.tile([P, count], U32, name="z_codes%d" % first, align_bytes=64)
+            z_sc[first] = keep.tile([P, count], U8, name="z_sc%d" % first, align_bytes=64)
+            nc.vector.quantize_mx(out=z_codes[first][:].bitcast(FP8X4), scales=z_sc[first][:], in_=z_grouped[first][:].rearrange("p c t -> p (c t)"))
 
         def layer2(dst, b, first):
             cols = slice(b * P, (b + 1) * P)
-            nc.tensor.matmul_mx(out=dst, lhsT=w2_codes[:, cols].bitcast(FP8X4), lhsT_scale=w2_sc[:, cols], rhs=z_codes[first].bitcast(FP8X4), rhs_scale=z_sc[first][:], start=True, stop=True)
+            nc.tensor.matmul_mx(out=dst, lhsT=w2_codes[:, cols].bitcast(FP8X4), lhsT_scale=w2_sc[:, cols], rhs=z_codes[first][:].bitcast(FP8X4), rhs_scale=z_sc[first][:], start=True, stop=True)
 
-        def quantise_cells(first, count, codes):
-            z_codes[first] = codes
-            z_sc[first] = keep.tile([P, count], U8, name="z_sc%d" % first, align_bytes=64)
-            nc.vector.quantize_mx(out=codes.bitcast(FP8X4), scales=z_sc[first][:], in_=z_grouped[first].rearrange("p c t -> p (c t)"))
-
-        for (first, count), tag in zip(pieces[:3], ("emb_sb%d" % FOURTH, "z_codes", "z_planes1")):
-            quantise_cells(first, count, keep.tile([P, count], U32, name="z_codes%d" % first, tag=tag, align_bytes=64)[:])
-        late_codes = keep.tile([P, 384], U32, name="late_codes", tag="placed0", align_bytes=64)
-        for first, count in pieces[3:]:
-            quantise_cells(first, count, late_codes[:, first - 384 : first - 384 + count])
+        y = [keep.tile([P, U], F32, name="y%d" % b) for b in range(N // P)]
         for n, (first, count) in enumerate(pieces):
-            acc = bank((0, 1, 2, 3, 6, 7, 4)[n], count)
+            acc = bank(n, count)
             layer2(acc[:], 0, first)
-            unload = nc.vector.tensor_copy if n in (1, 3) else nc.scalar.copy
+            unload = nc.vector.tensor_copy if n == 3 else nc.scalar.copy
             unload(y[0][:, first : first + count], acc[:])
         for g in range(U // BANK):
             acc = bank(4 - g)
@@ -253,9 +184,15 @@ def tile_picked_devox_none_e_kernel(tc, xT, w1, w2_words, w2_scales, gate, emb, 
                     layer2(acc[:, first % BANK : first % BANK + count], 1, first)
             nc.scalar.copy(y[1][:, g * BANK : (g + 1) * BANK], acc[:])
 
+        def turn(dst, src, first, last):
+            blocks = src.shape[1] // P
+            for k in range(blocks):
+                cols = slice(k * P, (k + 1) * P)
+                nc.tensor.matmul(dst[:, cols], src[:, cols], ident[:], start=first and k == 0, stop=last and k == blocks - 1, is_transpose=True)
+
         def weighted(term, b, d, first):
             count = term.shape[1]
-            nc.vector.tensor_tensor(term, y[b][:].indirect(pos_sb[d][:, first // LIST_COLS : (first + count) // LIST_COLS]), gate_sb[d][:, first : first + count], MULT)
+            nc.vector.tensor_tensor(term, y[b][:].indirect(entries(pos_sb[d], first, count)), gate_sb[d][:, first : first + count], MULT)
 
         halves = [slice(a * V // 2, (a + 1) * V // 2) for a in range(2)]
         sum_turned = [bank(5 + a, V // 2) for a in range(2)]
@@ -264,6 +201,11 @@ def tile_picked_devox_none_e_kernel(tc, xT, w1, w2_words, w2_scales, gate, emb, 
             weighted(term[:], 0, d, 0)
             for a in range(2):
                 turn(sum_turned[a], term[:, halves[a]], d == 0, d == D - 1)
+        raw = []
+        for d in range(2):
+            tile = keep.tile([P, V], F32, name="raw%d" % d)
+            nc.scalar.activation(tile[:], y[1][:].indirect(pos_sb[d][:]), COPY)
+            raw.append(tile)
         sum_back = []
         for a in range(2):
             sum_sb = keep.tile([P, V // 2], F32, name="sum_sb%d" % a)
@@ -275,19 +217,14 @@ def tile_picked_devox_none_e_kernel(tc, xT, w1, w2_words, w2_scales, gate, emb, 
             nc.scalar.copy(result0[:], sum_back[a][:])
             nc.scalar.dma_start(out[0:P, halves[a]], result0[:])
 
-        terms = [keep.tile([P, V], F32, name="term1_%d" % d) for d in range(D - 1)]
-        for d in range(D - 1):
-            weighted(terms[d][:], 1, d, 0)
-        last_early = keep.tile([P, V // 2], F32, name="last_early")
-        weighted(last_early[:], 1, D - 1, 0)
+        terms = [keep.tile([P, V], F32, name="term1_%d" % d) for d in range(D)]
+        nc.vector.tensor_tensor(terms[0][:], raw[0][:], gate_sb[0][:], MULT)
+        weighted(terms[2][:], 1, 2, 0)
+        nc.vector.tensor_tensor(terms[1][:], raw[1][:], gate_sb[1][:], MULT)
         pair = keep.tile([P, V], F32, name="pair")
-        nc.vector.tensor_tensor(pair[:], terms[0][:], terms[1][:], ADD)
-        last_late = keep.tile([P, V // 2], F32, name="last_late", tag="gate_sb1")
-        parts = [(0, last_early[:]), (V // 2, last_late[:, : V // 4]), (3 * V // 4, last_late[:, V // 4 :])]
-        for first, last in parts[1:]:
-            weighted(last, 1, D - 1, first)
-        for first, last in parts:
-            cols = slice(first, first + last.shape[1])
-            result1 = keep.tile([P, last.shape[1]], F32, name="result1_%d" % first)
-            nc.vector.tensor_tensor(result1[:], pair[:, cols], last, ADD)
+        nc.vector.tensor_tensor(pair[:], terms[0][:], terms[2][:], ADD)
+        for first, count in ((0, 256), (256, 128), (384, 128)):
+            cols = slice(first, first + count)
+            result1 = keep.tile([P, count], F32, name="result1_%d" % first)
+            nc.vector.tensor_tensor(result1[:], pair[:, cols], terms[1][:, cols], ADD)
             nc.sync.dma_start(out[P : 2 * P, cols], result1[:])

@@ -51,9 +51,9 @@ def tile_picked_devox_none_e_kernel(tc, xT, w1, w2_words, w2_scales, gate, emb, 
             if j == 0:
                 offs_sb = list_tile("offs_sb", offs)
         w1_rows = w1.rearrange("(p j) c -> p j c", j=PACK)
-        w1_sb = [keep.tile([P, 2, H], F32, name="w1_sb%d" % u) for u in range(2)]
+        w1_sb = keep.tile([P, PACK, H], F32, name="w1_sb")
         for u in range(2):
-            nc.sync.dma_start(w1_sb[u][:], w1_rows[:, 2 * u : 2 * u + 2, :])
+            nc.sync.dma_start(w1_sb[:, 2 * u : 2 * u + 2, :], w1_rows[:, 2 * u : 2 * u + 2, :])
         cell_sb = list_tile("cell_sb", cell)
 
         emb_rows = emb.rearrange("(p t) r -> t p r", t=PACK)
@@ -92,97 +92,120 @@ def tile_picked_devox_none_e_kernel(tc, xT, w1, w2_words, w2_scales, gate, emb, 
             nc.vector.quantize_mx(out=x_codes[:, points].bitcast(FP8X4), scales=x_sc[:, points], in_=x_grouped[a][:].rearrange("p c j -> p (c j)"))
 
         w1_grouped = [keep.tile([P, 2, P, PACK], BF16, name="w1_grouped%d" % g, align_bytes=64) for g in range(2)]
-        w1_codes = [keep.tile([P, 2 * P], U32, name="w1_codes%d" % g, align_bytes=64) for g in range(2)]
-        w1_sc = [keep.tile([P, 2 * P], U8, name="w1_sc%d" % g, align_bytes=64) for g in range(2)]
+        w1_mx = {}
 
-        def deal(copy, g, u):
-            copy(w1_grouped[g][:, :, :, 2 * u : 2 * u + 2], w1_sb[u][:].rearrange("p j (m t) -> p t m j", t=PACK)[:, 2 * g : 2 * g + 2, :, :])
+        def deal(copy, g, rows):
+            copy(w1_grouped[g][:, :, :, rows].rearrange("p e m j -> p m j e"), w1_sb[:, rows, :].rearrange("p j (m t) -> p m j t", t=PACK)[:, :, :, 2 * g : 2 * g + 2])
 
-        for g in range(2):
-            deal(nc.scalar.copy, g, 0)
-        for g in range(2):
-            deal(nc.vector.tensor_copy, g, 1)
-            nc.vector.quantize_mx(out=w1_codes[g][:].bitcast(FP8X4), scales=w1_sc[g][:], in_=w1_grouped[g][:].rearrange("p e m j -> p (e m j)"))
+        def quantise_w1(first, count):
+            codes = keep.tile([P, count * P], U32, name="w1_codes%d" % first, align_bytes=64)
+            scales = keep.tile([P, count * P], U8, name="w1_sc%d" % first, align_bytes=64)
+            src = w1_grouped[first // 2][:, first % 2 : first % 2 + count, :, :]
+            nc.vector.quantize_mx(out=codes[:].bitcast(FP8X4), scales=scales[:], in_=src.rearrange("p e m j -> p (e m j)"))
+            for e in range(count):
+                w1_mx[first + e] = (codes[:, e * P : (e + 1) * P], scales[:, e * P : (e + 1) * P])
+
+        deal(nc.scalar.copy, 0, slice(0, 2))
+        deal(nc.vector.tensor_copy, 0, slice(2, 4))
+        deal(nc.scalar.copy, 1, slice(0, 4))
+        quantise_w1(0, 1)
+        quantise_w1(1, 1)
+        quantise_w1(2, 2)
 
         h = [keep.tile([P, S], F32, name="h%d" % t) for t in range(PACK)]
 
         def product(t, first, count, number):
             acc = bank(number, count)
-            cols = slice(t % 2 * P, (t % 2 + 1) * P)
             points = slice(first, first + count)
-            nc.tensor.matmul_mx(out=acc[:], lhsT=w1_codes[t // 2][:, cols].bitcast(FP8X4), lhsT_scale=w1_sc[t // 2][:, cols], rhs=x_codes[:, points].bitcast(FP8X4), rhs_scale=x_sc[:, points], start=True, stop=True)
+            nc.tensor.matmul_mx(out=acc[:], lhsT=w1_mx[t][0].bitcast(FP8X4), lhsT_scale=w1_mx[t][1], rhs=x_codes[:, points].bitcast(FP8X4), rhs_scale=x_sc[:, points], start=True, stop=True)
             return acc
 
         def relu_scalar(t, first, count, number):
             nc.scalar.activation(h[t][:, first : first + count], product(t, first, count, number)[:], RELU)
 
-        def relu_vector(t, first, count, number):
-            nc.vector.tensor_scalar_max(h[t][:, first : first + count], product(t, first, count, number)[:], 0.0)
-
         def scatter_scalar(t, first, count):
             nc.scalar.activation(up[t][:].indirect(entries(cell_sb, first, count)), h[t][:, first : first + count], COPY)
 
-        def scatter_vector(t):
-            nc.vector.tensor_copy(up[t][:].indirect(cell_sb[:]), h[t][:])
+        def relu_vector(t, first, count, number):
+            nc.vector.tensor_scalar_max(h[t][:, first : first + count], product(t, first, count, number)[:], 0.0)
 
-        relu_scalar(0, 0, S, 0)
+        def scatter_vector(t, first, count):
+            nc.vector.tensor_copy(up[t][:].indirect(entries(cell_sb, first, count)), h[t][:, first : first + count])
+
+        relu_scalar(0, 0, HALF, 0)
+        scatter_vector(0, 0, HALF)
         relu_scalar(1, 0, HALF, 1)
-        scatter_vector(0)
-        relu_scalar(1, HALF, HALF, 2)
+        relu_scalar(0, HALF, HALF, 3)
         scatter_scalar(1, 0, HALF)
-        relu_scalar(3, 0, HALF, 4)
+        relu_vector(1, HALF, HALF, 0)
+        scatter_vector(0, HALF, HALF)
+        relu_scalar(2, 0, S, 5)
+        scatter_vector(2, 0, S)
+        relu_scalar(3, 0, HALF, 6)
         scatter_scalar(1, HALF, HALF)
-        relu_vector(2, 0, S, 3)
-        scatter_vector(2)
+        relu_scalar(3, HALF, HALF, 7)
         scatter_scalar(3, 0, HALF)
-        relu_scalar(3, HALF, HALF, 5)
         scatter_scalar(3, HALF, HALF)
 
-        spans = [(0, 256), (256, 384), (640, 384)]
-        z_planes = {first: keep.tile([P, PACK, count], BF16, name="z_planes%d" % first, align_bytes=64) for first, count in spans}
+        z_planes = keep.tile([P, U // P, PACK, P], BF16, name="z_planes")
 
         def add_emb(engine, t, first, count):
             cols = slice(first, first + count)
-            engine.tensor_tensor(z_planes[first][:, t, :], up[t][:, cols], emb_sb[t][:, cols], ADD)
+            engine.tensor_tensor(z_planes[:, first // P : (first + count) // P, t, :], up[t][:, cols].rearrange("p (b c) -> p b c", c=P), emb_sb[t][:, cols].rearrange("p (b c) -> p b c", c=P), ADD)
 
-        for t in range(2):
-            for first, count in spans:
-                add_emb(nc.gpsimd, t, first, count)
-        for first, count in spans:
-            for t in range(2, PACK):
-                add_emb(nc.vector, t, first, count)
+        add_emb(nc.gpsimd, 0, 0, U)
+        add_emb(nc.gpsimd, 1, 0, 256)
+        add_emb(nc.vector, 1, 256, 768)
+        add_emb(nc.vector, 2, 0, U)
+        for first, count in ((0, 256), (256, 256), (512, 512)):
+            add_emb(nc.vector, 3, first, count)
 
-        pieces = [(0, 256), (640, 256), (256, 256), (896, 128), (512, 128)]
-        z_grouped = {first: keep.tile([P, count, PACK], BF16, name="z_grouped%d" % first, align_bytes=64) for first, count in pieces}
-        for first, count in sorted(pieces):
-            home = max(start for start, width in spans if start <= first)
-            weave = nc.scalar.copy if first < 640 else nc.vector.tensor_copy
-            src = z_planes[home][:, :, first - home : first - home + count]
-            weave(z_grouped[first][:].rearrange("p (c i) t -> p c t i", i=4), src.rearrange("p t (c i) -> p c t i", i=4))
+        z_grouped = {}
+        z_mx = {}
 
-        z_codes = {}
-        z_sc = {}
-        for first, count in pieces:
-            z_codes[first] = keep.tile([P, count], U32, name="z_codes%d" % first, align_bytes=64)
-            z_sc[first] = keep.tile([P, count], U8, name="z_sc%d" % first, align_bytes=64)
-            nc.vector.quantize_mx(out=z_codes[first][:].bitcast(FP8X4), scales=z_sc[first][:], in_=z_grouped[first][:].rearrange("p c t -> p (c t)"))
+        def weave(copy, first, count):
+            z_grouped[first] = keep.tile([P, count, PACK], BF16, name="z_grouped%d" % first, align_bytes=64)
+            src = z_planes[:, first // P : (first + count) // P, :, :]
+            copy(z_grouped[first][:].rearrange("p (b c i) t -> p b c t i", c=P // 4, i=4), src.rearrange("p b t (c i) -> p b c t i", i=4))
 
-        def layer2(dst, b, first):
+        def quantise_z(first, count, home):
+            codes = keep.tile([P, count], U32, name="z_codes%d" % first, align_bytes=64)
+            scales = keep.tile([P, count], U8, name="z_sc%d" % first, align_bytes=64)
+            src = z_grouped[home][:, first - home : first - home + count, :]
+            nc.vector.quantize_mx(out=codes[:].bitcast(FP8X4), scales=scales[:], in_=src.rearrange("p c t -> p (c t)"))
+            z_mx[first] = (codes, scales)
+
+        weave(nc.scalar.copy, 0, 256)
+        weave(nc.scalar.copy, 256, 256)
+        weave(nc.vector.tensor_copy, 512, 256)
+        quantise_z(0, 256, 0)
+        quantise_z(512, 256, 512)
+        weave(nc.vector.tensor_copy, 768, 256)
+        quantise_z(256, 256, 256)
+        quantise_z(768, 128, 768)
+        quantise_z(896, 128, 768)
+
+        y = [keep.tile([P, U], F32, name="y%d" % b, tag="y%d" % b) for b in range(N // P)]
+
+        def layer2(unload, b, first, count, number):
+            acc = bank(number, count)
             cols = slice(b * P, (b + 1) * P)
-            nc.tensor.matmul_mx(out=dst, lhsT=w2_codes[:, cols].bitcast(FP8X4), lhsT_scale=w2_sc[:, cols], rhs=z_codes[first][:].bitcast(FP8X4), rhs_scale=z_sc[first][:], start=True, stop=True)
+            for start in sorted(z_mx):
+                if first <= start < first + count:
+                    codes, scales = z_mx[start]
+                    width = codes.shape[1]
+                    nc.tensor.matmul_mx(out=acc[:, start - first : start - first + width], lhsT=w2_codes[:, cols].bitcast(FP8X4), lhsT_scale=w2_sc[:, cols], rhs=codes[:].bitcast(FP8X4), rhs_scale=scales[:], start=True, stop=True)
+            unload(y[b][:, first : first + count], acc[:])
 
-        y = [keep.tile([P, U], F32, name="y%d" % b) for b in range(N // P)]
-        for n, (first, count) in enumerate(pieces):
-            acc = bank(n, count)
-            layer2(acc[:], 0, first)
-            unload = nc.vector.tensor_copy if n == 3 else nc.scalar.copy
-            unload(y[0][:, first : first + count], acc[:])
-        for g in range(U // BANK):
-            acc = bank(4 - g)
-            for first, count in sorted(pieces):
-                if first // BANK == g:
-                    layer2(acc[:, first % BANK : first % BANK + count], 1, first)
-            nc.scalar.copy(y[1][:, g * BANK : (g + 1) * BANK], acc[:])
+        layer2(nc.scalar.copy, 0, 0, 256, 0)
+        layer2(nc.scalar.copy, 1, 0, 256, 1)
+        layer2(nc.scalar.copy, 0, 512, 256, 2)
+        layer2(nc.scalar.copy, 1, 512, 256, 3)
+        layer2(nc.scalar.copy, 0, 256, 256, 4)
+        layer2(nc.scalar.copy, 1, 256, 256, 7)
+        layer2(nc.vector.tensor_copy, 0, 768, 128, 5)
+        layer2(nc.vector.tensor_copy, 0, 896, 128, 6)
+        layer2(nc.scalar.copy, 1, 768, 256, 0)
 
         def turn(dst, src, first, last):
             blocks = src.shape[1] // P
@@ -195,36 +218,36 @@ def tile_picked_devox_none_e_kernel(tc, xT, w1, w2_words, w2_scales, gate, emb, 
             nc.vector.tensor_tensor(term, y[b][:].indirect(entries(pos_sb[d], first, count)), gate_sb[d][:, first : first + count], MULT)
 
         halves = [slice(a * V // 2, (a + 1) * V // 2) for a in range(2)]
-        sum_turned = [bank(5 + a, V // 2) for a in range(2)]
+        sum_turned = [bank(1 + a, V // 2) for a in range(2)]
         for d in range(D):
             term = keep.tile([P, V], F32, name="term0_%d" % d)
             weighted(term[:], 0, d, 0)
             for a in range(2):
                 turn(sum_turned[a], term[:, halves[a]], d == 0, d == D - 1)
         raw = []
-        for d in range(2):
+        for d in range(D):
             tile = keep.tile([P, V], F32, name="raw%d" % d)
             nc.scalar.activation(tile[:], y[1][:].indirect(pos_sb[d][:]), COPY)
             raw.append(tile)
         sum_back = []
+        sum_sb = keep.tile([P, V], F32, name="sum_sb", tag="y1")
         for a in range(2):
-            sum_sb = keep.tile([P, V // 2], F32, name="sum_sb%d" % a)
-            nc.scalar.copy(sum_sb[:], sum_turned[a][:])
-            sum_back.append(bank((7, 0)[a], V // 2))
-            turn(sum_back[a], sum_sb, True, True)
+            nc.scalar.copy(sum_sb[:, halves[a]], sum_turned[a][:])
+            sum_back.append(bank(3 + a, V // 2))
+            turn(sum_back[a], sum_sb[:, halves[a]], True, True)
         for a in range(2):
             result0 = keep.tile([P, V // 2], F32, name="result0_%d" % a)
             nc.scalar.copy(result0[:], sum_back[a][:])
             nc.scalar.dma_start(out[0:P, halves[a]], result0[:])
 
         terms = [keep.tile([P, V], F32, name="term1_%d" % d) for d in range(D)]
-        nc.vector.tensor_tensor(terms[0][:], raw[0][:], gate_sb[0][:], MULT)
-        weighted(terms[2][:], 1, 2, 0)
-        nc.vector.tensor_tensor(terms[1][:], raw[1][:], gate_sb[1][:], MULT)
+        for d in range(2):
+            nc.vector.tensor_tensor(terms[d][:], raw[d][:], gate_sb[d][:], MULT)
+        nc.vector.tensor_tensor(terms[2][:], raw[2][:], gate_sb[2][:], MULT)
         pair = keep.tile([P, V], F32, name="pair")
-        nc.vector.tensor_tensor(pair[:], terms[0][:], terms[2][:], ADD)
+        nc.vector.tensor_tensor(pair[:], terms[0][:], terms[1][:], ADD)
         for first, count in ((0, 256), (256, 128), (384, 128)):
             cols = slice(first, first + count)
             result1 = keep.tile([P, count], F32, name="result1_%d" % first)
-            nc.vector.tensor_tensor(result1[:], pair[:, cols], terms[1][:, cols], ADD)
+            nc.vector.tensor_tensor(result1[:], pair[:, cols], terms[2][:, cols], ADD)
             nc.sync.dma_start(out[P : 2 * P, cols], result1[:])

@@ -29,6 +29,7 @@ def tile_picked_devox_none_e_kernel(tc, xT, w1, w2_words, w2_scales, gate, emb, 
     nc = tc.nc
     with ExitStack() as ctx:
         keep = ctx.enter_context(tc.tile_pool(name="keep", bufs=1))
+        turns = ctx.enter_context(tc.tile_pool(name="turns", bufs=1))
         psum = ctx.enter_context(tc.psum_pool(name="psum", bufs=1))
 
         def bank(number, width=BANK):
@@ -56,22 +57,30 @@ def tile_picked_devox_none_e_kernel(tc, xT, w1, w2_words, w2_scales, gate, emb, 
             nc.sync.dma_start(w1_sb[:, 2 * u : 2 * u + 2, :], w1_rows[:, 2 * u : 2 * u + 2, :])
         cell_sb = list_tile("cell_sb", cell)
 
-        emb_rows = emb.rearrange("(p t) r -> t p r", t=PACK)
-        emb_sb = [keep.tile([P, U], F32, name="emb_sb%d" % t) for t in range(PACK)]
-        for t in range(2):
-            nc.sync.dma_start(emb_sb[t][:], emb_rows[t])
+        emb_rows = emb.rearrange("(p t) r -> p t r", t=PACK)
+        emb_sb = {}
+
+        def load_emb(low, high, first, count):
+            tile = keep.tile([P, high - low, count], F32, name="emb%d_%d" % (low, first))
+            nc.sync.dma_start(tile[:], emb_rows[:, low:high, first : first + count])
+            for t in range(low, high):
+                emb_sb[(t, first)] = tile[:, t - low, :]
+
+        load_emb(0, 1, 0, U)
+        load_emb(1, 2, 0, 512)
+        load_emb(2, 4, 0, 256)
+        load_emb(2, 4, 256, 256)
+        load_emb(1, 4, 512, 512)
         w2_codes = keep.tile([P, N], U32, name="w2_codes", align_bytes=64)
         nc.sync.dma_start(w2_codes[:].bitcast(I32), w2_words[0].rearrange("p n t -> p (n t)").bitcast(I32))
         w2_sc = keep.tile([P, N], U8, name="w2_sc", align_bytes=64)
         nc.vector.memset(w2_sc[:].bitcast(I32), 0)
         for q in range(4):
             nc.sync.dma_start(w2_sc[32 * q : 32 * q + 4, :].bitcast(I32), w2_scales[0, 4 * q : 4 * q + 4, :].bitcast(I32))
-        for t in range(2, PACK):
-            nc.sync.dma_start(emb_sb[t][:], emb_rows[t])
-        gate_sb = [keep.tile([P, V], F32, name="gate_sb%d" % d) for d in range(D)]
-        for d in range(D):
-            nc.sync.dma_start(gate_sb[d][:], gate[d])
         pos_sb = [list_tile("pos%d_sb" % d, src) for d, src in enumerate((pos1, pos2, pos3))]
+        gates = keep.tile([P, D, V], F32, name="gates")
+        nc.sync.dma_start(gates[:], gate.rearrange("d p v -> p d v"))
+        gate_sb = [gates[:, d, :] for d in range(D)]
 
         ident = keep.tile([P, P], F32, name="ident")
         make_identity(nc, ident[:])
@@ -114,51 +123,48 @@ def tile_picked_devox_none_e_kernel(tc, xT, w1, w2_words, w2_scales, gate, emb, 
 
         h = [keep.tile([P, S], F32, name="h%d" % t) for t in range(PACK)]
 
-        def product(t, first, count, number):
-            acc = bank(number, count)
-            points = slice(first, first + count)
-            nc.tensor.matmul_mx(out=acc[:], lhsT=w1_mx[t][0].bitcast(FP8X4), lhsT_scale=w1_mx[t][1], rhs=x_codes[:, points].bitcast(FP8X4), rhs_scale=x_sc[:, points], start=True, stop=True)
-            return acc
-
-        def relu_scalar(t, first, count, number):
-            nc.scalar.activation(h[t][:, first : first + count], product(t, first, count, number)[:], RELU)
+        def layer1(t, first, widths, number):
+            acc = bank(number, sum(widths))
+            start = 0
+            for width in widths:
+                points = slice(first + start, first + start + width)
+                nc.tensor.matmul_mx(out=acc[:, start : start + width], lhsT=w1_mx[t][0].bitcast(FP8X4), lhsT_scale=w1_mx[t][1], rhs=x_codes[:, points].bitcast(FP8X4), rhs_scale=x_sc[:, points], start=True, stop=True)
+                start = start + width
+            nc.scalar.activation(h[t][:, first : first + start], acc[:], RELU)
 
         def scatter_scalar(t, first, count):
             nc.scalar.activation(up[t][:].indirect(entries(cell_sb, first, count)), h[t][:, first : first + count], COPY)
 
-        def relu_vector(t, first, count, number):
-            nc.vector.tensor_scalar_max(h[t][:, first : first + count], product(t, first, count, number)[:], 0.0)
-
         def scatter_vector(t, first, count):
             nc.vector.tensor_copy(up[t][:].indirect(entries(cell_sb, first, count)), h[t][:, first : first + count])
 
-        relu_scalar(0, 0, HALF, 0)
-        scatter_vector(0, 0, HALF)
-        relu_scalar(1, 0, HALF, 1)
-        relu_scalar(0, HALF, HALF, 3)
+        layer1(0, 0, [128], 0)
+        scatter_vector(0, 0, 128)
+        layer1(0, 128, [128, 256], 1)
+        scatter_vector(0, 128, 384)
+        layer1(1, 0, [HALF], 2)
+        layer1(1, HALF, [HALF], 3)
         scatter_scalar(1, 0, HALF)
-        relu_vector(1, HALF, HALF, 0)
-        scatter_vector(0, HALF, HALF)
-        relu_scalar(2, 0, S, 5)
+        layer1(3, 0, [S], 5)
+        scatter_vector(3, 0, 128)
+        layer1(2, 0, [S], 6)
         scatter_vector(2, 0, S)
-        relu_scalar(3, 0, HALF, 6)
         scatter_scalar(1, HALF, HALF)
-        relu_scalar(3, HALF, HALF, 7)
-        scatter_scalar(3, 0, HALF)
-        scatter_scalar(3, HALF, HALF)
+        scatter_scalar(3, 128, 384)
 
-        z_planes = keep.tile([P, U // P, PACK, P], BF16, name="z_planes")
+        z_planes = turns.tile([P, U // P, PACK, P], BF16, name="z_planes", offset=0)
 
         def add_emb(engine, t, first, count):
             cols = slice(first, first + count)
-            engine.tensor_tensor(z_planes[:, first // P : (first + count) // P, t, :], up[t][:, cols].rearrange("p (b c) -> p b c", c=P), emb_sb[t][:, cols].rearrange("p (b c) -> p b c", c=P), ADD)
+            engine.tensor_tensor(z_planes[:, first // P : (first + count) // P, t, :], up[t][:, cols].rearrange("p (b c) -> p b c", c=P), emb_sb[(t, first)].rearrange("p (b c) -> p b c", c=P), ADD)
 
         add_emb(nc.gpsimd, 0, 0, U)
-        add_emb(nc.gpsimd, 1, 0, 256)
-        add_emb(nc.vector, 1, 256, 768)
-        add_emb(nc.vector, 2, 0, U)
-        for first, count in ((0, 256), (256, 256), (512, 512)):
-            add_emb(nc.vector, 3, first, count)
+        add_emb(nc.gpsimd, 1, 0, 512)
+        for first in (0, 256):
+            add_emb(nc.vector, 3, first, 256)
+            add_emb(nc.vector, 2, first, 256)
+        for t in range(1, PACK):
+            add_emb(nc.vector, t, 512, 512)
 
         z_grouped = {}
         z_mx = {}
@@ -177,15 +183,16 @@ def tile_picked_devox_none_e_kernel(tc, xT, w1, w2_words, w2_scales, gate, emb, 
 
         weave(nc.scalar.copy, 0, 256)
         weave(nc.scalar.copy, 256, 256)
-        weave(nc.vector.tensor_copy, 512, 256)
+        weave(nc.scalar.copy, 512, 128)
+        weave(nc.scalar.copy, 640, 128)
         quantise_z(0, 256, 0)
-        quantise_z(512, 256, 512)
         weave(nc.vector.tensor_copy, 768, 256)
         quantise_z(256, 256, 256)
-        quantise_z(768, 128, 768)
-        quantise_z(896, 128, 768)
+        quantise_z(768, 256, 768)
+        quantise_z(512, 128, 512)
+        quantise_z(640, 128, 640)
 
-        y = [keep.tile([P, U], F32, name="y%d" % b, tag="y%d" % b) for b in range(N // P)]
+        y = [turns.tile([P, U], F32, name="y%d" % b, offset=4 * U * b) for b in range(N // P)]
 
         def layer2(unload, b, first, count, number):
             acc = bank(number, count)
@@ -197,15 +204,15 @@ def tile_picked_devox_none_e_kernel(tc, xT, w1, w2_words, w2_scales, gate, emb, 
                     nc.tensor.matmul_mx(out=acc[:, start - first : start - first + width], lhsT=w2_codes[:, cols].bitcast(FP8X4), lhsT_scale=w2_sc[:, cols], rhs=codes[:].bitcast(FP8X4), rhs_scale=scales[:], start=True, stop=True)
             unload(y[b][:, first : first + count], acc[:])
 
-        layer2(nc.scalar.copy, 0, 0, 256, 0)
-        layer2(nc.scalar.copy, 1, 0, 256, 1)
-        layer2(nc.scalar.copy, 0, 512, 256, 2)
-        layer2(nc.scalar.copy, 1, 512, 256, 3)
-        layer2(nc.scalar.copy, 0, 256, 256, 4)
-        layer2(nc.scalar.copy, 1, 256, 256, 7)
-        layer2(nc.vector.tensor_copy, 0, 768, 128, 5)
-        layer2(nc.vector.tensor_copy, 0, 896, 128, 6)
+        layer2(nc.scalar.copy, 0, 0, 256, 1)
+        layer2(nc.scalar.copy, 1, 0, 256, 2)
+        layer2(nc.scalar.copy, 0, 256, 256, 3)
+        layer2(nc.scalar.copy, 1, 256, 256, 4)
+        layer2(nc.vector.tensor_copy, 0, 768, 256, 5)
         layer2(nc.scalar.copy, 1, 768, 256, 0)
+        layer2(nc.vector.tensor_copy, 0, 512, 128, 6)
+        layer2(nc.vector.tensor_copy, 0, 640, 128, 7)
+        layer2(nc.scalar.copy, 1, 512, 256, 1)
 
         def turn(dst, src, first, last):
             blocks = src.shape[1] // P
@@ -218,34 +225,40 @@ def tile_picked_devox_none_e_kernel(tc, xT, w1, w2_words, w2_scales, gate, emb, 
             nc.vector.tensor_tensor(term, y[b][:].indirect(entries(pos_sb[d], first, count)), gate_sb[d][:, first : first + count], MULT)
 
         halves = [slice(a * V // 2, (a + 1) * V // 2) for a in range(2)]
-        sum_turned = [bank(1 + a, V // 2) for a in range(2)]
+        sum_turned = [bank(2 + a, V // 2) for a in range(2)]
         for d in range(D):
-            term = keep.tile([P, V], F32, name="term0_%d" % d)
+            term = keep.tile([P, V], F32, name="term0_%d" % d, tag="term0_%d" % d)
             weighted(term[:], 0, d, 0)
             for a in range(2):
                 turn(sum_turned[a], term[:, halves[a]], d == 0, d == D - 1)
-        raw = []
-        for d in range(D):
-            tile = keep.tile([P, V], F32, name="raw%d" % d)
-            nc.scalar.activation(tile[:], y[1][:].indirect(pos_sb[d][:]), COPY)
-            raw.append(tile)
+
+        def fetch(dst, d, first):
+            nc.scalar.activation(dst, y[1][:].indirect(entries(pos_sb[d], first, dst.shape[1])), COPY)
+
+        raw = [keep.tile([P, V], F32, name="raw%d" % d) for d in range(D - 1)]
+        for d in range(D - 1):
+            fetch(raw[d][:], d, 0)
+        last_raw = [keep.tile([P, V // 2], F32, name="last_raw%d" % a, tag=("last_raw", "term0_2")[a]) for a in range(2)]
+        fetch(last_raw[0][:], D - 1, 0)
         sum_back = []
-        sum_sb = keep.tile([P, V], F32, name="sum_sb", tag="y1")
         for a in range(2):
-            nc.scalar.copy(sum_sb[:, halves[a]], sum_turned[a][:])
-            sum_back.append(bank(3 + a, V // 2))
-            turn(sum_back[a], sum_sb[:, halves[a]], True, True)
+            sum_sb = keep.tile([P, V // 2], F32, name="sum_sb%d" % a)
+            nc.scalar.copy(sum_sb[:], sum_turned[a][:])
+            sum_back.append(bank(4 + a, V // 2))
+            turn(sum_back[a], sum_sb, True, True)
+        fetch(last_raw[1][:], D - 1, V // 2)
         for a in range(2):
             result0 = keep.tile([P, V // 2], F32, name="result0_%d" % a)
             nc.scalar.copy(result0[:], sum_back[a][:])
             nc.scalar.dma_start(out[0:P, halves[a]], result0[:])
 
         terms = [keep.tile([P, V], F32, name="term1_%d" % d) for d in range(D)]
-        for d in range(2):
-            nc.vector.tensor_tensor(terms[d][:], raw[d][:], gate_sb[d][:], MULT)
-        nc.vector.tensor_tensor(terms[2][:], raw[2][:], gate_sb[2][:], MULT)
+        for d in range(D - 1):
+            nc.vector.tensor_tensor(terms[d][:], raw[d][:], gate_sb[d], MULT)
+        nc.vector.tensor_tensor(terms[2][:, halves[0]], last_raw[0][:], gate_sb[2][:, halves[0]], MULT)
         pair = keep.tile([P, V], F32, name="pair")
         nc.vector.tensor_tensor(pair[:], terms[0][:], terms[1][:], ADD)
+        nc.vector.tensor_tensor(terms[2][:, halves[1]], last_raw[1][:], gate_sb[2][:, halves[1]], MULT)
         for first, count in ((0, 256), (256, 128), (384, 128)):
             cols = slice(first, first + count)
             result1 = keep.tile([P, count], F32, name="result1_%d" % first)

@@ -67,10 +67,10 @@ def tile_picked_devox_none_e_kernel(tc, xT, w1, w2_words, w2_scales, gate, emb, 
                 emb_sb[(t, first)] = tile[:, t - low, :]
 
         load_emb(0, 1, 0, U)
-        load_emb(1, 2, 0, 512)
+        load_emb(1, 2, 0, 640)
         load_emb(2, 4, 0, 256)
-        load_emb(2, 4, 256, 256)
-        load_emb(1, 4, 512, 512)
+        load_emb(2, 4, 256, 384)
+        load_emb(1, 4, 640, 384)
         w2_codes = keep.tile([P, N], U32, name="w2_codes", align_bytes=64)
         nc.sync.dma_start(w2_codes[:].bitcast(I32), w2_words[0].rearrange("p n t -> p (n t)").bitcast(I32))
         w2_sc = keep.tile([P, N], U8, name="w2_sc", align_bytes=64)
@@ -159,12 +159,12 @@ def tile_picked_devox_none_e_kernel(tc, xT, w1, w2_words, w2_scales, gate, emb, 
             engine.tensor_tensor(z_planes[:, first // P : (first + count) // P, t, :], up[t][:, cols].rearrange("p (b c) -> p b c", c=P), emb_sb[(t, first)].rearrange("p (b c) -> p b c", c=P), ADD)
 
         add_emb(nc.gpsimd, 0, 0, U)
-        add_emb(nc.gpsimd, 1, 0, 512)
-        for first in (0, 256):
-            add_emb(nc.vector, 3, first, 256)
-            add_emb(nc.vector, 2, first, 256)
+        add_emb(nc.gpsimd, 1, 0, 640)
+        for first, count in ((0, 256), (256, 384)):
+            add_emb(nc.vector, 3, first, count)
+            add_emb(nc.vector, 2, first, count)
         for t in range(1, PACK):
-            add_emb(nc.vector, t, 512, 512)
+            add_emb(nc.vector, t, 640, 384)
 
         z_grouped = {}
         z_mx = {}
@@ -186,10 +186,10 @@ def tile_picked_devox_none_e_kernel(tc, xT, w1, w2_words, w2_scales, gate, emb, 
         weave(nc.scalar.copy, 512, 128)
         weave(nc.scalar.copy, 640, 128)
         quantise_z(0, 256, 0)
-        weave(nc.vector.tensor_copy, 768, 256)
         quantise_z(256, 256, 256)
-        quantise_z(768, 256, 768)
+        weave(nc.vector.tensor_copy, 768, 256)
         quantise_z(512, 128, 512)
+        quantise_z(768, 256, 768)
         quantise_z(640, 128, 640)
 
         y = [turns.tile([P, U], F32, name="y%d" % b, offset=4 * U * b) for b in range(N // P)]
@@ -205,14 +205,15 @@ def tile_picked_devox_none_e_kernel(tc, xT, w1, w2_words, w2_scales, gate, emb, 
             unload(y[b][:, first : first + count], acc[:])
 
         layer2(nc.scalar.copy, 0, 0, 256, 1)
-        layer2(nc.scalar.copy, 1, 0, 256, 2)
         layer2(nc.scalar.copy, 0, 256, 256, 3)
+        layer2(nc.scalar.copy, 1, 0, 256, 2)
         layer2(nc.scalar.copy, 1, 256, 256, 4)
-        layer2(nc.vector.tensor_copy, 0, 768, 256, 5)
-        layer2(nc.scalar.copy, 1, 768, 256, 0)
         layer2(nc.vector.tensor_copy, 0, 512, 128, 6)
+        layer2(nc.vector.tensor_copy, 1, 512, 128, 0)
+        layer2(nc.vector.tensor_copy, 0, 768, 256, 5)
         layer2(nc.vector.tensor_copy, 0, 640, 128, 7)
-        layer2(nc.scalar.copy, 1, 512, 256, 1)
+        layer2(nc.scalar.copy, 1, 640, 128, 1)
+        layer2(nc.scalar.copy, 1, 768, 256, 3)
 
         def turn(dst, src, first, last):
             blocks = src.shape[1] // P
@@ -226,27 +227,34 @@ def tile_picked_devox_none_e_kernel(tc, xT, w1, w2_words, w2_scales, gate, emb, 
 
         halves = [slice(a * V // 2, (a + 1) * V // 2) for a in range(2)]
         sum_turned = [bank(2 + a, V // 2) for a in range(2)]
+
+        def fetch(dst, b, d, first):
+            nc.scalar.activation(dst, y[b][:].indirect(entries(pos_sb[d], first, dst.shape[1])), COPY)
+
         for d in range(D):
             term = keep.tile([P, V], F32, name="term0_%d" % d, tag="term0_%d" % d)
-            weighted(term[:], 0, d, 0)
+            if d < D - 1:
+                weighted(term[:], 0, d, 0)
+            else:
+                weighted(term[:, halves[0]], 0, d, 0)
+                raw_half = keep.tile([P, V // 2], F32, name="raw_half")
+                fetch(raw_half[:], 0, d, V // 2)
+                nc.vector.tensor_tensor(term[:, halves[1]], raw_half[:], gate_sb[d][:, halves[1]], MULT)
             for a in range(2):
                 turn(sum_turned[a], term[:, halves[a]], d == 0, d == D - 1)
 
-        def fetch(dst, d, first):
-            nc.scalar.activation(dst, y[1][:].indirect(entries(pos_sb[d], first, dst.shape[1])), COPY)
-
         raw = [keep.tile([P, V], F32, name="raw%d" % d) for d in range(D - 1)]
         for d in range(D - 1):
-            fetch(raw[d][:], d, 0)
+            fetch(raw[d][:], 1, d, 0)
         last_raw = [keep.tile([P, V // 2], F32, name="last_raw%d" % a, tag=("last_raw", "term0_2")[a]) for a in range(2)]
-        fetch(last_raw[0][:], D - 1, 0)
+        fetch(last_raw[0][:], 1, D - 1, 0)
         sum_back = []
         for a in range(2):
             sum_sb = keep.tile([P, V // 2], F32, name="sum_sb%d" % a)
             nc.scalar.copy(sum_sb[:], sum_turned[a][:])
             sum_back.append(bank(4 + a, V // 2))
             turn(sum_back[a], sum_sb, True, True)
-        fetch(last_raw[1][:], D - 1, V // 2)
+        fetch(last_raw[1][:], 1, D - 1, V // 2)
         for a in range(2):
             result0 = keep.tile([P, V // 2], F32, name="result0_%d" % a)
             nc.scalar.copy(result0[:], sum_back[a][:])
@@ -257,7 +265,8 @@ def tile_picked_devox_none_e_kernel(tc, xT, w1, w2_words, w2_scales, gate, emb, 
             nc.vector.tensor_tensor(terms[d][:], raw[d][:], gate_sb[d], MULT)
         nc.vector.tensor_tensor(terms[2][:, halves[0]], last_raw[0][:], gate_sb[2][:, halves[0]], MULT)
         pair = keep.tile([P, V], F32, name="pair")
-        nc.vector.tensor_tensor(pair[:], terms[0][:], terms[1][:], ADD)
+        for a in range(2):
+            nc.vector.tensor_tensor(pair[:, halves[a]], terms[0][:, halves[a]], terms[1][:, halves[a]], ADD)
         nc.vector.tensor_tensor(terms[2][:, halves[1]], last_raw[1][:], gate_sb[2][:, halves[1]], MULT)
         for first, count in ((0, 256), (256, 128), (384, 128)):
             cols = slice(first, first + count)

@@ -115,7 +115,8 @@ def tile_picked_devox_none_e_kernel(tc, xT, w1, w2_words, w2_scales, gate, emb, 
                 w1_mx[first + e] = (codes[:, e * P : (e + 1) * P], scales[:, e * P : (e + 1) * P])
 
         deal(nc.scalar.copy, 0, slice(0, 2))
-        deal(nc.vector.tensor_copy, 0, slice(2, 4))
+        for e in range(2):
+            nc.vector.tensor_copy(w1_grouped[0][:, e, :, 2:4], w1_sb[:, 2:4, :].rearrange("p j (m t) -> p m j t", t=PACK)[:, :, :, e])
         deal(nc.scalar.copy, 1, slice(0, 4))
         quantise_w1(0, 1)
         quantise_w1(1, 1)

@@ -100,7 +100,7 @@ def tile_picked_devox_none_e_kernel(tc, xT, w1, w2_words, w2_scales, gate, emb, 
             points = slice(a * HALF, (a + 1) * HALF)
             nc.vector.quantize_mx(out=x_codes[:, points].bitcast(FP8X4), scales=x_sc[:, points], in_=x_grouped[a][:].rearrange("p c j -> p (c j)"))
 
-        w1_grouped = [keep.tile([P, 2, P, PACK], BF16, name="w1_grouped%d" % g, align_bytes=64) for g in range(2)]
+        w1_grouped = [keep.tile([P, 2, P, PACK], BF16, name="w1_grouped%d" % g, tag="w1_grouped", align_bytes=64) for g in range(2)]
         w1_mx = {}
 
         def deal(copy, g, rows):
@@ -117,10 +117,9 @@ def tile_picked_devox_none_e_kernel(tc, xT, w1, w2_words, w2_scales, gate, emb, 
         deal(nc.scalar.copy, 0, slice(0, 2))
         for e in range(2):
             nc.vector.tensor_copy(w1_grouped[0][:, e, :, 2:4], w1_sb[:, 2:4, :].rearrange("p j (m t) -> p m j t", t=PACK)[:, :, :, e])
-        deal(nc.scalar.copy, 1, slice(0, 4))
         quantise_w1(0, 1)
         quantise_w1(1, 1)
-        quantise_w1(2, 2)
+        deal(nc.vector.tensor_copy, 1, slice(0, 4))
 
         h = [keep.tile([P, S], F32, name="h%d" % t) for t in range(PACK)]
 
@@ -141,6 +140,7 @@ def tile_picked_devox_none_e_kernel(tc, xT, w1, w2_words, w2_scales, gate, emb, 
 
         layer1(0, 0, [128], 0)
         scatter_vector(0, 0, 128)
+        quantise_w1(2, 2)
         layer1(0, 128, [128, 256], 1)
         scatter_vector(0, 128, 384)
         layer1(1, 0, [HALF], 2)

@@ -245,32 +245,44 @@ def tile_picked_devox_none_e_kernel(tc, xT, w1, w2_words, w2_scales, gate, emb, 
                 turn(sum_turned[a], term[:, halves[a]], d == 0, d == D - 1)
 
         raw = [keep.tile([P, V], F32, name="raw%d" % d) for d in range(D - 1)]
-        for d in range(D - 1):
-            fetch(raw[d][:], 1, d, 0)
-        last_raw = [keep.tile([P, V // 2], F32, name="last_raw%d" % a, tag=("last_raw", "term0_2")[a]) for a in range(2)]
-        fetch(last_raw[0][:], 1, D - 1, 0)
+        last_raw = [keep.tile([P, (384, 128)[a]], F32, name="last_raw%d" % a, tag=("last_raw", "term0_2")[a]) for a in range(2)]
+        fetch(raw[0][:], 1, 0, 0)
+        fetch(last_raw[0][:, :256], 1, D - 1, 0)
+        for a in range(2):
+            fetch(raw[1][:, halves[a]], 1, 1, a * V // 2)
+        fetch(last_raw[0][:, 256:], 1, D - 1, 256)
         sum_back = []
         for a in range(2):
             sum_sb = keep.tile([P, V // 2], F32, name="sum_sb%d" % a)
             nc.scalar.copy(sum_sb[:], sum_turned[a][:])
             sum_back.append(bank(4 + a, V // 2))
             turn(sum_back[a], sum_sb, True, True)
-        fetch(last_raw[1][:], 1, D - 1, V // 2)
+        fetch(last_raw[1][:], 1, D - 1, 384)
         for a in range(2):
             result0 = keep.tile([P, V // 2], F32, name="result0_%d" % a)
             nc.scalar.copy(result0[:], sum_back[a][:])
             nc.scalar.dma_start(out[0:P, halves[a]], result0[:])
 
         terms = [keep.tile([P, V], F32, name="term1_%d" % d) for d in range(D)]
-        for d in range(D - 1):
-            nc.vector.tensor_tensor(terms[d][:], raw[d][:], gate_sb[d], MULT)
-        nc.vector.tensor_tensor(terms[2][:, halves[0]], last_raw[0][:], gate_sb[2][:, halves[0]], MULT)
         pair = keep.tile([P, V], F32, name="pair")
-        for a in range(2):
-            nc.vector.tensor_tensor(pair[:, halves[a]], terms[0][:, halves[a]], terms[1][:, halves[a]], ADD)
-        nc.vector.tensor_tensor(terms[2][:, halves[1]], last_raw[1][:], gate_sb[2][:, halves[1]], MULT)
-        for first, count in ((0, 256), (256, 128), (384, 128)):
+
+        def weigh(d, src, cols):
+            nc.vector.tensor_tensor(terms[d][:, cols], src, gate_sb[d][:, cols], MULT)
+
+        def finish(d, first, count):
             cols = slice(first, first + count)
             result1 = keep.tile([P, count], F32, name="result1_%d" % first)
-            nc.vector.tensor_tensor(result1[:], pair[:, cols], terms[2][:, cols], ADD)
+            nc.vector.tensor_tensor(result1[:], pair[:, cols], terms[d][:, cols], ADD)
             nc.sync.dma_start(out[P : 2 * P, cols], result1[:])
+
+        weigh(0, raw[0][:], slice(0, V))
+        weigh(2, last_raw[0][:, :256], halves[0])
+        weigh(1, raw[1][:, halves[0]], halves[0])
+        nc.vector.tensor_tensor(pair[:, halves[0]], terms[0][:, halves[0]], terms[2][:, halves[0]], ADD)
+        weigh(1, raw[1][:, halves[1]], halves[1])
+        finish(1, 0, 256)
+        weigh(2, last_raw[0][:, 256:], slice(256, 384))
+        nc.vector.tensor_tensor(pair[:, halves[1]], terms[0][:, halves[1]], terms[1][:, halves[1]], ADD)
+        weigh(2, last_raw[1][:], slice(384, V))
+        finish(2, 256, 128)
+        finish(2, 384, 128)

@@ -44,13 +44,12 @@ def tile_picked_devox_none_e_kernel(tc, xT, w1, w2_words, w2_scales, gate, emb, 
             return tile[:, first // LIST_COLS : (first + count) // LIST_COLS]
 
         x_rows = xT.rearrange("(p j) t -> j p t", j=PACK)
+        offs_sb = list_tile("offs_sb", offs)
         x_planes = []
         for j in range(PACK):
             plane = keep.tile([P, T], F32, name="x_plane%d" % j)
-            nc.sync.dma_start(plane[:], x_rows[j])
+            (nc.scalar if j == 0 else nc.sync).dma_start(plane[:], x_rows[j])
             x_planes.append(plane)
-            if j == 0:
-                offs_sb = list_tile("offs_sb", offs)
         w1_rows = w1.rearrange("(p j) c -> p j c", j=PACK)
         w1_sb = keep.tile([P, PACK, H], F32, name="w1_sb")
         for u in range(2):

@@ -23,13 +23,13 @@ PACK = 4
 HALF = S // 2
 LIST_COLS = 16
 BANK = 512
+TURNED = 384
 
 
 def tile_picked_devox_none_e_kernel(tc, xT, w1, w2_words, w2_scales, gate, emb, offs, cell, pos1, pos2, pos3, out):
     nc = tc.nc
     with ExitStack() as ctx:
         keep = ctx.enter_context(tc.tile_pool(name="keep", bufs=1))
-        turns = ctx.enter_context(tc.tile_pool(name="turns", bufs=1))
         psum = ctx.enter_context(tc.psum_pool(name="psum", bufs=1))
 
         def bank(number, width=BANK):
@@ -60,23 +60,27 @@ def tile_picked_devox_none_e_kernel(tc, xT, w1, w2_words, w2_scales, gate, emb, 
         emb_sb = {}
 
         def load_emb(low, high, first, count):
-            tile = keep.tile([P, high - low, count], F32, name="emb%d_%d" % (low, first))
+            tile = keep.tile([P, high - low, count], F32, name="emb%d_%d" % (low, first), tag="emb%d_%d" % (low, first), align_bytes=64)
             nc.sync.dma_start(tile[:], emb_rows[:, low:high, first : first + count])
             for t in range(low, high):
                 emb_sb[(t, first)] = tile[:, t - low, :]
 
-        load_emb(0, 1, 0, U)
-        load_emb(1, 2, 0, 640)
-        load_emb(2, 4, 0, 256)
-        load_emb(2, 4, 256, 384)
-        load_emb(1, 4, 640, 384)
+        load_emb(0, 1, TURNED, U - TURNED)
+        load_emb(1, 2, TURNED, U - TURNED)
         w2_codes = keep.tile([P, N], U32, name="w2_codes", align_bytes=64)
         nc.sync.dma_start(w2_codes[:].bitcast(I32), w2_words[0].rearrange("p n t -> p (n t)").bitcast(I32))
         w2_sc = keep.tile([P, N], U8, name="w2_sc", align_bytes=64)
         nc.vector.memset(w2_sc[:].bitcast(I32), 0)
         for q in range(4):
             nc.sync.dma_start(w2_sc[32 * q : 32 * q + 4, :].bitcast(I32), w2_scales[0, 4 * q : 4 * q + 4, :].bitcast(I32))
-        pos_sb = [list_tile("pos%d_sb" % d, src) for d, src in enumerate((pos1, pos2, pos3))]
+            if q == 0:
+                load_emb(0, 4, 0, TURNED)
+        last_list = list_tile("pos2_sb", pos3)
+        load_emb(2, 4, 384, 256)
+        load_emb(2, 3, 640, 384)
+        load_emb(3, 4, 640, 384)
+        pos_sb = [list_tile("pos%d_sb" % d, src) for d, src in enumerate((pos1, pos2))]
+        pos_sb.append(last_list)
         gates = keep.tile([P, D, V], F32, name="gates")
         nc.sync.dma_start(gates[:], gate.rearrange("d p v -> p d v"))
         gate_sb = [gates[:, d, :] for d in range(D)]
@@ -85,7 +89,7 @@ def tile_picked_devox_none_e_kernel(tc, xT, w1, w2_words, w2_scales, gate, emb, 
         make_identity(nc, ident[:])
         up = []
         for t in range(PACK):
-            tile = keep.tile([P, U], F32, name="up%d" % t)
+            tile = keep.tile([P, U], F32, name="up%d" % t, tag="up%d" % t, align_bytes=64)
             (nc.vector if t < 2 else nc.gpsimd).memset(tile[:], 0.0)
             up.append(tile)
 
@@ -152,68 +156,101 @@ def tile_picked_devox_none_e_kernel(tc, xT, w1, w2_words, w2_scales, gate, emb, 
         scatter_scalar(1, HALF, HALF)
         scatter_scalar(3, 128, 384)
 
-        z_planes = turns.tile([P, U // P, PACK, P], BF16, name="z_planes", offset=0)
+        z_planes = keep.tile([P, (U - TURNED) // P, PACK, P], BF16, name="z_planes")
 
-        def add_emb(engine, t, first, count):
-            cols = slice(first, first + count)
-            engine.tensor_tensor(z_planes[:, first // P : (first + count) // P, t, :], up[t][:, cols].rearrange("p (b c) -> p b c", c=P), emb_sb[(t, first)].rearrange("p (b c) -> p b c", c=P), ADD)
+        def planes(first, count):
+            return z_planes[:, (first - TURNED) // P : (first + count - TURNED) // P, :, :]
 
-        add_emb(nc.gpsimd, 0, 0, U)
-        add_emb(nc.gpsimd, 1, 0, 640)
-        for first, count in ((0, 256), (256, 384)):
-            add_emb(nc.vector, 3, first, count)
-            add_emb(nc.vector, 2, first, count)
-        for t in range(1, PACK):
-            add_emb(nc.vector, t, 640, 384)
+        def add_emb(engine, t, first, count, home):
+            rows = emb_sb[(t, home)][:, first - home : first - home + count]
+            engine.tensor_tensor(planes(first, count)[:, :, t, :], up[t][:, first : first + count].rearrange("p (b c) -> p b c", c=P), rows.rearrange("p (b c) -> p b c", c=P), ADD)
+
+        for t in range(2):
+            add_emb(nc.gpsimd, t, TURNED, U - TURNED, TURNED)
+
+        stretches = ((0, 256), (256, 128))
+        turned = {}
+        for u in range(2):
+            for k, (first, count) in enumerate(stretches):
+                turned[(u, first)] = bank(((4, 7), (0, 1))[u][k], 2 * count)
+
+        def turn_sum(src, t, first, count, opens, closes):
+            blocks = count // P
+            for b in range(blocks):
+                dst = turned[(t // 2, first)][:, (2 * b + t % 2) * P : (2 * b + t % 2 + 1) * P]
+                nc.tensor.matmul(dst, src[:, first + b * P : first + (b + 1) * P], ident[:], start=opens and b == 0, stop=closes and b == blocks - 1, is_transpose=True)
+
+        for t in range(PACK):
+            for first, count in stretches:
+                turn_sum(emb_sb[(t, 0)], t, first, count, t % 2 == 0, False)
+        for t in range(PACK):
+            for first, count in stretches:
+                turn_sum(up[t], t, first, count, False, t % 2 == 1)
+
+        back = {first: bank(2 + k, 2 * count) for k, (first, count) in enumerate(stretches)}
+        for u in range(2):
+            for first, count in stretches:
+                pairs = keep.tile([P, count // P, P, 2], BF16, name="z_turned%d_%d" % (u, first))
+                nc.scalar.copy(pairs[:], turned[(u, first)][:].rearrange("c (b e p) -> c b p e", e=2, p=P))
+                words = pairs[:].rearrange("c b p e -> c b (p e)").bitcast(F32)
+                for b in range(count // P):
+                    nc.tensor.transpose(back[first][:, (2 * b + u) * P : (2 * b + u + 1) * P], words[:, b, :], ident[:])
 
         z_grouped = {}
         z_mx = {}
 
-        def weave(copy, first, count):
-            z_grouped[first] = keep.tile([P, count, PACK], BF16, name="z_grouped%d" % first, align_bytes=64)
-            src = z_planes[:, first // P : (first + count) // P, :, :]
-            copy(z_grouped[first][:].rearrange("p (b c i) t -> p b c t i", c=P // 4, i=4), src.rearrange("p b t (c i) -> p b c t i", i=4))
+        def weave(copy, first, count, buffer):
+            z_grouped[first] = keep.tile([P, count, PACK], BF16, name="z_grouped%d" % first, tag=buffer, align_bytes=64)
+            copy(z_grouped[first][:].rearrange("p (b c i) t -> p b c t i", c=P // 4, i=4), planes(first, count).rearrange("p b t (c i) -> p b c t i", i=4))
 
-        def quantise_z(first, count, home):
-            codes = keep.tile([P, count], U32, name="z_codes%d" % first, align_bytes=64)
+        def lay_back(first, count, buffer):
+            z_grouped[first] = keep.tile([P, count, PACK], BF16, name="z_grouped%d" % first, tag=buffer, align_bytes=64)
+            dst = z_grouped[first][:].rearrange("p c t -> p (c t)").bitcast(F32)
+            nc.scalar.copy(dst.rearrange("p (b c u) -> p b c u", c=P, u=2), back[first][:].rearrange("p (b u c) -> p b c u", u=2, c=P))
+
+        for first, count in ((384, 256), (640, 384)):
+            for t in (2, 3):
+                add_emb(nc.vector, t, first, count, first)
+        weave(nc.scalar.copy, 384, 128, "z_grouped384")
+        lay_back(0, 256, "emb2_384")
+        lay_back(256, 128, "emb2_640")
+
+        def quantise_z(first, count, home, buffer):
+            codes = keep.tile([P, count], U32, name="z_codes%d" % first, tag=buffer, align_bytes=64)
             scales = keep.tile([P, count], U8, name="z_sc%d" % first, align_bytes=64)
             src = z_grouped[home][:, first - home : first - home + count, :]
             nc.vector.quantize_mx(out=codes[:].bitcast(FP8X4), scales=scales[:], in_=src.rearrange("p c t -> p (c t)"))
             z_mx[first] = (codes, scales)
 
-        weave(nc.scalar.copy, 0, 256)
-        weave(nc.scalar.copy, 256, 256)
-        weave(nc.scalar.copy, 512, 128)
-        weave(nc.scalar.copy, 640, 128)
-        quantise_z(0, 256, 0)
-        quantise_z(256, 256, 256)
-        weave(nc.vector.tensor_copy, 768, 256)
-        quantise_z(512, 128, 512)
-        quantise_z(768, 256, 768)
-        quantise_z(640, 128, 640)
+        weave(nc.vector.tensor_copy, 512, 128, "z_grouped512")
+        quantise_z(512, 128, 512, "z_codes512")
+        weave(nc.vector.tensor_copy, 640, 256, "z_grouped640")
+        quantise_z(384, 128, 384, "emb3_640")
+        quantise_z(640, 256, 640, "z_codes640")
+        weave(nc.vector.tensor_copy, 896, 128, "z_grouped384")
+        quantise_z(0, 256, 0, "z_grouped640")
+        quantise_z(896, 128, 896, "z_codes896")
+        quantise_z(256, 128, 256, "emb2_384")
 
-        y = [turns.tile([P, U], F32, name="y%d" % b, offset=4 * U * b) for b in range(N // P)]
+        y = [keep.tile([P, U], F32, name="y%d" % b) for b in range(N // P)]
 
         def layer2(unload, b, first, count, number):
             acc = bank(number, count)
             cols = slice(b * P, (b + 1) * P)
-            for start in sorted(z_mx):
+            for start in z_mx:
                 if first <= start < first + count:
                     codes, scales = z_mx[start]
                     width = codes.shape[1]
                     nc.tensor.matmul_mx(out=acc[:, start - first : start - first + width], lhsT=w2_codes[:, cols].bitcast(FP8X4), lhsT_scale=w2_sc[:, cols], rhs=codes[:].bitcast(FP8X4), rhs_scale=scales[:], start=True, stop=True)
             unload(y[b][:, first : first + count], acc[:])
 
-        layer2(nc.scalar.copy, 0, 0, 256, 1)
-        layer2(nc.scalar.copy, 0, 256, 256, 3)
-        layer2(nc.scalar.copy, 1, 0, 256, 2)
-        layer2(nc.scalar.copy, 1, 256, 256, 4)
-        layer2(nc.vector.tensor_copy, 0, 512, 128, 6)
-        layer2(nc.vector.tensor_copy, 1, 512, 128, 0)
-        layer2(nc.vector.tensor_copy, 0, 768, 256, 5)
-        layer2(nc.vector.tensor_copy, 0, 640, 128, 7)
-        layer2(nc.scalar.copy, 1, 640, 128, 1)
-        layer2(nc.scalar.copy, 1, 768, 256, 3)
+        layer2(nc.scalar.copy, 0, 384, 512, 5)
+        layer2(nc.scalar.copy, 1, 384, 512, 6)
+        layer2(nc.vector.tensor_copy, 0, 0, 256, 4)
+        layer2(nc.vector.tensor_copy, 0, 896, 128, 1)
+        layer2(nc.vector.tensor_copy, 0, 256, 128, 0)
+        layer2(nc.scalar.copy, 1, 896, 128, 5)
+        layer2(nc.scalar.copy, 1, 0, 384, 7)
 
         def turn(dst, src, first, last):
             blocks = src.shape[1] // P
@@ -237,7 +274,7 @@ def tile_picked_devox_none_e_kernel(tc, xT, w1, w2_words, w2_scales, gate, emb, 
                 weighted(term[:], 0, d, 0)
             else:
                 weighted(term[:, halves[0]], 0, d, 0)
-                raw_half = keep.tile([P, V // 2], F32, name="raw_half")
+                raw_half = keep.tile([P, V // 2], F32, name="raw_half", tag="emb2_384", align_bytes=64)
                 fetch(raw_half[:], 0, d, V // 2)
                 nc.vector.tensor_tensor(term[:, halves[1]], raw_half[:], gate_sb[d][:, halves[1]], MULT)
             for a in range(2):

@@ -24,6 +24,7 @@ HALF = S // 2
 LIST_COLS = 16
 BANK = 512
 TURNED = 384
+HP = P // 2
 
 
 def tile_picked_devox_none_e_kernel(tc, xT, w1, w2_words, w2_scales, gate, emb, offs, cell, pos1, pos2, pos3, out):
@@ -51,12 +52,15 @@ def tile_picked_devox_none_e_kernel(tc, xT, w1, w2_words, w2_scales, gate, emb, 
             (nc.scalar if j == 0 else nc.sync).dma_start(plane[:], x_rows[j])
             x_planes.append(plane)
         w1_rows = w1.rearrange("(p j) c -> p j c", j=PACK)
-        w1_sb = keep.tile([P, PACK, H], F32, name="w1_sb")
-        for u in range(2):
-            nc.sync.dma_start(w1_sb[:, 2 * u : 2 * u + 2, :], w1_rows[:, 2 * u : 2 * u + 2, :])
+        w1_half = []
+        for g in range(2):
+            tile = keep.tile([P, PACK, H // 2], F32, name="w1_half%d" % g)
+            nc.sync.dma_start(tile[:], w1_rows[:, :, g * H // 2 : (g + 1) * H // 2])
+            w1_half.append(tile)
         cell_sb = list_tile("cell_sb", cell)
 
         emb_rows = emb.rearrange("(p t) r -> p t r", t=PACK)
+        emb_early_rows = emb.rearrange("(g m t) r -> t m g r", g=2, t=PACK)
         emb_sb = {}
 
         def load_emb(low, high, first, count):
@@ -65,32 +69,34 @@ def tile_picked_devox_none_e_kernel(tc, xT, w1, w2_words, w2_scales, gate, emb, 
             for t in range(low, high):
                 emb_sb[(t, first)] = tile[:, t - low, :]
 
-        load_emb(0, 1, TURNED, U - TURNED)
-        load_emb(1, 2, TURNED, U - TURNED)
+        def load_emb_early(first, count):
+            tile = keep.tile([P, 2, count], F32, name="emb_early%d" % first)
+            for e in range(2):
+                nc.sync.dma_start(tile[e * HP : (e + 1) * HP], emb_early_rows[e][:, :, first : first + count])
+            for g in range(2):
+                emb_sb[(g, first)] = tile[:, g, :]
+
+        load_emb_early(TURNED, U - TURNED)
         w2_codes = keep.tile([P, N], U32, name="w2_codes", align_bytes=64)
         nc.sync.dma_start(w2_codes[:].bitcast(I32), w2_words[0].rearrange("p n t -> p (n t)").bitcast(I32))
         w2_sc = keep.tile([P, N], U8, name="w2_sc", align_bytes=64)
         nc.vector.memset(w2_sc[:].bitcast(I32), 0)
+        load_emb_early(0, TURNED)
+        load_emb(2, 4, 0, TURNED)
+        load_emb(2, 4, 384, 256)
+        load_emb(2, 4, 640, 384)
         for q in range(4):
             nc.sync.dma_start(w2_sc[32 * q : 32 * q + 4, :].bitcast(I32), w2_scales[0, 4 * q : 4 * q + 4, :].bitcast(I32))
-            if q == 0:
-                load_emb(0, 4, 0, TURNED)
         last_list = list_tile("pos2_sb", pos3)
-        load_emb(2, 4, 384, 256)
-        load_emb(2, 3, 640, 384)
-        load_emb(3, 4, 640, 384)
         pos_sb = [list_tile("pos%d_sb" % d, src) for d, src in enumerate((pos1, pos2))]
         pos_sb.append(last_list)
-        gates = keep.tile([P, D, V], F32, name="gates")
-        nc.sync.dma_start(gates[:], gate.rearrange("d p v -> p d v"))
-        gate_sb = [gates[:, d, :] for d in range(D)]
 
         ident = keep.tile([P, P], F32, name="ident")
         make_identity(nc, ident[:])
         up = []
-        for t in range(PACK):
+        for t in range(PACK + 1):
             tile = keep.tile([P, U], F32, name="up%d" % t, tag="up%d" % t, align_bytes=64)
-            (nc.vector if t < 2 else nc.gpsimd).memset(tile[:], 0.0)
+            (nc.vector if t in (0, 4) else nc.gpsimd).memset(tile[:], 0.0)
             up.append(tile)
 
         x_grouped = [keep.tile([P, HALF, PACK], BF16, name="x_grouped%d" % a, align_bytes=64) for a in range(2)]
@@ -99,74 +105,107 @@ def tile_picked_devox_none_e_kernel(tc, xT, w1, w2_words, w2_scales, gate, emb, 
         for j in range(PACK):
             for a in range(2):
                 nc.vector.tensor_copy(x_grouped[a][:, :, j], x_planes[j][:].indirect(entries(offs_sb, a * HALF, HALF)))
-        for a in range(2):
+
+        def quantise_x(a):
             points = slice(a * HALF, (a + 1) * HALF)
             nc.vector.quantize_mx(out=x_codes[:, points].bitcast(FP8X4), scales=x_sc[:, points], in_=x_grouped[a][:].rearrange("p c j -> p (c j)"))
 
-        w1_grouped = [keep.tile([P, 2, P, PACK], BF16, name="w1_grouped%d" % g, tag="w1_grouped", align_bytes=64) for g in range(2)]
-        w1_mx = {}
+        w1_codes = [keep.tile([P, P], U32, name="w1_codes%d" % t, align_bytes=64) for t in range(PACK)]
+        w1_sc = [keep.tile([P, P], U8, name="w1_sc%d" % t, align_bytes=64) for t in range(PACK)]
 
-        def deal(copy, g, rows):
-            copy(w1_grouped[g][:, :, :, rows].rearrange("p e m j -> p m j e"), w1_sb[:, rows, :].rearrange("p j (m t) -> p m j t", t=PACK)[:, :, :, 2 * g : 2 * g + 2])
+        def deal(copy, g, u):
+            tile = keep.tile([P, 2, HP, PACK], BF16, name="w1_grouped%d_%d" % (g, u), tag="w1_grouped%d" % u, align_bytes=64)
+            copy(tile[:].rearrange("p e m j -> p m j e"), w1_half[g][:].rearrange("p j (m t) -> p m j t", t=PACK)[:, :, :, 2 * u : 2 * u + 2])
+            return tile
 
-        def quantise_w1(first, count):
-            codes = keep.tile([P, count * P], U32, name="w1_codes%d" % first, align_bytes=64)
-            scales = keep.tile([P, count * P], U8, name="w1_sc%d" % first, align_bytes=64)
-            src = w1_grouped[first // 2][:, first % 2 : first % 2 + count, :, :]
-            nc.vector.quantize_mx(out=codes[:].bitcast(FP8X4), scales=scales[:], in_=src.rearrange("p e m j -> p (e m j)"))
-            for e in range(count):
-                w1_mx[first + e] = (codes[:, e * P : (e + 1) * P], scales[:, e * P : (e + 1) * P])
+        def quantise_early(g, grouped):
+            nc.vector.quantize_mx(out=w1_codes[g][:].bitcast(FP8X4), scales=w1_sc[g][:], in_=grouped[:].rearrange("p e m j -> p (e m j)"))
 
-        deal(nc.scalar.copy, 0, slice(0, 2))
-        for e in range(2):
-            nc.vector.tensor_copy(w1_grouped[0][:, e, :, 2:4], w1_sb[:, 2:4, :].rearrange("p j (m t) -> p m j t", t=PACK)[:, :, :, e])
-        quantise_w1(0, 1)
-        quantise_w1(1, 1)
-        deal(nc.vector.tensor_copy, 1, slice(0, 4))
+        def quantise_late(g, grouped):
+            cols = slice(g * HP, (g + 1) * HP)
+            for e in range(2):
+                nc.vector.quantize_mx(out=w1_codes[2 + e][:, cols].bitcast(FP8X4), scales=w1_sc[2 + e][:, cols], in_=grouped[:, e].rearrange("p m j -> p (m j)"))
 
-        h = [keep.tile([P, S], F32, name="h%d" % t) for t in range(PACK)]
+        quantise_x(0)
+        quantise_early(0, deal(nc.scalar.copy, 0, 0))
+        quantise_x(1)
+        quantise_late(0, deal(nc.scalar.copy, 0, 1))
+        early1 = deal(nc.vector.tensor_copy, 1, 0)
+        late1 = deal(nc.vector.tensor_copy, 1, 1)
 
-        def layer1(t, first, widths, number):
-            acc = bank(number, sum(widths))
+        h = keep.tile([P, PACK * S], F32, name="h")
+
+        def place(t, first):
+            return t * S + ((first + 384) % S if t == 2 else first)
+
+        def layer1(number, *parts):
+            acc = bank(number, sum(count for t, first, count in parts))
             start = 0
-            for width in widths:
-                points = slice(first + start, first + start + width)
-                nc.tensor.matmul_mx(out=acc[:, start : start + width], lhsT=w1_mx[t][0].bitcast(FP8X4), lhsT_scale=w1_mx[t][1], rhs=x_codes[:, points].bitcast(FP8X4), rhs_scale=x_sc[:, points], start=True, stop=True)
-                start = start + width
-            nc.scalar.activation(h[t][:, first : first + start], acc[:], RELU)
+            for t, first, count in parts:
+                points = slice(first, first + count)
+                nc.tensor.matmul_mx(out=acc[:, start : start + count], lhsT=w1_codes[t][:].bitcast(FP8X4), lhsT_scale=w1_sc[t][:], rhs=x_codes[:, points].bitcast(FP8X4), rhs_scale=x_sc[:, points], start=True, stop=True)
+                start = start + count
+            home = place(parts[0][0], parts[0][1])
+            nc.scalar.activation(h[:, home : home + start], acc[:], RELU)
 
-        def scatter_scalar(t, first, count):
-            nc.scalar.activation(up[t][:].indirect(entries(cell_sb, first, count)), h[t][:, first : first + count], COPY)
+        def scatter_scalar(window, t, first, count):
+            nc.scalar.activation(up[window][:].indirect(entries(cell_sb, first, count)), h[:, place(t, first) : place(t, first) + count], COPY)
 
-        def scatter_vector(t, first, count):
-            nc.vector.tensor_copy(up[t][:].indirect(entries(cell_sb, first, count)), h[t][:, first : first + count])
+        def scatter_vector(window, t, first, count):
+            nc.vector.tensor_copy(up[window][:].indirect(entries(cell_sb, first, count)), h[:, place(t, first) : place(t, first) + count])
 
-        layer1(0, 0, [128], 0)
-        scatter_vector(0, 0, 128)
-        quantise_w1(2, 2)
-        layer1(0, 128, [128, 256], 1)
-        scatter_vector(0, 128, 384)
-        layer1(1, 0, [HALF], 2)
-        layer1(1, HALF, [HALF], 3)
-        scatter_scalar(1, 0, HALF)
-        layer1(3, 0, [S], 5)
-        scatter_vector(3, 0, 128)
-        layer1(2, 0, [S], 6)
-        scatter_vector(2, 0, S)
-        scatter_scalar(1, HALF, HALF)
-        scatter_scalar(3, 128, 384)
+        layer1(0, (0, 0, 128))
+        layer1(1, (0, 128, 128))
+        layer1(2, (0, 256, 128))
+        scatter_scalar(4, 0, 0, 128)
+        scatter_vector(0, 0, 128, 128)
+        quantise_early(1, early1)
+        quantise_late(1, late1)
+        scatter_vector(0, 0, 256, 128)
+        layer1(3, (0, 384, 128), (1, 0, 256))
+        layer1(5, (1, 256, 256))
+        scatter_scalar(4, 0, 384, 128)
+        scatter_vector(1, 1, 0, S)
+        layer1(6, (2, 0, 128), (3, 0, 256))
+        layer1(2, (2, 128, 128), (2, 256, 256))
+        scatter_scalar(2, 2, 0, 128)
+        layer1(3, (3, 256, 256))
+        scatter_vector(2, 2, 128, 384)
+        scatter_scalar(3, 3, 0, HALF)
+        scatter_scalar(3, 3, HALF, HALF)
 
-        z_planes = keep.tile([P, (U - TURNED) // P, PACK, P], BF16, name="z_planes")
+        z_planes = {first: keep.tile([P, PACK, count], BF16, name="planes%d" % first, tag="planes%d" % first, align_bytes=64) for first, count in ((384, 256), (640, 384))}
 
         def planes(first, count):
-            return z_planes[:, (first - TURNED) // P : (first + count - TURNED) // P, :, :]
+            home = 384 if first < 640 else 640
+            return z_planes[home][:, :, first - home : first - home + count]
 
         def add_emb(engine, t, first, count, home):
             rows = emb_sb[(t, home)][:, first - home : first - home + count]
-            engine.tensor_tensor(planes(first, count)[:, :, t, :], up[t][:, first : first + count].rearrange("p (b c) -> p b c", c=P), rows.rearrange("p (b c) -> p b c", c=P), ADD)
+            engine.tensor_tensor(planes(first, count)[:, t, :], up[t][:, first : first + count], rows, ADD)
 
-        for t in range(2):
-            add_emb(nc.gpsimd, t, TURNED, U - TURNED, TURNED)
+        both = keep.tile([P, U - TURNED], F32, name="both", tag="z_early1")
+        nc.gpsimd.tensor_tensor(both[:], up[0][:, TURNED:], up[4][:, TURNED:], ADD)
+        z_tiles = [keep.tile([P, U - TURNED], BF16, name="z_early%d" % g, tag="z_early%d" % g) for g in range(2)]
+
+        def add_early(g, first, count):
+            cols = slice(first - TURNED, first - TURNED + count)
+            nc.gpsimd.tensor_tensor(z_tiles[g][:, cols], (both[:], up[1][:, TURNED:])[g][:, cols], emb_sb[(g, TURNED)][:, cols], ADD)
+
+        def put_early(g, first, count):
+            for e in range(2):
+                src = z_tiles[g][e * HP : (e + 1) * HP, first - TURNED : first - TURNED + count]
+                nc.sync.dma_start(planes(first, count)[g * HP : (g + 1) * HP, e, :], src)
+
+        add_early(0, 384, 640)
+        for first, count in ((384, 256), (640, 384)):
+            put_early(0, first, count)
+        for first, count in ((384, 256), (640, 384)):
+            add_early(1, first, count)
+            put_early(1, first, count)
+        gates = keep.tile([P, D, V], F32, name="gates", tag="z_early1")
+        nc.sync.dma_start(gates[:], gate.rearrange("d p v -> p d v"))
+        gate_sb = [gates[:, d, :] for d in range(D)]
 
         stretches = ((0, 256), (256, 128))
         turned = {}
@@ -183,15 +222,21 @@ def tile_picked_devox_none_e_kernel(tc, xT, w1, w2_words, w2_scales, gate, emb, 
         for t in range(PACK):
             for first, count in stretches:
                 turn_sum(emb_sb[(t, 0)], t, first, count, t % 2 == 0, False)
-        for t in range(PACK):
+        for window, t in ((4, 0), (0, 0), (1, 1)):
             for first, count in stretches:
+                turn_sum(up[window], t, first, count, False, t % 2 == 1)
+        for first, count in stretches:
+            for t in (2, 3):
                 turn_sum(up[t], t, first, count, False, t % 2 == 1)
 
         back = {first: bank(2 + k, 2 * count) for k, (first, count) in enumerate(stretches)}
         for u in range(2):
             for first, count in stretches:
                 pairs = keep.tile([P, count // P, P, 2], BF16, name="z_turned%d_%d" % (u, first))
-                nc.scalar.copy(pairs[:], turned[(u, first)][:].rearrange("c (b e p) -> c b p e", e=2, p=P))
+                if u == 0:
+                    nc.scalar.copy(pairs[:].rearrange("c b (g m) e -> c (b g) m e", g=2), turned[(u, first)][:].rearrange("c (b e m) -> c b m e", e=2, m=HP))
+                else:
+                    nc.scalar.copy(pairs[:], turned[(u, first)][:].rearrange("c (b e p) -> c b p e", e=2, p=P))
                 words = pairs[:].rearrange("c b p e -> c b (p e)").bitcast(F32)
                 for b in range(count // P):
                     nc.tensor.transpose(back[first][:, (2 * b + u) * P : (2 * b + u + 1) * P], words[:, b, :], ident[:])
@@ -201,19 +246,20 @@ def tile_picked_devox_none_e_kernel(tc, xT, w1, w2_words, w2_scales, gate, emb, 
 
         def weave(copy, first, count, buffer):
             z_grouped[first] = keep.tile([P, count, PACK], BF16, name="z_grouped%d" % first, tag=buffer, align_bytes=64)
-            copy(z_grouped[first][:].rearrange("p (b c i) t -> p b c t i", c=P // 4, i=4), planes(first, count).rearrange("p b t (c i) -> p b c t i", i=4))
+            copy(z_grouped[first][:].rearrange("p (c i) t -> p c t i", i=4), planes(first, count).rearrange("p t (c i) -> p c t i", i=4))
 
-        def lay_back(first, count, buffer):
-            z_grouped[first] = keep.tile([P, count, PACK], BF16, name="z_grouped%d" % first, tag=buffer, align_bytes=64)
-            dst = z_grouped[first][:].rearrange("p c t -> p (c t)").bitcast(F32)
+        def lay_back(first, count):
+            dst = z_grouped[0][:, first : first + count, :].rearrange("p c t -> p (c t)").bitcast(F32)
             nc.scalar.copy(dst.rearrange("p (b c u) -> p b c u", c=P, u=2), back[first][:].rearrange("p (b u c) -> p b c u", u=2, c=P))
 
         for first, count in ((384, 256), (640, 384)):
             for t in (2, 3):
                 add_emb(nc.vector, t, first, count, first)
         weave(nc.scalar.copy, 384, 128, "z_grouped384")
-        lay_back(0, 256, "emb2_384")
-        lay_back(256, 128, "emb2_640")
+        weave(nc.vector.tensor_copy, 512, 128, "z_grouped512")
+        z_grouped[0] = keep.tile([P, TURNED, PACK], BF16, name="z_grouped0", tag="planes384", align_bytes=64)
+        lay_back(0, 256)
+        lay_back(256, 128)
 
         def quantise_z(first, count, home, buffer):
             codes = keep.tile([P, count], U32, name="z_codes%d" % first, tag=buffer, align_bytes=64)
@@ -222,35 +268,40 @@ def tile_picked_devox_none_e_kernel(tc, xT, w1, w2_words, w2_scales, gate, emb, 
             nc.vector.quantize_mx(out=codes[:].bitcast(FP8X4), scales=scales[:], in_=src.rearrange("p c t -> p (c t)"))
             z_mx[first] = (codes, scales)
 
-        weave(nc.vector.tensor_copy, 512, 128, "z_grouped512")
         quantise_z(512, 128, 512, "z_codes512")
+        quantise_z(384, 128, 384, "z_codes384")
         weave(nc.vector.tensor_copy, 640, 256, "z_grouped640")
-        quantise_z(384, 128, 384, "emb3_640")
+        quantise_z(0, 256, 0, "z_codes0")
         quantise_z(640, 256, 640, "z_codes640")
         weave(nc.vector.tensor_copy, 896, 128, "z_grouped384")
-        quantise_z(0, 256, 0, "z_grouped640")
+        quantise_z(256, 128, 0, "z_grouped640")
         quantise_z(896, 128, 896, "z_codes896")
-        quantise_z(256, 128, 256, "emb2_384")
 
         y = [keep.tile([P, U], F32, name="y%d" % b) for b in range(N // P)]
 
-        def layer2(unload, b, first, count, number):
-            acc = bank(number, count)
+        def layer2(unload, b, number, *pieces):
+            width = sum(z_mx[start][0].shape[1] for start in pieces)
+            acc = bank(number, width)
             cols = slice(b * P, (b + 1) * P)
-            for start in z_mx:
-                if first <= start < first + count:
-                    codes, scales = z_mx[start]
-                    width = codes.shape[1]
-                    nc.tensor.matmul_mx(out=acc[:, start - first : start - first + width], lhsT=w2_codes[:, cols].bitcast(FP8X4), lhsT_scale=w2_sc[:, cols], rhs=codes[:].bitcast(FP8X4), rhs_scale=scales[:], start=True, stop=True)
-            unload(y[b][:, first : first + count], acc[:])
+            done = 0
+            for start in pieces:
+                codes, scales = z_mx[start]
+                count = codes.shape[1]
+                nc.tensor.matmul_mx(out=acc[:, done : done + count], lhsT=w2_codes[:, cols].bitcast(FP8X4), lhsT_scale=w2_sc[:, cols], rhs=codes[:].bitcast(FP8X4), rhs_scale=scales[:], start=True, stop=True)
+                done = done + count
+            if pieces == (256, 896):
+                unload(y[b][:].rearrange("p (a c) -> p a c", c=P)[:, 2:8:5, :], acc[:].rearrange("p (a c) -> p a c", c=P))
+            else:
+                unload(y[b][:, pieces[0] : pieces[0] + width], acc[:])
 
-        layer2(nc.scalar.copy, 0, 384, 512, 5)
-        layer2(nc.scalar.copy, 1, 384, 512, 6)
-        layer2(nc.vector.tensor_copy, 0, 0, 256, 4)
-        layer2(nc.vector.tensor_copy, 0, 896, 128, 1)
-        layer2(nc.vector.tensor_copy, 0, 256, 128, 0)
-        layer2(nc.scalar.copy, 1, 896, 128, 5)
-        layer2(nc.scalar.copy, 1, 0, 384, 7)
+        layer2(nc.scalar.copy, 0, 5, 384, 512)
+        layer2(nc.scalar.copy, 1, 6, 384, 512)
+        layer2(nc.vector.tensor_copy, 0, 4, 0)
+        layer2(nc.scalar.copy, 1, 7, 0)
+        layer2(nc.scalar.copy, 0, 0, 640)
+        layer2(nc.scalar.copy, 1, 1, 640)
+        layer2(nc.vector.tensor_copy, 0, 2, 256, 896)
+        layer2(nc.scalar.copy, 1, 3, 256, 896)
 
         def turn(dst, src, first, last):
             blocks = src.shape[1] // P
@@ -274,7 +325,7 @@ def tile_picked_devox_none_e_kernel(tc, xT, w1, w2_words, w2_scales, gate, emb, 
                 weighted(term[:], 0, d, 0)
             else:
                 weighted(term[:, halves[0]], 0, d, 0)
-                raw_half = keep.tile([P, V // 2], F32, name="raw_half", tag="emb2_384", align_bytes=64)
+                raw_half = keep.tile([P, V // 2], F32, name="raw_half", tag="z_grouped640", align_bytes=64)
                 fetch(raw_half[:], 0, d, V // 2)
                 nc.vector.tensor_tensor(term[:, halves[1]], raw_half[:], gate_sb[d][:, halves[1]], MULT)
             for a in range(2):

@@ -72,7 +72,7 @@ def tile_picked_devox_none_e_kernel(tc, xT, w1, w2_words, w2_scales, gate, emb, 
         def load_emb_early(first, count):
             tile = keep.tile([P, 2, count], F32, name="emb_early%d" % first)
             for e in range(2):
-                nc.sync.dma_start(tile[e * HP : (e + 1) * HP], emb_early_rows[e][:, :, first : first + count])
+                nc.sync.dma_start(tile[e:P:2], emb_early_rows[e][:, :, first : first + count])
             for g in range(2):
                 emb_sb[(g, first)] = tile[:, g, :]
 
@@ -114,17 +114,17 @@ def tile_picked_devox_none_e_kernel(tc, xT, w1, w2_words, w2_scales, gate, emb, 
         w1_sc = [keep.tile([P, P], U8, name="w1_sc%d" % t, align_bytes=64) for t in range(PACK)]
 
         def deal(copy, g, u):
-            tile = keep.tile([P, 2, HP, PACK], BF16, name="w1_grouped%d_%d" % (g, u), tag="w1_grouped%d" % u, align_bytes=64)
-            copy(tile[:].rearrange("p e m j -> p m j e"), w1_half[g][:].rearrange("p j (m t) -> p m j t", t=PACK)[:, :, :, 2 * u : 2 * u + 2])
+            tile = keep.tile([P, P, PACK], BF16, name="w1_grouped%d_%d" % (g, u), tag="w1_grouped%d" % u, align_bytes=64)
+            copy(tile[:].rearrange(("p (m e) j -> p m j e", "p (e m) j -> p m j e")[u], e=2), w1_half[g][:].rearrange("p j (m t) -> p m j t", t=PACK)[:, :, :, 2 * u : 2 * u + 2])
             return tile
 
         def quantise_early(g, grouped):
-            nc.vector.quantize_mx(out=w1_codes[g][:].bitcast(FP8X4), scales=w1_sc[g][:], in_=grouped[:].rearrange("p e m j -> p (e m j)"))
+            nc.vector.quantize_mx(out=w1_codes[g][:].bitcast(FP8X4), scales=w1_sc[g][:], in_=grouped[:].rearrange("p c j -> p (c j)"))
 
         def quantise_late(g, grouped):
             cols = slice(g * HP, (g + 1) * HP)
             for e in range(2):
-                nc.vector.quantize_mx(out=w1_codes[2 + e][:, cols].bitcast(FP8X4), scales=w1_sc[2 + e][:, cols], in_=grouped[:, e].rearrange("p m j -> p (m j)"))
+                nc.vector.quantize_mx(out=w1_codes[2 + e][:, cols].bitcast(FP8X4), scales=w1_sc[2 + e][:, cols], in_=grouped[:, e * HP : (e + 1) * HP, :].rearrange("p m j -> p (m j)"))
 
         quantise_x(0)
         quantise_early(0, deal(nc.scalar.copy, 0, 0))
@@ -194,7 +194,7 @@ def tile_picked_devox_none_e_kernel(tc, xT, w1, w2_words, w2_scales, gate, emb, 
 
         def put_early(g, first, count):
             for e in range(2):
-                src = z_tiles[g][e * HP : (e + 1) * HP, first - TURNED : first - TURNED + count]
+                src = z_tiles[g][e:P:2, first - TURNED : first - TURNED + count]
                 nc.sync.dma_start(planes(first, count)[g * HP : (g + 1) * HP, e, :], src)
 
         add_early(0, 384, 640)
@@ -234,7 +234,7 @@ def tile_picked_devox_none_e_kernel(tc, xT, w1, w2_words, w2_scales, gate, emb, 
             for first, count in stretches:
                 pairs = keep.tile([P, count // P, P, 2], BF16, name="z_turned%d_%d" % (u, first))
                 if u == 0:
-                    nc.scalar.copy(pairs[:].rearrange("c b (g m) e -> c (b g) m e", g=2), turned[(u, first)][:].rearrange("c (b e m) -> c b m e", e=2, m=HP))
+                    nc.scalar.copy(pairs[:].rearrange("c b p e -> c (b p e)"), turned[(u, first)][:])
                 else:
                     nc.scalar.copy(pairs[:], turned[(u, first)][:].rearrange("c (b e p) -> c b p e", e=2, p=P))
                 words = pairs[:].rearrange("c b p e -> c b (p e)").bitcast(F32)
@@ -268,14 +268,14 @@ def tile_picked_devox_none_e_kernel(tc, xT, w1, w2_words, w2_scales, gate, emb, 
             nc.vector.quantize_mx(out=codes[:].bitcast(FP8X4), scales=scales[:], in_=src.rearrange("p c t -> p (c t)"))
             z_mx[first] = (codes, scales)
 
+        weave(nc.vector.tensor_copy, 640, 256, "z_grouped640")
         quantise_z(512, 128, 512, "z_codes512")
         quantise_z(384, 128, 384, "z_codes384")
-        weave(nc.vector.tensor_copy, 640, 256, "z_grouped640")
-        quantise_z(0, 256, 0, "z_codes0")
         quantise_z(640, 256, 640, "z_codes640")
         weave(nc.vector.tensor_copy, 896, 128, "z_grouped384")
-        quantise_z(256, 128, 0, "z_grouped640")
+        quantise_z(0, 256, 0, "z_codes0")
         quantise_z(896, 128, 896, "z_codes896")
+        quantise_z(256, 128, 0, "z_grouped640")
 
         y = [keep.tile([P, U], F32, name="y%d" % b) for b in range(N // P)]
 
@@ -296,10 +296,10 @@ def tile_picked_devox_none_e_kernel(tc, xT, w1, w2_words, w2_scales, gate, emb, 
 
         layer2(nc.scalar.copy, 0, 5, 384, 512)
         layer2(nc.scalar.copy, 1, 6, 384, 512)
-        layer2(nc.vector.tensor_copy, 0, 4, 0)
-        layer2(nc.scalar.copy, 1, 7, 0)
         layer2(nc.scalar.copy, 0, 0, 640)
         layer2(nc.scalar.copy, 1, 1, 640)
+        layer2(nc.vector.tensor_copy, 0, 4, 0)
+        layer2(nc.scalar.copy, 1, 7, 0)
         layer2(nc.vector.tensor_copy, 0, 2, 256, 896)
         layer2(nc.scalar.copy, 1, 3, 256, 896)
 

@@ -90,6 +90,9 @@ def tile_picked_devox_none_e_kernel(tc, xT, w1, w2_words, w2_scales, gate, emb, 
         last_list = list_tile("pos2_sb", pos3)
         pos_sb = [list_tile("pos%d_sb" % d, src) for d, src in enumerate((pos1, pos2))]
         pos_sb.append(last_list)
+        gates = keep.tile([P, D, V], F32, name="gates")
+        nc.sync.dma_start(gates[:], gate.rearrange("d p v -> p d v"))
+        gate_sb = [gates[:, d, :] for d in range(D)]
 
         ident = keep.tile([P, P], F32, name="ident")
         make_identity(nc, ident[:])
@@ -203,9 +206,6 @@ def tile_picked_devox_none_e_kernel(tc, xT, w1, w2_words, w2_scales, gate, emb, 
         for first, count in ((384, 256), (640, 384)):
             add_early(1, first, count)
             put_early(1, first, count)
-        gates = keep.tile([P, D, V], F32, name="gates", tag="z_early1")
-        nc.sync.dma_start(gates[:], gate.rearrange("d p v -> p d v"))
-        gate_sb = [gates[:, d, :] for d in range(D)]
 
         stretches = ((0, 256), (256, 128))
         turned = {}

@@ -84,7 +84,7 @@ def tile_picked_devox_none_e_kernel(tc, xT, w1, w2_words, w2_scales, gate, emb, 
         load_emb_early(0, TURNED)
         load_emb(2, 4, 0, TURNED)
         load_emb(2, 4, 384, 256)
-        load_emb(2, 4, 640, 384)
+        load_emb(2, 3, 640, 384)
         for q in range(4):
             nc.sync.dma_start(w2_sc[32 * q : 32 * q + 4, :].bitcast(I32), w2_scales[0, 4 * q : 4 * q + 4, :].bitcast(I32))
         last_list = list_tile("pos2_sb", pos3)
@@ -187,9 +187,9 @@ def tile_picked_devox_none_e_kernel(tc, xT, w1, w2_words, w2_scales, gate, emb, 
             rows = emb_sb[(t, home)][:, first - home : first - home + count]
             engine.tensor_tensor(planes(first, count)[:, t, :], up[t][:, first : first + count], rows, ADD)
 
-        both = keep.tile([P, U - TURNED], F32, name="both", tag="z_early1")
+        both = keep.tile([P, U - TURNED], F32, name="both", tag="z_early1", align_bytes=64)
         nc.gpsimd.tensor_tensor(both[:], up[0][:, TURNED:], up[4][:, TURNED:], ADD)
-        z_tiles = [keep.tile([P, U - TURNED], BF16, name="z_early%d" % g, tag="z_early%d" % g) for g in range(2)]
+        z_tiles = [keep.tile([P, U - TURNED], BF16, name="z_early%d" % g, tag="z_early%d" % g, align_bytes=64) for g in range(2)]
 
         def add_early(g, first, count):
             cols = slice(first - TURNED, first - TURNED + count)
@@ -203,9 +203,11 @@ def tile_picked_devox_none_e_kernel(tc, xT, w1, w2_words, w2_scales, gate, emb, 
         add_early(0, 384, 640)
         for first, count in ((384, 256), (640, 384)):
             put_early(0, first, count)
-        for first, count in ((384, 256), (640, 384)):
-            add_early(1, first, count)
-            put_early(1, first, count)
+        add_early(1, 384, 256)
+        put_early(1, 384, 256)
+        load_emb(3, 4, 640, 384)
+        add_early(1, 640, 384)
+        put_early(1, 640, 384)
 
         stretches = ((0, 256), (256, 128))
         turned = {}
@@ -252,12 +254,13 @@ def tile_picked_devox_none_e_kernel(tc, xT, w1, w2_words, w2_scales, gate, emb, 
             dst = z_grouped[0][:, first : first + count, :].rearrange("p c t -> p (c t)").bitcast(F32)
             nc.scalar.copy(dst.rearrange("p (b c u) -> p b c u", c=P, u=2), back[first][:].rearrange("p (b u c) -> p b c u", u=2, c=P))
 
-        for first, count in ((384, 256), (640, 384)):
-            for t in (2, 3):
-                add_emb(nc.vector, t, first, count, first)
-        weave(nc.scalar.copy, 384, 128, "z_grouped384")
-        weave(nc.vector.tensor_copy, 512, 128, "z_grouped512")
-        z_grouped[0] = keep.tile([P, TURNED, PACK], BF16, name="z_grouped0", tag="planes384", align_bytes=64)
+        for t in (2, 3):
+            add_emb(nc.vector, t, 384, 256, 384)
+        add_emb(nc.vector, 2, 640, 384, 640)
+        weave(nc.vector.tensor_copy, 384, 256, "z_grouped384")
+        add_emb(nc.vector, 3, 640, 384, 640)
+        weave(nc.scalar.copy, 896, 128, "z_grouped896")
+        z_grouped[0] = keep.tile([P, TURNED, PACK], BF16, name="z_grouped0", tag="z_early1", align_bytes=64)
         lay_back(0, 256)
         lay_back(256, 128)
 
@@ -268,16 +271,14 @@ def tile_picked_devox_none_e_kernel(tc, xT, w1, w2_words, w2_scales, gate, emb, 
             nc.vector.quantize_mx(out=codes[:].bitcast(FP8X4), scales=scales[:], in_=src.rearrange("p c t -> p (c t)"))
             z_mx[first] = (codes, scales)
 
+        quantise_z(384, 256, 384, "z_codes384")
         weave(nc.vector.tensor_copy, 640, 256, "z_grouped640")
-        quantise_z(512, 128, 512, "z_codes512")
-        quantise_z(384, 128, 384, "z_codes384")
-        quantise_z(640, 256, 640, "z_codes640")
-        weave(nc.vector.tensor_copy, 896, 128, "z_grouped384")
-        quantise_z(0, 256, 0, "z_codes0")
         quantise_z(896, 128, 896, "z_codes896")
+        quantise_z(640, 256, 640, "z_codes640")
+        quantise_z(0, 256, 0, "z_codes0")
         quantise_z(256, 128, 0, "z_grouped640")
 
-        y = [keep.tile([P, U], F32, name="y%d" % b) for b in range(N // P)]
+        y = [keep.tile([P, U], F32, name="y%d" % b, tag=("planes640", "z_grouped896")[b], align_bytes=64) for b in range(N // P)]
 
         def layer2(unload, b, number, *pieces):
             width = sum(z_mx[start][0].shape[1] for start in pieces)
@@ -289,19 +290,16 @@ def tile_picked_devox_none_e_kernel(tc, xT, w1, w2_words, w2_scales, gate, emb, 
                 count = codes.shape[1]
                 nc.tensor.matmul_mx(out=acc[:, done : done + count], lhsT=w2_codes[:, cols].bitcast(FP8X4), lhsT_scale=w2_sc[:, cols], rhs=codes[:].bitcast(FP8X4), rhs_scale=scales[:], start=True, stop=True)
                 done = done + count
-            if pieces == (256, 896):
-                unload(y[b][:].rearrange("p (a c) -> p a c", c=P)[:, 2:8:5, :], acc[:].rearrange("p (a c) -> p a c", c=P))
-            else:
-                unload(y[b][:, pieces[0] : pieces[0] + width], acc[:])
+            unload(y[b][:, min(pieces) : min(pieces) + width], acc[:])
 
-        layer2(nc.scalar.copy, 0, 5, 384, 512)
-        layer2(nc.scalar.copy, 1, 6, 384, 512)
-        layer2(nc.scalar.copy, 0, 0, 640)
-        layer2(nc.scalar.copy, 1, 1, 640)
+        layer2(nc.scalar.copy, 0, 5, 384)
+        layer2(nc.scalar.copy, 1, 6, 384)
+        layer2(nc.scalar.copy, 0, 0, 640, 896)
+        layer2(nc.scalar.copy, 1, 1, 640, 896)
         layer2(nc.vector.tensor_copy, 0, 4, 0)
         layer2(nc.scalar.copy, 1, 7, 0)
-        layer2(nc.vector.tensor_copy, 0, 2, 256, 896)
-        layer2(nc.scalar.copy, 1, 3, 256, 896)
+        layer2(nc.vector.tensor_copy, 0, 2, 256)
+        layer2(nc.vector.tensor_copy, 1, 3, 256)
 
         def turn(dst, src, first, last):
             blocks = src.shape[1] // P

@@ -55,7 +55,8 @@ def tile_picked_devox_none_e_kernel(tc, xT, w1, w2_words, w2_scales, gate, emb, 
         w1_half = []
         for g in range(2):
             tile = keep.tile([P, PACK, H // 2], F32, name="w1_half%d" % g)
-            nc.sync.dma_start(tile[:], w1_rows[:, :, g * H // 2 : (g + 1) * H // 2])
+            for u in range(2):
+                nc.sync.dma_start(tile[:, 2 * u : 2 * u + 2, :], w1_rows[:, 2 * u : 2 * u + 2, g * H // 2 : (g + 1) * H // 2])
             w1_half.append(tile)
         cell_sb = list_tile("cell_sb", cell)
 
@@ -99,7 +100,10 @@ def tile_picked_devox_none_e_kernel(tc, xT, w1, w2_words, w2_scales, gate, emb, 
         up = []
         for t in range(PACK + 1):
             tile = keep.tile([P, U], F32, name="up%d" % t, tag="up%d" % t, align_bytes=64)
-            (nc.vector if t in (0, 4) else nc.gpsimd).memset(tile[:], 0.0)
+            if t < PACK:
+                (nc.vector if t < 2 else nc.gpsimd).memset(tile[:], 0.0)
+            else:
+                nc.scalar.copy(tile[:], up[0][:])
             up.append(tile)
 
         x_grouped = [keep.tile([P, HALF, PACK], BF16, name="x_grouped%d" % a, align_bytes=64) for a in range(2)]

@@ -71,29 +71,26 @@ def tile_picked_devox_none_e_kernel(tc, xT, w1, w2_words, w2_scales, gate, emb, 
                 emb_sb[(t, first)] = tile[:, t - low, :]
 
         def load_emb_early(first, count):
-            tile = keep.tile([P, 2, count], F32, name="emb_early%d" % first)
+            tile = keep.tile([P, 2, count], F32, name="emb_early%d" % first, tag="emb_early%d" % first)
             for e in range(2):
                 nc.sync.dma_start(tile[e:P:2], emb_early_rows[e][:, :, first : first + count])
             for g in range(2):
                 emb_sb[(g, first)] = tile[:, g, :]
 
         load_emb_early(TURNED, U - TURNED)
-        w2_codes = keep.tile([P, N], U32, name="w2_codes", align_bytes=64)
-        nc.sync.dma_start(w2_codes[:].bitcast(I32), w2_words[0].rearrange("p n t -> p (n t)").bitcast(I32))
-        w2_sc = keep.tile([P, N], U8, name="w2_sc", align_bytes=64)
-        nc.vector.memset(w2_sc[:].bitcast(I32), 0)
         load_emb_early(0, TURNED)
         load_emb(2, 4, 0, TURNED)
         load_emb(2, 4, 384, 256)
         load_emb(2, 3, 640, 384)
+        w2_codes = keep.tile([P, N], U32, name="w2_codes", align_bytes=64)
+        nc.sync.dma_start(w2_codes[:].bitcast(I32), w2_words[0].rearrange("p n t -> p (n t)").bitcast(I32))
+        w2_sc = keep.tile([P, N], U8, name="w2_sc", align_bytes=64)
+        nc.vector.memset(w2_sc[:].bitcast(I32), 0)
         for q in range(4):
             nc.sync.dma_start(w2_sc[32 * q : 32 * q + 4, :].bitcast(I32), w2_scales[0, 4 * q : 4 * q + 4, :].bitcast(I32))
         last_list = list_tile("pos2_sb", pos3)
         pos_sb = [list_tile("pos%d_sb" % d, src) for d, src in enumerate((pos1, pos2))]
         pos_sb.append(last_list)
-        gates = keep.tile([P, D, V], F32, name="gates")
-        nc.sync.dma_start(gates[:], gate.rearrange("d p v -> p d v"))
-        gate_sb = [gates[:, d, :] for d in range(D)]
 
         ident = keep.tile([P, P], F32, name="ident")
         make_identity(nc, ident[:])
@@ -212,6 +209,9 @@ def tile_picked_devox_none_e_kernel(tc, xT, w1, w2_words, w2_scales, gate, emb, 
         load_emb(3, 4, 640, 384)
         add_early(1, 640, 384)
         put_early(1, 640, 384)
+        gates = keep.tile([P, D, V], F32, name="gates", tag="emb_early384")
+        nc.sync.dma_start(gates[:], gate.rearrange("d p v -> p d v"))
+        gate_sb = [gates[:, d, :] for d in range(D)]
 
         stretches = ((0, 256), (256, 128))
         turned = {}

from contextlib import ExitStack

import concourse.mybir as mybir
from concourse.masks import make_identity

K, T, S, D, V, H, N, U = 512, 2048, 512, 3, 512, 512, 256, 1024
FLOPS = 2 * K * H * S + 2 * H * N * U

F32 = mybir.dt.float32
BF16 = mybir.dt.bfloat16
I32 = mybir.dt.int32
U32 = mybir.dt.uint32
U16 = mybir.dt.uint16
U8 = mybir.dt.uint8
FP8X4 = mybir.dt.float8_e4m3fn_x4
ADD = mybir.AluOpType.add
MULT = mybir.AluOpType.mult
RELU = mybir.ActivationFunctionType.Relu
COPY = mybir.ActivationFunctionType.Copy

P = 128
PACK = 4
HALF = S // 2
LIST_COLS = 16
BANK = 512
TURNED = 384
HP = P // 2


def tile_picked_devox_none_e_kernel(tc, xT, w1, w2_words, w2_scales, gate, emb, offs, cell, pos1, pos2, pos3, out):
    nc = tc.nc
    with ExitStack() as ctx:
        keep = ctx.enter_context(tc.tile_pool(name="keep", bufs=1))
        psum = ctx.enter_context(tc.psum_pool(name="psum", bufs=1))

        def bank(number, width=BANK):
            return psum.tile([P, width], F32, name="bank%d" % number)

        def list_tile(name, src):
            tile = keep.tile([P, S // LIST_COLS], U16, name=name)
            nc.sync.dma_start(tile[:], src)
            return tile

        def entries(tile, first, count):
            return tile[:, first // LIST_COLS : (first + count) // LIST_COLS]

        x_rows = xT.rearrange("(p j) t -> j p t", j=PACK)
        offs_sb = list_tile("offs_sb", offs)
        x_planes = []
        for j in range(PACK):
            plane = keep.tile([P, T], F32, name="x_plane%d" % j)
            (nc.scalar if j == 0 else nc.sync).dma_start(plane[:], x_rows[j])
            x_planes.append(plane)
        w1_rows = w1.rearrange("(p j) c -> p j c", j=PACK)
        w1_half = []
        for g in range(2):
            tile = keep.tile([P, PACK, H // 2], F32, name="w1_half%d" % g)
            for u in range(2):
                nc.sync.dma_start(tile[:, 2 * u : 2 * u + 2, :], w1_rows[:, 2 * u : 2 * u + 2, g * H // 2 : (g + 1) * H // 2])
            w1_half.append(tile)
        cell_sb = list_tile("cell_sb", cell)

        emb_rows = emb.rearrange("(p t) r -> p t r", t=PACK)
        emb_early_rows = emb.rearrange("(g m t) r -> t m g r", g=2, t=PACK)
        emb_sb = {}

        def load_emb(low, high, first, count):
            tile = keep.tile([P, high - low, count], F32, name="emb%d_%d" % (low, first), tag="emb%d_%d" % (low, first), align_bytes=64)
            nc.sync.dma_start(tile[:], emb_rows[:, low:high, first : first + count])
            for t in range(low, high):
                emb_sb[(t, first)] = tile[:, t - low, :]

        def load_emb_early(first, count):
            tile = keep.tile([P, 2, count], F32, name="emb_early%d" % first, tag="emb_early%d" % first)
            for e in range(2):
                nc.sync.dma_start(tile[e:P:2], emb_early_rows[e][:, :, first : first + count])
            for g in range(2):
                emb_sb[(g, first)] = tile[:, g, :]

        load_emb_early(TURNED, U - TURNED)
        load_emb_early(0, TURNED)
        load_emb(2, 4, 0, TURNED)
        load_emb(2, 4, 384, 256)
        load_emb(2, 3, 640, 384)
        w2_codes = keep.tile([P, N], U32, name="w2_codes", align_bytes=64)
        nc.sync.dma_start(w2_codes[:].bitcast(I32), w2_words[0].rearrange("p n t -> p (n t)").bitcast(I32))
        w2_sc = keep.tile([P, N], U8, name="w2_sc", align_bytes=64)
        nc.vector.memset(w2_sc[:].bitcast(I32), 0)
        for q in range(4):
            nc.sync.dma_start(w2_sc[32 * q : 32 * q + 4, :].bitcast(I32), w2_scales[0, 4 * q : 4 * q + 4, :].bitcast(I32))
        last_list = list_tile("pos2_sb", pos3)
        pos_sb = [list_tile("pos%d_sb" % d, src) for d, src in enumerate((pos1, pos2))]
        pos_sb.append(last_list)

        ident = keep.tile([P, P], F32, name="ident")
        make_identity(nc, ident[:])
        up = []
        for t in range(PACK + 1):
            tile = keep.tile([P, U], F32, name="up%d" % t, tag="up%d" % t, align_bytes=64)
            if t < PACK:
                (nc.vector if t < 2 else nc.gpsimd).memset(tile[:], 0.0)
            else:
                nc.scalar.copy(tile[:], up[0][:])
            up.append(tile)

        x_grouped = [keep.tile([P, HALF, PACK], BF16, name="x_grouped%d" % a, align_bytes=64) for a in range(2)]
        x_codes = keep.tile([P, S], U32, name="x_codes", align_bytes=64)
        x_sc = keep.tile([P, S], U8, name="x_sc", align_bytes=64)
        for j in range(PACK):
            for a in range(2):
                nc.vector.tensor_copy(x_grouped[a][:, :, j], x_planes[j][:].indirect(entries(offs_sb, a * HALF, HALF)))

        def quantise_x(a):
            points = slice(a * HALF, (a + 1) * HALF)
            nc.vector.quantize_mx(out=x_codes[:, points].bitcast(FP8X4), scales=x_sc[:, points], in_=x_grouped[a][:].rearrange("p c j -> p (c j)"))

        w1_codes = [keep.tile([P, P], U32, name="w1_codes%d" % t, align_bytes=64) for t in range(PACK)]
        w1_sc = [keep.tile([P, P], U8, name="w1_sc%d" % t, align_bytes=64) for t in range(PACK)]

        def deal(copy, g, u):
            tile = keep.tile([P, P, PACK], BF16, name="w1_grouped%d_%d" % (g, u), tag="w1_grouped%d" % u, align_bytes=64)
            copy(tile[:].rearrange(("p (m e) j -> p m j e", "p (e m) j -> p m j e")[u], e=2), w1_half[g][:].rearrange("p j (m t) -> p m j t", t=PACK)[:, :, :, 2 * u : 2 * u + 2])
            return tile

        def quantise_early(g, grouped):
            nc.vector.quantize_mx(out=w1_codes[g][:].bitcast(FP8X4), scales=w1_sc[g][:], in_=grouped[:].rearrange("p c j -> p (c j)"))

        def quantise_late(g, grouped):
            cols = slice(g * HP, (g + 1) * HP)
            for e in range(2):
                nc.vector.quantize_mx(out=w1_codes[2 + e][:, cols].bitcast(FP8X4), scales=w1_sc[2 + e][:, cols], in_=grouped[:, e * HP : (e + 1) * HP, :].rearrange("p m j -> p (m j)"))

        quantise_x(0)
        quantise_early(0, deal(nc.scalar.copy, 0, 0))
        quantise_x(1)
        quantise_late(0, deal(nc.scalar.copy, 0, 1))
        early1 = deal(nc.vector.tensor_copy, 1, 0)
        late1 = deal(nc.vector.tensor_copy, 1, 1)

        h = keep.tile([P, PACK * S], F32, name="h")

        def place(t, first):
            return t * S + ((first + 384) % S if t == 2 else first)

        def layer1(number, *parts):
            acc = bank(number, sum(count for t, first, count in parts))
            start = 0
            for t, first, count in parts:
                points = slice(first, first + count)
                nc.tensor.matmul_mx(out=acc[:, start : start + count], lhsT=w1_codes[t][:].bitcast(FP8X4), lhsT_scale=w1_sc[t][:], rhs=x_codes[:, points].bitcast(FP8X4), rhs_scale=x_sc[:, points], start=True, stop=True)
                start = start + count
            home = place(parts[0][0], parts[0][1])
            nc.scalar.activation(h[:, home : home + start], acc[:], RELU)

        def scatter_scalar(window, t, first, count):
            nc.scalar.activation(up[window][:].indirect(entries(cell_sb, first, count)), h[:, place(t, first) : place(t, first) + count], COPY)

        def scatter_vector(window, t, first, count):
            nc.vector.tensor_copy(up[window][:].indirect(entries(cell_sb, first, count)), h[:, place(t, first) : place(t, first) + count])

        layer1(0, (0, 0, 128))
        layer1(1, (0, 128, 128))
        layer1(2, (0, 256, 128))
        scatter_scalar(4, 0, 0, 128)
        scatter_vector(0, 0, 128, 128)
        quantise_early(1, early1)
        quantise_late(1, late1)
        scatter_vector(0, 0, 256, 128)
        layer1(3, (0, 384, 128), (1, 0, 256))
        layer1(5, (1, 256, 256))
        scatter_scalar(4, 0, 384, 128)
        scatter_vector(1, 1, 0, S)
        layer1(6, (2, 0, 128), (3, 0, 256))
        layer1(2, (2, 128, 128), (2, 256, 256))
        scatter_scalar(2, 2, 0, 128)
        layer1(3, (3, 256, 256))
        scatter_vector(2, 2, 128, 384)
        scatter_scalar(3, 3, 0, HALF)
        scatter_scalar(3, 3, HALF, HALF)

        z_planes = {first: keep.tile([P, PACK, count], BF16, name="planes%d" % first, tag="planes%d" % first, align_bytes=64) for first, count in ((384, 256), (640, 384))}

        def planes(first, count):
            home = 384 if first < 640 else 640
            return z_planes[home][:, :, first - home : first - home + count]

        def add_emb(engine, t, first, count, home):
            rows = emb_sb[(t, home)][:, first - home : first - home + count]
            engine.tensor_tensor(planes(first, count)[:, t, :], up[t][:, first : first + count], rows, ADD)

        both = keep.tile([P, U - TURNED], F32, name="both", tag="z_early1", align_bytes=64)
        nc.gpsimd.tensor_tensor(both[:], up[0][:, TURNED:], up[4][:, TURNED:], ADD)
        z_tiles = [keep.tile([P, U - TURNED], BF16, name="z_early%d" % g, tag="z_early%d" % g, align_bytes=64) for g in range(2)]

        def add_early(g, first, count):
            cols = slice(first - TURNED, first - TURNED + count)
            nc.gpsimd.tensor_tensor(z_tiles[g][:, cols], (both[:], up[1][:, TURNED:])[g][:, cols], emb_sb[(g, TURNED)][:, cols], ADD)

        def put_early(g, first, count):
            for e in range(2):
                src = z_tiles[g][e:P:2, first - TURNED : first - TURNED + count]
                nc.sync.dma_start(planes(first, count)[g * HP : (g + 1) * HP, e, :], src)

        add_early(0, 384, 640)
        for first, count in ((384, 256), (640, 384)):
            put_early(0, first, count)
        add_early(1, 384, 256)
        put_early(1, 384, 256)
        load_emb(3, 4, 640, 384)
        add_early(1, 640, 384)
        put_early(1, 640, 384)
        gates = keep.tile([P, D, V], F32, name="gates", tag="emb_early384")
        nc.sync.dma_start(gates[:], gate.rearrange("d p v -> p d v"))
        gate_sb = [gates[:, d, :] for d in range(D)]

        stretches = ((0, 256), (256, 128))
        turned = {}
        for u in range(2):
            for k, (first, count) in enumerate(stretches):
                turned[(u, first)] = bank(((4, 7), (0, 1))[u][k], 2 * count)

        def turn_sum(src, t, first, count, opens, closes):
            blocks = count // P
            for b in range(blocks):
                dst = turned[(t // 2, first)][:, (2 * b + t % 2) * P : (2 * b + t % 2 + 1) * P]
                nc.tensor.matmul(dst, src[:, first + b * P : first + (b + 1) * P], ident[:], start=opens and b == 0, stop=closes and b == blocks - 1, is_transpose=True)

        for t in range(PACK):
            for first, count in stretches:
                turn_sum(emb_sb[(t, 0)], t, first, count, t % 2 == 0, False)
        for window, t in ((4, 0), (0, 0), (1, 1)):
            for first, count in stretches:
                turn_sum(up[window], t, first, count, False, t % 2 == 1)
        for first, count in stretches:
            for t in (2, 3):
                turn_sum(up[t], t, first, count, False, t % 2 == 1)

        back = {first: bank(2 + k, 2 * count) for k, (first, count) in enumerate(stretches)}
        for u in range(2):
            for first, count in stretches:
                pairs = keep.tile([P, count // P, P, 2], BF16, name="z_turned%d_%d" % (u, first))
                if u == 0:
                    nc.scalar.copy(pairs[:].rearrange("c b p e -> c (b p e)"), turned[(u, first)][:])
                else:
                    nc.scalar.copy(pairs[:], turned[(u, first)][:].rearrange("c (b e p) -> c b p e", e=2, p=P))
                words = pairs[:].rearrange("c b p e -> c b (p e)").bitcast(F32)
                for b in range(count // P):
                    nc.tensor.transpose(back[first][:, (2 * b + u) * P : (2 * b + u + 1) * P], words[:, b, :], ident[:])

        z_grouped = {}
        z_mx = {}

        def weave(copy, first, count, buffer):
            z_grouped[first] = keep.tile([P, count, PACK], BF16, name="z_grouped%d" % first, tag=buffer, align_bytes=64)
            copy(z_grouped[first][:].rearrange("p (c i) t -> p c t i", i=4), planes(first, count).rearrange("p t (c i) -> p c t i", i=4))

        def lay_back(first, count):
            dst = z_grouped[0][:, first : first + count, :].rearrange("p c t -> p (c t)").bitcast(F32)
            nc.scalar.copy(dst.rearrange("p (b c u) -> p b c u", c=P, u=2), back[first][:].rearrange("p (b u c) -> p b c u", u=2, c=P))

        for t in (2, 3):
            add_emb(nc.vector, t, 384, 256, 384)
        add_emb(nc.vector, 2, 640, 384, 640)
        weave(nc.vector.tensor_copy, 384, 256, "z_grouped384")
        add_emb(nc.vector, 3, 640, 384, 640)
        weave(nc.scalar.copy, 896, 128, "z_grouped896")
        z_grouped[0] = keep.tile([P, TURNED, PACK], BF16, name="z_grouped0", tag="z_early1", align_bytes=64)
        lay_back(0, 256)
        lay_back(256, 128)

        def quantise_z(first, count, home, buffer):
            codes = keep.tile([P, count], U32, name="z_codes%d" % first, tag=buffer, align_bytes=64)
            scales = keep.tile([P, count], U8, name="z_sc%d" % first, align_bytes=64)
            src = z_grouped[home][:, first - home : first - home + count, :]
            nc.vector.quantize_mx(out=codes[:].bitcast(FP8X4), scales=scales[:], in_=src.rearrange("p c t -> p (c t)"))
            z_mx[first] = (codes, scales)

        quantise_z(384, 256, 384, "z_codes384")
        weave(nc.vector.tensor_copy, 640, 256, "z_grouped640")
        quantise_z(896, 128, 896, "z_codes896")
        quantise_z(640, 256, 640, "z_codes640")
        quantise_z(0, 256, 0, "z_codes0")
        quantise_z(256, 128, 0, "z_grouped640")

        y = [keep.tile([P, U], F32, name="y%d" % b, tag=("planes640", "z_grouped896")[b], align_bytes=64) for b in range(N // P)]

        def layer2(unload, b, number, *pieces):
            width = sum(z_mx[start][0].shape[1] for start in pieces)
            acc = bank(number, width)
            cols = slice(b * P, (b + 1) * P)
            done = 0
            for start in pieces:
                codes, scales = z_mx[start]
                count = codes.shape[1]
                nc.tensor.matmul_mx(out=acc[:, done : done + count], lhsT=w2_codes[:, cols].bitcast(FP8X4), lhsT_scale=w2_sc[:, cols], rhs=codes[:].bitcast(FP8X4), rhs_scale=scales[:], start=True, stop=True)
                done = done + count
            unload(y[b][:, min(pieces) : min(pieces) + width], acc[:])

        layer2(nc.scalar.copy, 0, 5, 384)
        layer2(nc.scalar.copy, 1, 6, 384)
        layer2(nc.scalar.copy, 0, 0, 640, 896)
        layer2(nc.scalar.copy, 1, 1, 640, 896)
        layer2(nc.vector.tensor_copy, 0, 4, 0)
        layer2(nc.scalar.copy, 1, 7, 0)
        layer2(nc.vector.tensor_copy, 0, 2, 256)
        layer2(nc.vector.tensor_copy, 1, 3, 256)

        def turn(dst, src, first, last):
            blocks = src.shape[1] // P
            for k in range(blocks):
                cols = slice(k * P, (k + 1) * P)
                nc.tensor.matmul(dst[:, cols], src[:, cols], ident[:], start=first and k == 0, stop=last and k == blocks - 1, is_transpose=True)

        def weighted(term, b, d, first):
            count = term.shape[1]
            nc.vector.tensor_tensor(term, y[b][:].indirect(entries(pos_sb[d], first, count)), gate_sb[d][:, first : first + count], MULT)

        halves = [slice(a * V // 2, (a + 1) * V // 2) for a in range(2)]
        sum_turned = [bank(2 + a, V // 2) for a in range(2)]

        def fetch(dst, b, d, first):
            nc.scalar.activation(dst, y[b][:].indirect(entries(pos_sb[d], first, dst.shape[1])), COPY)

        for d in range(D):
            term = keep.tile([P, V], F32, name="term0_%d" % d, tag="term0_%d" % d)
            if d < D - 1:
                weighted(term[:], 0, d, 0)
            else:
                weighted(term[:, halves[0]], 0, d, 0)
                raw_half = keep.tile([P, V // 2], F32, name="raw_half", tag="z_grouped640", align_bytes=64)
                fetch(raw_half[:], 0, d, V // 2)
                nc.vector.tensor_tensor(term[:, halves[1]], raw_half[:], gate_sb[d][:, halves[1]], MULT)
            for a in range(2):
                turn(sum_turned[a], term[:, halves[a]], d == 0, d == D - 1)

        raw = [keep.tile([P, V], F32, name="raw%d" % d) for d in range(D - 1)]
        last_raw = [keep.tile([P, (384, 128)[a]], F32, name="last_raw%d" % a, tag=("last_raw", "term0_2")[a]) for a in range(2)]
        fetch(raw[0][:], 1, 0, 0)
        fetch(last_raw[0][:, :256], 1, D - 1, 0)
        for a in range(2):
            fetch(raw[1][:, halves[a]], 1, 1, a * V // 2)
        fetch(last_raw[0][:, 256:], 1, D - 1, 256)
        sum_back = []
        for a in range(2):
            sum_sb = keep.tile([P, V // 2], F32, name="sum_sb%d" % a)
            nc.scalar.copy(sum_sb[:], sum_turned[a][:])
            sum_back.append(bank(4 + a, V // 2))
            turn(sum_back[a], sum_sb, True, True)
        fetch(last_raw[1][:], 1, D - 1, 384)
        for a in range(2):
            result0 = keep.tile([P, V // 2], F32, name="result0_%d" % a)
            nc.scalar.copy(result0[:], sum_back[a][:])
            nc.scalar.dma_start(out[0:P, halves[a]], result0[:])

        terms = [keep.tile([P, V], F32, name="term1_%d" % d) for d in range(D)]
        pair = keep.tile([P, V], F32, name="pair")

        def weigh(d, src, cols):
            nc.vector.tensor_tensor(terms[d][:, cols], src, gate_sb[d][:, cols], MULT)

        def finish(d, first, count):
            cols = slice(first, first + count)
            result1 = keep.tile([P, count], F32, name="result1_%d" % first)
            nc.vector.tensor_tensor(result1[:], pair[:, cols], terms[d][:, cols], ADD)
            nc.sync.dma_start(out[P : 2 * P, cols], result1[:])

        weigh(0, raw[0][:], slice(0, V))
        weigh(2, last_raw[0][:, :256], halves[0])
        weigh(1, raw[1][:, halves[0]], halves[0])
        nc.vector.tensor_tensor(pair[:, halves[0]], terms[0][:, halves[0]], terms[2][:, halves[0]], ADD)
        weigh(1, raw[1][:, halves[1]], halves[1])
        finish(1, 0, 256)
        weigh(2, last_raw[0][:, 256:], slice(256, 384))
        nc.vector.tensor_tensor(pair[:, halves[1]], terms[0][:, halves[1]], terms[1][:, halves[1]], ADD)
        weigh(2, last_raw[1][:], slice(384, V))
        finish(2, 256, 128)
        finish(2, 384, 128)
